import numpy as np, ml_dtypes
CORES = [23,119,17,113]
N = 4
BF = ml_dtypes.bfloat16
def gentries(a):
    return np.ascontiguousarray(a.reshape(8, 16, -1).transpose(0, 2, 1)).reshape(8, -1)
def gtable(e):
    e = np.asarray(e); return np.ascontiguousarray(e.reshape(8, -1, 16).transpose(0, 2, 1)).reshape(128, -1).astype(np.int32)
Q, A, S, RO, B = 1024, 256, 4, 5, 1024
W, H = N * Q, A // 4
def some(rng, shape, n):
    u = rng.random(shape); u = np.where(rng.random(shape) < 0.5, u, u * u)
    return np.minimum((n * u).astype(np.int64), n - 1)
def parts(rng):
    F = (rng.integers(0, 256, (8, 16, W)) * np.sqrt(rng.random((8, 1, W)))).astype(np.int64)
    NB = np.zeros((8, 16, W), np.int64); HO = np.zeros((N, 8, A), np.int64)
    for g in range(8):
        o = rng.permutation(W); NB[g] = o[some(rng, (16, W), W)]; HO[:, g] = o[some(rng, (N, A), W)]
    return F, NB, HO
def plant(rng):
    F, NB, HO = parts(rng); own = np.zeros((N, 8, H, S + 3), np.int64); k = N * H * (S + 3)
    for g in range(8):
        o = rng.permutation(W); mine, rest = o[:k], o[k:]
        own[:, g] = mine.reshape(N, H, S + 3)
        NB[g] = rest[some(rng, (16, W), W - k)]; HO[:, g] = rest[some(rng, (N, A), W - k)]
        for r in range(N): HO[r, g, rng.permutation(A)[:H]] = own[r, g, :, 0]
        NB[g][:, mine] = mine; F[g][:, mine] = 0
    return F, NB, HO, own
def lead(rng, NB, g, t, *cs):
    z = np.argsort(rng.random((16, len(t))), axis=0)
    for i, c in enumerate(cs):
        NB[g, z[2 * i], t] = c; NB[g, z[2 * i + 1], t] = c
def climb(rng, F, NB, g, e):
    n = len(e); m = np.zeros((16, n), np.int64)
    for k in range(S + 1):
        a = rng.integers(0, 40, (16, n)) * (rng.random((16, n)) < 0.2 * rng.random((1, n))); a[rng.integers(0, 16, n), np.arange(n)] += 1
        m = m + a; F[g][:, e[:, 1 + k]] = m; lead(rng, NB, g, e[:, k], e[:, 1 + k])
def pack(F, NB, HO):
    return {"feat": np.stack([F[:, :, r * Q:(r + 1) * Q].reshape(128, Q) for r in range(N)]).astype(np.float32).astype(BF),
            "nb": np.stack([NB[:, :, r * Q:(r + 1) * Q].reshape(128, Q) for r in range(N)]).astype(np.int32),
            "home": np.stack([gtable(a) for a in HO])}
def setup_inputs(rng):
    F, NB, HO = parts(rng)
    return pack(F, NB, HO)
def setup_inputs_cut(rng):
    F, NB, HO, own = plant(rng); j = np.arange(H); odd = j % 2 == 1
    for g in range(8):
        for r in range(N):
            e = own[r, g]
            if r % 2 == 0:
                u = e[:, 1]; F[g][8:, u] = 255; lead(rng, NB, g, e[:, 0], u)
                lead(rng, NB, g, u, own[np.where(j < H // 2, (r + 1) % N, (r - 1) % N), g, j, 1])
            else:
                t = [e[:, 1 + k] for k in range(S + 1)]; alt = e[:, S + 2]
                m = np.zeros((16, H), np.int64); m[:8] = rng.integers(100, 181, (8, H)); F[g][:, t[0]] = m
                b = np.zeros((16, H), np.int64); b[8:] = rng.integers(1, 91, (8, H))
                for k in range(1, S + 1):
                    y = np.where(m > 0, m + rng.integers(1, 10, (16, H)), 0)
                    if k == 1: y = np.where(odd, b, y)
                    F[g][:, t[k]] = y; m = np.maximum(m, y); lead(rng, NB, g, t[k - 1], t[k])
                F[g][:8, alt] = rng.integers(1, 50, (8, H)); lead(rng, NB, g, alt, t[1])
                lead(rng, NB, g, e[:, 0], t[0], np.where(odd, t[1], alt))
    return pack(F, NB, HO)
def setup_inputs_full(rng):
    F, NB, HO = parts(rng); rf = int(rng.integers(0, N - 1)); n = A * (2 * S + 2); w = 16 // (2 * S - 1)
    for g in range(8):
        o = rng.permutation(W); mine, rest = o[:n], o[n:]; e = mine.reshape(A, 2 * S + 2)
        NB[g] = rest[some(rng, (16, W), W - n)]; HO[:, g] = rest[some(rng, (N, A), W - n)]
        NB[g][:, mine] = mine; F[g][:, mine] = 0; HO[rf, g] = e[:, 0]
        if g % 2 == 0: climb(rng, F, NB, g, e)
        else:
            rn = N - 1 if rf == 0 and g > 4 else rf + 1
            k = np.arange(A) % S if g % 4 == 1 else np.full(A, S - 1)
            for i in range(2 * S - 1):
                F[g][w * i:w * i + w, e[:, 1 + i]] = rng.integers(1, 256, (w, A)); lead(rng, NB, g, e[:, i], e[:, 1 + i])
            want = e[np.arange(A), 1 + k]; x = e[:, 2 * S]; HO[rn, g] = e[:, 2 * S + 1]
            if g != 7: F[g][15, x] = 1
            lead(rng, NB, g, x, want); lead(rng, NB, g, e[:, 2 * S + 1], want, x)
    return pack(F, NB, HO)
def setup_inputs_same(rng):
    F, NB, HO = parts(rng)
    for g in range(8):
        if g % 2 == 0:
            kinds = rng.integers(0, 256, (16, 6)); kinds[:, 0] = 0; F[g] = kinds[:, rng.integers(0, 6, W)]
        if g < 2: HO[:, g] = rng.permutation(W)[:24][rng.integers(0, 24, (N, A))]
        if g % 4 == 3: NB[g, 8:] = NB[g, :8]
        if g in (4, 5):
            h = int(rng.integers(0, W)); t = int(rng.integers(0, N)) * Q + rng.permutation(Q)[:5]; t = t[t != h][:1 if g == 4 else 4]
            HO[:, g] = h; NB[g][:, h] = t[np.arange(16) % len(t)]; F[g][:, t] = rng.integers(1, 256, (16, len(t)))
    return pack(F, NB, HO)
def setup_inputs_ends(rng):
    F, NB, HO = parts(rng)
    F = 255 * (rng.random((8, 16, W)) < 0.6 * rng.random((8, 1, W))).astype(np.int64); F[:, :, 0] = 255; F[:, :, W - 1] = 255
    ends = np.concatenate([np.arange(N) * Q, np.arange(N) * Q + Q - 1])
    for g in range(8):
        if g % 2 == 0:
            NB[g] = np.where(rng.random((16, W)) < 0.3, rng.choice(ends, (16, W)), NB[g])
            HO[:, g, ::3] = rng.choice(ends, HO[:, g, ::3].shape)
        if g % 4 == 1:
            m = np.nonzero(rng.random(W) < 0.3)[0]; NB[g][:, m] = m
        if g % 4 == 3:
            q = int(rng.integers(0, N)); NB[g] = q * Q + NB[g] % Q; HO[:, g] = q * Q + HO[:, g] % Q
    return pack(F, NB, HO)
def setup_inputs_spread(rng):
    F, NB, HO = parts(rng)
    F = (rng.random((8, 16, W)) * np.exp2(rng.integers(0, 9, (8, 1, W))) * (rng.random((8, 1, W)) > 0.0625)).astype(np.int64)
    for g in range(8):
        o = rng.permutation(W)
        NB[g] = o[np.minimum((W * rng.random((16, W)) ** 4).astype(np.int64), W - 1)]; HO[:, g] = o[np.minimum((W * rng.random((N, A)) ** 3).astype(np.int64), W - 1)]
    return pack(F, NB, HO)
def check_inputs(d):
    bad = []; v = np.asarray(d["feat"]).astype(np.float32)
    if not (np.min(v) >= 0 and np.max(v) <= 255 and np.all(v == np.floor(v))): bad.append("feat: whole numbers from 0 to 255")
    for k in ("nb", "home"):
        if np.min(d[k]) < 0 or np.max(d[k]) > W - 1: bad.append("range of " + k)
    return bad
def reference(feat, nb, home):
    F = np.concatenate([a.astype(np.float32).astype(np.int64).reshape(8, 16, Q) for a in feat], axis=2)
    C = np.concatenate([a.astype(np.int64).reshape(8, 16, Q) for a in nb], axis=2)
    F = np.ascontiguousarray(F.transpose(0, 2, 1)); C = np.ascontiguousarray(C.transpose(0, 2, 1))
    h = np.stack([gentries(a) for a in home]).astype(np.int64)
    ri = np.arange(N)[:, None, None]; gi = np.arange(8)[None, :, None]; ids = np.arange(N * A).reshape(N, 1, A, 1)
    bt = np.zeros((N, 8, S, A), np.int64); bk = np.zeros((N, 8, S, A), np.int64); cnt = np.zeros((N, 8, A), np.int64)
    T = np.zeros((N, 8, W), np.int64)
    for rnd in range(RO):
        V = np.maximum(T, np.maximum(np.roll(T, 1, axis=0), np.roll(T, -1, axis=0)))
        still = np.ones((N, 8, A), bool); n = np.zeros((N, 8, A), np.int64); M = np.zeros((N, 8, A, 16), np.int64); last = h
        for k in range(S):
            b = bt[:, :, k]
            still = still & (k < cnt) & (V[ri, gi, b] == bk[:, :, k])
            M = np.where(still[..., None], np.maximum(M, F[gi, b]), M); last = np.where(still, b, last); n = n + still
        c = C[gi, last]
        gain = np.add.reduce(np.maximum(F[gi[..., None], c] - M[:, :, :, None, :], 0), axis=-1)
        key = B * gain + (B - 1) - ids
        ok = (n < S)[..., None] & (gain > 0) & (key > V[ri[..., None], gi[..., None], c])
        p = np.argmax(np.where(ok, gain, 0), axis=-1)[..., None]
        ct = np.take_along_axis(c, p, -1)[..., 0]; kt = np.take_along_axis(key, p, -1)[..., 0]; bid = np.any(ok, axis=-1)
        best = np.zeros((N, 8, W), np.int64); np.maximum.at(best, (ri, gi, ct), np.where(bid, kt, 0))
        win = bid & (best[ri, gi, ct] == kt)
        T = np.zeros((N, 8, W), np.int64)
        for k in range(S):
            w = np.nonzero(k < n); T[w[0], w[1], bt[:, :, k][w]] = bk[:, :, k][w]
        w = np.nonzero(win); T[w[0], w[1], ct[w]] = kt[w]
        bt[w[0], w[1], n[w], w[2]] = ct[w]; bk[w[0], w[1], n[w], w[2]] = kt[w]; cnt = n + win
    yb = np.where(np.arange(S)[None, None, :, None] < cnt[:, :, None, :], bt, -1)
    return {"yb": yb.reshape(N, 8, S * A).astype(np.float32), "yt": T.astype(np.float32)}

@@ -1,0 +1,682 @@
+from concourse.bass import DstId, RemoteDMATransfer
+from concourse.mybir import AluOpType as OP, AxisListType as AX, ActivationFunctionType as AF
+
+F32, BF, I32, U16 = "float32", "bfloat16", "int32", "uint16"
+SB = {
+    "Fw": (4352, BF), "Nw": (4096, F32), "Wo": (5120, F32), "Wl": (4096, F32), "Bw": (4096, BF), "Wf": (5120, F32),
+    "Fd": (4096, BF), "Vd": (4096, F32), "CD": (3072, BF), "PM": (1536, BF), "M": (512, BF),
+    "sh": (16, I32), "lh": (64, I32), "sn": (1024, I32), "sf": (1024, BF), "ln": (1024, I32), "lf": (1024, BF),
+    "nh": (1024, BF), "nl": (1024, BF), "hf": (64, F32), "hx": (512, F32),
+    "ip": (1, I32), "ic": (16, I32), "fc": (56, F32), "iof": (256, F32), "D16": (16, F32), "D16b": (32, BF), "BD": (16, F32),
+    "I": (128, F32), "t0": (512, F32), "t1": (512, F32), "t2": (512, F32), "t3": (512, F32), "t4": (512, F32),
+    "t5": (512, F32), "pw": (16, F32), "sg": (16, F32), "inc": (16, F32), "EU": (336, U16),
+    "mL": (256, F32), "DX": (512, F32), "dP": (16, F32), "on": (320, F32), "onb": (256, BF),
+    "r15": (240, F32), "r5": (320, F32), "r8": (128, F32), "PJ": (512, F32), "PJb": (512, BF), "Kt": (512, BF),
+    "Kk": (512, F32), "idc": (32, F32), "CI": (256, BF), "CW": (640, BF), "SF": (40, BF), "SM": (320, BF), "SV": (56, F32),
+    "SU": (32, BF), "SC": (24, BF), "Sh": (256, F32), "SS": (24, BF), "SQ": (512, BF), "mH": (128, F32), "RH": (4, F32),
+    "mD": (256, F32), "Ib": (128, BF), "D256": (16, F32), "zr": (256, F32),
+    "VX": (88, F32), "NK": (80, F32), "NK3": (240, F32), "cum": (240, F32), "val": (80, F32), "sv": (80, F32), "vi": (16, I32),
+    "Li": (24, I32), "Rf": (24, F32), "XL": (256, F32), "XR": (128, F32), "cG": (256, F32),
+    "cT": (256, F32), "cu": (256, U16), "ge": (80, F32), "zq": (88, F32), "ZD": (80, F32), "XZ": (512, F32),
+    "am": (256, F32), "ss": (512, F32), "sc": (512, F32), "bi": (32, I32), "I1": (40, I32), "gi": (96, I32), "X1": (256, BF),
+    "CL": (240, U16), "ctf": (16, F32), "Kp": (256, F32), "La": (256, BF), "Lo": (256, BF), "R": (256, BF),
+    "st": (96, F32), "tz": (16, F32), "acc": (16, F32), "al": (16, F32), "ow": (24, F32), "XW": (128, F32),
+    "Va": (256, F32), "sm": (96, F32),
+    "o2": (32, F32), "s1": (32, F32), "l1": (32, F32), "s2": (64, F32), "l2": (64, F32), "yo": (256, F32),
+    "s3": (64, F32), "l3": (72, F32),
+}
+LISTS = {"E1": (0, 16), "E2": (16, 8), "EL": (32, 16), "EZ": (48, 32), "PC": (80, 16), "EH": (96, 32), "FS1": (128, 2),
+         "FS2": (132, 4), "FR": (144, 32), "FS3": (176, 4), "EY": (192, 32), "Lu": (224, 16), "Mu": (240, 16), "Wu": (256, 16),
+         "Zu": (272, 64)}
+SCRATCH = {k: ("sbuf", [128, n], d) for k, (n, d) in SB.items()}
+for _i in range(8):
+    SCRATCH["p%d" % _i] = ("psum", [128, 512], F32)
+SCRATCH["ts"] = ("dram", [4, 128, 64], F32)
+SCRATCH["tl"] = ("dram", [4, 128, 64], F32)
+NDMA = 20
+SEMAPHORES = (["qv", "qa", "qt", "qg", "sent", "ah", "at", "a1", "a2", "a3"] + ["an%d" % i for i in range(4)]
+              + ["af%d" % i for i in range(4)] + ["d%d" % i for i in range(NDMA)])
+BIG = float(2 ** 40)
+
+
+def A(name, c0=0, c1=None, cs=1, p0=0, p1=128, ps=1):
+    if name in LISTS:
+        o, n = LISTS[name]
+        return ("EU", o + c0, o + (n if c1 is None else c1), cs, p0, p1, ps)
+    return (name, c0, SB[name][0] if c1 is None else c1, cs, p0, p1, ps)
+
+
+def P(b, c0, c1, cs=1, p0=0, p1=128):
+    return ("p%d" % b, c0, c1, cs, p0, p1, 1)
+
+
+def IND(win, off):
+    return ("*", win, off)
+
+
+def _hit(a, b):
+    if a[3] == b[3] and (a[1] - b[1]) % a[3]:
+        return False
+    return a[0] == b[0] and a[1] < b[2] and b[1] < a[2] and a[4] < b[5] and b[4] < a[5]
+
+
+def rank_program(g, core, T, topo):
+    q = T.rank_of(core)
+    if q is None:
+        return
+    ops = []
+    groups = {}
+
+    def ap(a):
+        if not isinstance(a, tuple):
+            return a
+        if a[0] == "*":
+            return ap(a[1]).indirect(ap(a[2]))
+        if a[0] == "!":
+            return a[1]
+        n, c0, c1, cs, p0, p1, ps = a
+        return T[n][slice(p0, p1, ps) if ps > 1 else slice(p0, p1), slice(c0, c1, cs) if cs > 1 else slice(c0, c1)]
+
+    def add(qu, emit, outs, ins, grp=None, waits=()):
+        rd, wr = [], []
+        for a in ins:
+            if isinstance(a, tuple) and a[0] != "!":
+                rd += [a[1], a[2]] if a[0] == "*" else [a]
+        for a in outs:
+            if isinstance(a, tuple) and a[0] != "!":
+                if a[0] == "*":
+                    wr.append(a[1]); rd.append(a[2])
+                else:
+                    wr.append(a)
+        ops.append([qu, emit, rd, wr, grp, list(waits)])
+
+    def cp(o, i, w=()): add("v", lambda: g.vector.tensor_copy(ap(o), ap(i)), [o], [i], None, w)
+    def tt(o, a, b, op, w=()): add("v", lambda: g.vector.tensor_tensor(ap(o), ap(a), ap(b), op), [o], [a, b], None, w)
+    def ms(o, c): add("v", lambda: g.vector.memset(ap(o), c), [o], [])
+    def red(o, i, op): add("v", lambda: g.vector.tensor_reduce(ap(o), ap(i), AX.X, op), [o], [i])
+    def scan(o, a, b, i0, o0, o1): add("v", lambda: g.vector.tensor_tensor_scan(ap(o), ap(a), ap(b), i0, o0, o1), [o], [a, b])
+    def tr(o, i): add("v", lambda: g.vector.transpose(ap(o), ap(i)), [o], [i])
+
+    def ts(o, a, s1, o0, s2=None, o1=None):
+        if s2 is None:
+            add("v", lambda: g.vector.tensor_scalar(ap(o), ap(a), ap(s1), None, o0), [o], [a, s1])
+        else:
+            add("v", lambda: g.vector.tensor_scalar(ap(o), ap(a), ap(s1), ap(s2), o0, o1), [o], [a, s1, s2])
+
+    def act(o, i, f=AF.Identity, bias=None, scale=None, acc=None, w=()):
+        kw = {}
+        if bias is not None: kw["bias"] = bias
+        if scale is not None: kw["scale"] = scale
+        if acc is not None: kw["accum_out"] = acc
+        add("a", lambda: g.scalar.activation(ap(o), ap(i), f, **{k: ap(v) for k, v in kw.items()}), [o, acc], [i, bias, scale], None, w)
+
+    def mm(o, l, r, start=True, stop=True, w=()):
+        add("t", lambda: g.tensor.matmul(ap(o), ap(l), ap(r), start, stop), [o], [l, r], None, w)
+
+    def iota(o, pat, base=0, cm=0):
+        if SB[o[0]][1] == I32:
+            add("g", lambda: g.iota(ap(o), pat, base, cm), [o], [])
+        else:
+            add("g", lambda: g.iota(ap(o), pat, base, cm, allow_small_or_imprecise_dtypes=True), [o], [])
+
+    def sel(o, pat, op, base, cm, src=None):
+        if src is None:
+            n = 1
+            for _s, c in pat: n *= c
+            src = A("onb" if SB[o[0]][1] == BF else "on", 0, n)
+        add("g", lambda: g.affine_select(ap(o), ap(src), pat, op, 0.0, base, cm), [o], [src])
+
+    def zero(o):
+        iota(o, [[0, len(range(o[1], o[2], o[3]))]])
+
+    def dma(qu, o, i, grp, w=()):
+        groups[grp] = groups.get(grp, 0) + 1
+        eng = g.sync if qu == "s" else g.scalar
+        add(qu, lambda: eng.dma_start(ap(o), ap(i)), [o], [i], grp, w)
+
+    def shares(src):
+        others = [c for c in T.cores if c != src]
+        far = [c for c in others if topo.chip(c) != topo.chip(src)]
+        taken, out = set(), {}
+        for i, c in enumerate(far):
+            e = topo.engines(src, c); n = len(e) // len(far)
+            out[c] = e[i * n:(i + 1) * n]; taken |= set(e)
+        near = [c for c in others if c not in far]
+        for i, c in enumerate(near):
+            e = [x for x in topo.engines(src, c) if x not in taken]; n = len(e) // len(near)
+            out[c] = e[i * n:(i + 1) * n]
+        return out
+    mine = shares(core)
+    got = {s: len(shares(T.cores[s])[core]) for s in range(4) if s != q}
+    gotall = sum(got.values())
+    nsent = [0]
+
+    def send(src_of, dst, sem, reads, w=()):
+        trs = []
+        for r in range(4):
+            if r != q:
+                c = T.cores[r]; rid, pid, _ = topo.addr(c)
+                trs.append(RemoteDMATransfer(dst_ids=[DstId(rid=rid, pnc=pid)], dma_engine_mask=sum(1 << e for e in mine[c]),
+                                             remote_sem=T.sem[sem], src=src_of(r), dst=dst))
+                nsent[0] += len(mine[c])
+        add("g", lambda: g.remote_dma_fused(trs, local_sem=T.sem.sent), [], reads, "remote", w)
+
+    order = [(q + 1 + i) % 4 for i in range(3)]
+    dma("s", A("sh"), ("!", T.home[:, :]), "ldh")
+    for r in order:
+        dma("s", A("sn", 256 * r, 256 * r + 256), ("!", T.nb[32 * r:32 * r + 32, :]), "ldn")
+    dma("s", A("ln", 256 * q, 256 * q + 256), ("!", T.nb[32 * q:32 * q + 32, :]), "own")
+    for r in order:
+        dma("s", A("sf", 256 * r, 256 * r + 256), ("!", T.feat[32 * r:32 * r + 32, :]), "ldf")
+    dma("s", A("lf", 256 * q, 256 * q + 256), ("!", T.feat[32 * q:32 * q + 32, :]), "owf")
+    iota(A("ip"), [[0, 1]], 0, 1)
+    iota(A("iof"), [[1, 256]])
+    iota(A("t0", 0, 128), [[64, 2], [0, 4], [4, 16]])
+    iota(A("t3", 0, 16), [[2, 2], [4, 4], [0, 2]], -16)
+    iota(A("t3", 16, 48), [[16, 4], [0, 8]])
+    iota(A("mH"), [[1, 8], [0, 16]])
+    iota(A("t4", 0, 32), [[4, 2], [0, 4], [1, 4]])
+    send(lambda r: T.sh[:, :], T.lh[:, 16 * q:16 * q + 16], "ah", [A("sh")])
+    iota(A("mL"), [[0, 8], [1, 2], [0, 16]])
+    zero(A("Li")); zero(A("VX"))
+    send(lambda r: T.sn[:, 256 * r:256 * r + 256], T.ln[:, 256 * q:256 * q + 256], "an%d" % q, [A("sn")])
+    send(lambda r: T.sf[:, 256 * r:256 * r + 256], T.lf[:, 256 * q:256 * q + 256], "af%d" % q, [A("sf")])
+
+    EQL, GT = OP.is_equal, OP.is_gt
+
+    def spare(rho):
+        dx = A("DX", 128 * rho, 128 * rho + 128)
+        iota(dx, [[0, 8], [8, 2], [-255, 8]], 4096 + 256 * rho, 16)
+        sel(dx, [[0, 16], [-16, 8]], OP.is_ge, 0, 1, dx); sel(dx, [[0, 16], [16, 8]], OP.is_ge, 15, -1, dx)
+    iota(A("t0", 128, 320), [[0, 6], [-1, 4], [0, 8]], 3)
+    iota(A("t0", 320, 448), [[0, 16], [-64, 8]], 960)
+    iota(A("dP"), [[0, 8], [8, 2]], 4096)
+    iota(A("on"), [[0, 320]], 1)
+    sel(A("r8"), [[0, 16], [1, 8]], GT, 0, 0)
+    iota(A("onb"), [[0, 256]], 1)
+    zero(A("I1"))
+    for h in range(2):
+        zero(A("Kt", 256 * h, 256 * h + 128))
+    iota(A("Kt", 15, 512, 16), [[0, 32]], 1)
+    iota(A("Kt", 14, 512, 16), [[-128, 2], [0, 16]], 255, -1)
+    for h in range(2):
+        sel(A("PJb", 256 * h, 256 * h + 256), [[1, 16], [128, 2], [16, 8]], EQL, -128 * h, -1)
+    sel(A("Ib"), [[1, 128]], EQL, 0, -1)
+    iota(A("idc"), [[-128, 2], [0, 4], [-256, 4]], 1023, -1)
+    for h in range(2):
+        zero(A("Kk", 256 * h, 256 * h + 128))
+    iota(A("t2", 128, 144), [[1, 2], [8, 4], [2, 2]])
+    iota(A("t2", 160, 192), [[2, 4], [8, 8]], -64)
+    zero(A("tz")); zero(A("ow"))
+    for m in range(2):
+        sel(A("Sh", 64 * m, 64 * m + 48), [[1, 48]], EQL, 64 * m + 16, -1)
+        sel(A("Sh", 64 * m + 48, 64 * m + 64), [[1, 16]], EQL, 64 * m, -1)
+        sel(A("Sh", 128 + 64 * m, 144 + 64 * m), [[1, 16]], EQL, 64 * m + 48, -1)
+        sel(A("Sh", 144 + 64 * m, 192 + 64 * m), [[1, 48]], EQL, 64 * m, -1)
+    spare(0)
+    zero(A("ZD"))
+    iota(A("t1", 256, 264), [[1, 8]])
+    iota(A("t1", 264, 272, 4), [[4, 2]], 3); iota(A("t1", 275, 280, 4), [[4, 2]], 0)
+    for m in range(2):
+        iota(A("t1", 265 + 4 * m, 268 + 4 * m), [[1, 3]], 4 * m); iota(A("t1", 272 + 4 * m, 275 + 4 * m), [[1, 3]], 4 * m + 1)
+    iota(A("t3", 64, 384), [[0, 5], [1, 8], [0, 8]])
+    iota(A("t2", 64, 96), [[1, 4], [10, 8]], 1 - 80)
+    zero(A("Fw", 4096, 4352)); zero(A("PM", 0, 256))
+    sel(A("r15"), [[0, 16], [1, 15]], GT, 0, 0)
+    sel(A("r5"), [[0, 64], [1, 5]], GT, 0, 0)
+    zero(A("zq")); zero(A("Rf"))
+    for rho in range(1, 4):
+        spare(rho)
+    iota(A("PM", 1280, 1536), [[0, 256]], 255)
+    zero(A("l3", 64, 72))
+    iota(A("mD"), [[0, 16], [1, 16]])
+    for h in range(2):
+        sel(A("PJ", 256 * h, 256 * h + 256), [[1, 16], [128, 2], [16, 8]], EQL, -128 * h, -1)
+
+    def fc(k): return A("fc", k, k + 1)
+    AND, SHR, MUL, ADD = OP.bitwise_and, OP.logical_shift_right, OP.mult, OP.add
+    for k, (s, m) in enumerate([(0, 15), (4, 7), (0, 7), (3, 1), (4, 3), (4, 1), (3, 15), (0, 6), (0, 1), (1, 3), (0, 127),
+                                (0, 3), (6, 1)]):
+        ts(A("ic", k, k + 1), A("ip"), s, SHR, m, AND)
+    ms(A("t1", 0, 16), 2.0); ms(A("zr"), 0.0)
+    cp(A("fc", 0, 11), A("ic", 0, 11)); cp(A("fc", 41, 43), A("ic", 11, 13))
+    X, G, X8, HX, RK, ODD, P8, X6, X1, X13, PF = [fc(k) for k in range(11)]
+    io = lambda a, b: A("iof", a, b)
+    d16 = lambda k: A("D16", k, k + 1)
+    BD, D8 = A("BD", 0, 8), A("BD", 8, 16)
+    scan(A("pw"), A("t1", 0, 16), A("zr", 0, 16), 0.5, MUL, ADD)
+    ts(A("D16"), io(0, 16), X, EQL)
+    ts(BD, io(0, 8), G, EQL)
+    ts(A("inc", 0, 6), A("pw", 0, 6), d16(7), MUL)
+    ts(A("inc", 6, 12), A("pw", 0, 6), d16(6), MUL)
+    act(A("Wl", 0, 1), A("zr", 0, 1))
+    for c in range(2):
+        act(A("Wo", 256 * c, 256 * c + 256), A("zr"), AF.Silu)
+    for k in range(12):
+        act(A("Wl", 1 << k, 2 << k), A("Wl", 0, 1 << k), bias=A("inc", k, k + 1))
+    ts(A("sg"), A("D16"), -2.0, MUL, 1.0, ADD)
+    ts(fc(30), d16(12), 4096.0, MUL, d16(14), ADD)
+    ts(fc(33), d16(12), 2.0 ** 29, MUL)
+    ts(fc(22), RK, -(2.0 ** 23), MUL, 3 * 2.0 ** 23, ADD)
+    ts(fc(31), d16(13), 256.0, MUL, fc(30), ADD)
+    ts(fc(34), d16(13), 2.0 ** 25, MUL, fc(33), ADD)
+    ts(fc(32), X, 11.5, OP.is_lt, 1024.0, MUL)
+    ts(fc(35), d16(14), 2.0 ** 15, MUL, fc(34), ADD)
+    tt(A("Bw", 0, 1), fc(31), fc(32), ADD)
+    ts(fc(36), fc(22), d16(15), MUL, fc(35), ADD)
+    ts(fc(37), fc(31), -1.0, MUL)
+    fill = [lambda qt=qt: ts(A("SQ", 128 * qt, 128 * qt + 128), A("t0", 0, 128), float(qt), ADD, PF, EQL) for qt in range(4)]
+    fill += [lambda: ts(D8, io(0, 8), X8, EQL), lambda: tt(fc(11), X8, G, EQL), lambda: ts(fc(12), X, 16.0, MUL, G, ADD),
+             lambda: ts(A("I"), io(0, 128), PF, EQL), lambda: ts(A("EH"), A("t3", 16, 48), X, ADD),
+             lambda: ts(A("mH"), A("mH"), X8, EQL)]
+    for k in range(10):
+        ts(A("Bw", 1 << k, 2 << k), A("Bw", 0, 1 << k), A("sg", k, k + 1), MUL)
+        fill[k]()
+    EQ, XG = fc(11), fc(12)
+
+    def lst(name, src, col, zcol):
+        n = LISTS[name][1]
+        ts(A("t2", 0, n), src, col, ADD, EQ, MUL)
+        ts(A(name), A("t2", 0, n), float(zcol), ADD)
+
+    near = [s for s in range(4) if s != q and topo.chip(T.cores[s]) == topo.chip(core)]
+    far = [s for s in range(4) if s != q and s not in near]
+    bank = [0]; nsum = [0]
+    wf = lambda s: [("af%d" % s, got[s])]
+
+    def split(s):
+        raw = A("ln", 256 * s, 256 * s + 256); hi = A("nh", 256 * s, 256 * s + 256)
+        cp(hi, raw, [("an%d" % s, got[s])] if s != q else [])
+        tt(A("nl", 256 * s, 256 * s + 256), raw, hi, OP.subtract)
+
+    def spread(win, s, parts, banks=(0, 1, 2, 3, 6, 7)):
+        for half in range(2):
+            b = banks[bank[0] % len(banks)]; bank[0] += 1
+            for j in range(2):
+                sq = A("SQ", 128 * (2 * half + j), 128 * (2 * half + j) + 128)
+                for i, src in enumerate(parts):
+                    mm(P(b, 256 * j, 256 * j + 256), sq, A(src, 256 * s, 256 * s + 256), i == 0, i == len(parts) - 1)
+            act(A(win, 1024 * s + 512 * half, 1024 * s + 512 * half + 512), P(b, 0, 512))
+
+    def sums(ss, eng, b=5):
+        for i, s in enumerate(ss):
+            mm(P(b, 256 * i, 256 * i + 256, 1, 0, 32), A("SU"), A("lf", 256 * s, 256 * s + 256), w=wf(s) if s != q else ())
+        c0 = 256 * nsum[0]; n = 256 * len(ss); nsum[0] += len(ss)
+        if eng == "a": act(A("Vd", c0, c0 + n, 1, 0, 32), P(b, 0, n, 1, 0, 32))
+        else: cp(A("Vd", c0, c0 + n, 1, 0, 32), P(b, 0, n, 1, 0, 32))
+        for i, s in enumerate(ss):
+            dma("s", A("Wl", 1024 * s, 1024 * s + 1024, 1, 5, 128, 16), A("Vd", c0 + 256 * i, c0 + 256 * i + 256, 1, 0, 32), "su")
+    ts(fc(43), fc(42), 4.0, MUL, fc(41), ADD)
+    for S in range(2):
+        ts(fc(46 + S), d16(5), 1024.0, MUL, d16(6 + S), ADD)
+    ts(A("SU"), A("t4", 0, 32), fc(43), EQL)
+    for S in range(2):
+        ts(A("SV", 40 + 8 * S, 48 + 8 * S), BD, fc(46 + S), MUL)
+    NP = ["nh", "nl"]
+    split(q); spread("Nw", q, NP)
+    lst("EL", A("t3", 0, 16), HX, 16)
+    ts(A("RH"), io(0, 4), float(4 * q), ADD, P8, EQL)
+    ts(A("mL"), A("mL"), HX, EQL)
+    cp(A("lh", 16 * q, 16 * q + 16), A("sh"))
+    cp(A("hf"), A("lh"), [("ah", gotall)])
+    for r in range(4):
+        tt(A("hx", 128 * r, 128 * r + 128), IND(A("hf"), A("EH", 8 * r, 8 * r + 8)), A("mH"), MUL)
+        for m in range(2):
+            mm(P(4, 8 * m + 2 * r, 8 * m + 2 * r + 2), A("hx", 128 * r, 128 * r + 128), A("RH", 2 * m, 2 * m + 2))
+    sums([q], "a"); spread("Fw", q, ["lf"])
+    act(A("Bw", 1024, 2048), A("Bw", 0, 1024), scale=A("sg", 10, 11))
+    ts(fc(13), X8, 32.0, MUL); ts(fc(14), HX, 16.0, MUL)
+    e0, e1 = A("I", 0, 1), A("I", 1, 2)
+    ts(fc(15), e0, 2.0 ** 30, MUL); ts(fc(16), e1, 2.0 ** 22, MUL)
+    ts(A("PC"), io(0, 16), fc(13), ADD, fc(14), ADD)
+    ts(A("t1", 0, 256), io(0, 256), -1.0, MUL, 255.0, ADD)
+    ts(fc(17), RK, 0.5, GT, d16(1), MUL); ts(fc(18), RK, 2.5, OP.is_lt, d16(3), MUL)
+    ts(A("CI"), A("t1", 0, 256), e1, MUL, e0, ADD)
+    tt(fc(19), fc(17), d16(2), ADD); tt(fc(20), fc(18), d16(4), ADD)
+    for t in range(5):
+        ts(A("SF", 8 * t, 8 * t + 8), BD, 2.0 ** 32 if t < 3 else 1024.0, MUL)
+    for t, col in enumerate([d16(0), fc(19), fc(20), d16(6), d16(7)]):
+        ts(A("SV", 8 * t, 8 * t + 8), BD, col, MUL, -2.0 ** 22 if t < 3 else 1.0, MUL)
+    cp(A("Li", 0, 16), P(4, 0, 16)); cp(A("VX", 0, 80, 5), P(4, 0, 16))
+    tt(fc(49), A("sg", 10, 11), A("sg", 11, 12), MUL)
+    tt(A("XL"), IND(A("Li"), A("EL")), A("mL"), MUL)
+    for u in range(2):
+        mm(P(4, 16 + u, 32, 2), A("XL", 128 * u, 128 * u + 128), D8)
+    ts(A("Bw", 2048, 3072), A("Bw", 0, 1024), A("sg", 11, 12), MUL)
+    ts(A("Bw", 3072, 4096), A("Bw", 0, 1024), fc(49), MUL)
+    split(near[0]); spread("Nw", near[0], NP)
+    cp(A("Lu"), P(4, 16, 32))
+    split(far[0]); spread("Nw", far[0], NP)
+    split(far[1])
+    ts(fc(25), X6, 4.0, MUL, X1, ADD); ts(fc(27), X1, 5.0, MUL, 4.0, ADD)
+    ts(fc(26), HX, 2.0, MUL, fc(25), ADD); ts(fc(28), HX, 40.0, MUL, fc(27), ADD)
+    ts(A("FS1"), io(0, 2), 4.0, MUL, fc(26), ADD); ts(fc(29), X13, 80.0, MUL, fc(28), ADD)
+    ts(fc(48), X13, -3.0, ADD, fc(28), ADD)
+    ts(A("FS2"), io(0, 4), 10.0, MUL, fc(29), ADD); ts(A("FS3"), io(0, 4), 10.0, MUL, fc(48), ADD)
+    sums(far, "v"); sums(near, "v", 4)
+    spread("Nw", far[1], NP)
+    for ph in range(2):
+        ts(A("CW", 320 * ph, 320 * ph + 192), A("t0", 128, 320), fc(15), MUL, fc(16), ADD)
+        ts(A("CW", 320 * ph + 192, 320 * ph + 320), A("t0", 320, 448), -512.0 * ph, ADD, e0, MUL)
+    spread("Fw", near[0], ["lf"])
+
+    def late(k):
+        if k == 0:
+            ts(fc(21), fc(14), -32.0, ADD); ts(fc(24), HX, 5.0, MUL)
+            tt(A("t1", 16, 32), A("pw"), A("D16"), MUL)
+            lst("E1", io(0, 16), fc(21), 32)
+            red(fc(38), A("t1", 16, 32), ADD)
+            ts(A("t1", 0, 8), io(0, 8), 2.0, MUL, -16.0, ADD)
+            ts(fc(39), fc(38), fc(32), MUL, -(2.0 ** -21), MUL)
+            lst("E2", A("t1", 0, 8), HX, 16)
+            ts(fc(40), d16(15), -12.0 * 2 ** 20, MUL, fc(37), ADD)
+            ts(A("D16b", 0, 16), A("D16"), 64.0, MUL); cp(A("D16b", 16, 32), A("D16")); ts(A("D256"), A("D16"), 1.0 / 16, MUL)
+            ts(A("SS", 0, 8), BD, fc(39), MUL)
+            ts(A("SS", 8, 16), BD, fc(36), MUL, -1.0, MUL)
+            ts(A("SS", 16, 24), BD, fc(40), MUL)
+            ts(A("dP"), A("dP"), XG, ADD)
+            ms(A("NK"), -BIG)
+        if k == 1:
+            ts(A("SC"), A("t1", 256, 280), G, EQL, fc(36), MUL)
+            ts(A("SM", 0, 192), A("t3", 64, 256), G, EQL, -2.0 ** 32, MUL)
+            ts(A("SM", 192, 320), A("t3", 256, 384), G, EQL, -1024.0, MUL)
+            lst("EZ", A("t2", 64, 96), fc(24), 80)
+        if k == 2:
+            cp(A("FR", 0, 16), A("t2", 128, 144)); ts(A("FR", 16, 32), A("t2", 128, 144), 4.0, ADD)
+            lst("EY", A("t2", 160, 192), HX, 64)
+        if k == 3:
+            ts(A("mD"), A("mD"), X, EQL)
+
+    def open_scores():
+        for b in range(4):
+            mm(P(b, 0, 320), A("CI", 128 * (b % 2), 128 * (b % 2) + 128, 1, 0, 2),
+               A("CW", 320 * (b // 2), 320 * (b // 2) + 320, 1, 0, 2), True, False)
+    WO = A("Wo", 0, 4096)
+
+    for k in range(1, 6):
+        nr = k - 1
+        if k > 1:
+            tt(A("PM", 256 * nr, 256 * nr + 256), IND(A("Fw"), A("Wu")), A("M", 0, 256) if k > 2 else A("PM", 0, 256), OP.max)
+            blocks = [i for i in range(3 * nr) if i != 3 * nr - 3]
+            for n, i in enumerate(blocks):
+                rho, t = i // 3 + 1, i % 3
+                o = A("CD", 256 * i, 256 * i + 256); src = IND(WO, A("CL", 16 * i, 16 * i + 16))
+                if n % 2 == 0 or k == 2: act(o, src)
+                else: cp(o, src)
+                for h in range(2):
+                    c0 = 256 + 15 * h + 3 * rho + t
+                    mm(P(5, c0, 496, 30), A("CD", 256 * i + 128 * h, 256 * i + 128 * h + 128), A("SC", 8 * t, 8 * t + 8), False,
+                       i == blocks[-1] and h == 1)
+            open_scores()
+            scan(A("cum"), A("r15"), P(5, 256, 496), 0.0, MUL, OP.max)
+            tt(A("val"), A("VX", 0, 80), A("cum", 2, 240, 3), OP.subtract)
+            scan(A("sv"), A("r5", 0, 80), A("val"), 0.0, MUL, OP.max)
+            cp(A("vi"), A("sv", 4, 80, 5))
+            ts(A("Li", 0, 16), A("vi"), 4095, AND)
+            tt(A("XL"), IND(A("Li"), A("EL")), A("mL"), MUL)
+            for u in range(2):
+                mm(P(4, 16 + u, 32, 2), A("XL", 128 * u, 128 * u + 128), D8)
+            tt(A("Rf", 0, 16), A("sv", 4, 80, 5), A("Li", 0, 16), OP.subtract)
+            if k == 5:
+                ts(A("sm", 0, 80), A("val"), 4096.0, OP.is_ge)
+                scan(A("sv"), A("r5", 0, 80), A("sm", 0, 80), 0.0, MUL, ADD)
+                ts(A("sm", 80, 96), A("sv", 4, 80, 5), 4.0, EQL, 4096.0, MUL)
+                tt(A("Rf", 0, 16), A("Rf", 0, 16), A("sm", 80, 96), ADD)
+            act(A("XR"), IND(A("Rf"), A("E2")))
+            ts(A("ge"), A("val"), 0.0, OP.is_ge)
+            tt(A("zq", 0, 80), P(5, 256, 496, 3), A("ge"), EQL)
+            cp(A("Lu"), P(4, 16, 32))
+            mm(P(4, 32, 48), A("DX", 0, 128), A("D16"), True, False)
+            mm(P(4, 32, 48), A("XR"), A("D256"), False, True)
+            act(A("cG"), IND(A("Nw"), A("Lu")))
+            tt(A("zq", 0, 80), A("zq", 0, 80), A("ZD"), MUL)
+            ts(A("Mu"), P(4, 32, 48), -4096.0, ADD)
+            act(A("M", 0, 256), IND(A("PM", 0, 256 * k if k < 5 else 1536), A("Mu")))
+        else:
+            cp(A("cG"), IND(A("Nw"), A("Lu")))
+            open_scores()
+            for c in range(1, 8):
+                dma("s", A("Wo", 512 * c, 512 * c + 512), A("Wo", 0, 512), "wz", wf(far[1]))
+        tr(A("cT"), A("cG"))
+        cp(A("cu"), IND(A("cT"), A("PC")))
+        if k > 1:
+            if k < 5:
+                cp(A("XZ", 0, 128 * nr), IND(A("zq"), A("EZ", 0, 8 * nr)))
+            else:
+                cp(A("s3"), IND(A("zq"), A("FS3")))
+                send(lambda r: T.s3[:, 16 * r:16 * r + 16], T.l3[:, 16 * q:16 * q + 16], "a3", [A("s3")])
+            for b in range(4):
+                mm(P(b, 0, 320), A("M", 128 * (b % 2), 128 * (b % 2) + 128), A("SM"), False, False)
+
+        def post(ph):
+            bs = (2 * ph, 2 * ph + 1)
+            if k == 1:
+                for b in bs:
+                    scan(A("sc", 128 * b, 128 * b + 128), A("r8"), P(b, 192, 320), 0.0, MUL, OP.max)
+                return
+            for b in bs:
+                if ph == 1: cp(A("am", 64 * b, 64 * b + 64), P(b, 0, 64))
+            for t in (1, 2):
+                for b in bs:
+                    tt(A("am", 64 * b, 64 * b + 64), P(b, 64 * t, 64 * t + 64), A("am", 64 * b, 64 * b + 64), OP.min)
+            for b in bs:
+                for S in range(2):
+                    tt(A("ss", 128 * b + 64 * S, 128 * b + 64 * S + 64), P(b, 192 + 64 * S, 256 + 64 * S),
+                       A("am", 64 * b, 64 * b + 64), OP.min)
+            for b in bs:
+                scan(A("sc", 128 * b, 128 * b + 128), A("r8"), A("ss", 128 * b, 128 * b + 128), 0.0, MUL, OP.max)
+        for p in range(16):
+            if k == 1:
+                o = A("Vd", 256 * p, 256 * p + 256); src = IND(A("Wl"), A("cu", 16 * p, 16 * p + 16))
+                if p % 2 == 0 or p == 15: act(o, src)
+                else: cp(o, src)
+                for h in range(2):
+                    mm(P(2 * (p // 8) + h, 192 + p % 8, 320, 8), A("Vd", 256 * p + 128 * h, 256 * p + 128 * h + 128), A("SV", 40, 56),
+                       False, p % 8 == 7)
+                if p == 15:
+                    late(0); spread("Fw", far[0], ["lf"], (6, 7)); post(0)
+                continue
+            w = 1 if p < 2 else 2 - 2 * (p % 2)
+            if p == 0: act(A("M", 256, 512), A("M", 0, 256))
+            if p % 2 == 0:
+                act(A("Vd", 256 * p, 256 * p + 512), IND(A("Wl"), A("cu", 16 * p, 16 * p + 32)))
+            if w:
+                tt(A("Fd", 256 * p, 256 * (p + w)), IND(A("Fw", 0, 4096), A("cu", 16 * p, 16 * (p + w))), A("M", 0, 256 * w), OP.max)
+            for h in range(2):
+                o = P(2 * (p // 8) + h, p % 8, 320, 8); c0 = 256 * p + 128 * h
+                mm(o, A("Vd", c0, c0 + 128), A("SV", 0, 40), False, False)
+                mm(o, A("Fd", c0, c0 + 128), A("SF"), False, p % 8 == 7)
+            if p == 0 and k == 5: cp(A("l3", 16 * q, 16 * q + 16), A("s3", 16 * q, 16 * q + 16))
+            if p == 6 and k == 5: cp(A("XZ"), IND(A("l3"), A("EY")), [("a3", gotall)])
+            if p == (1 if k < 5 else 7):
+                for rho in range(nr):
+                    mm(P(4, 64 + 16 * rho, 80 + 16 * rho), A("DX", 128 * rho, 128 * rho + 128), A("D16"), True, False)
+                    mm(P(4, 64 + 16 * rho, 80 + 16 * rho), A("XZ", 128 * rho, 128 * rho + 128), A("D16"), False, True)
+            if p == 12: cp(A("Zu", 0, 16 * nr), P(4, 64, 64 + 16 * nr))
+            if p == 10:
+                for b in range(2): act(A("am", 64 * b, 64 * b + 64), P(b, 0, 64))
+            if p == 15: post(0)
+
+        def clear(rho):
+            act(IND(A("Wo" if k < 5 else "Wf"), A("Zu", 16 * rho, 16 * rho + 16)), A("zr"), AF.Silu)
+        for rho in range(nr if k < 5 else 2):
+            clear(rho)
+        post(1)
+        tt(A("bi"), A("sc", 7, 256, 8), A("sc", 263, 512, 8), OP.max)
+        ts(A("I1", 0, 32), A("bi"), 63, AND)
+        ts(A("gi", 0, 32), A("bi"), 14, SHR)
+        cp(A("X1"), IND(A("I1"), A("E1")))
+        for S in range(2):
+            mm(P(4, 0, 16), A("X1", 128 * S, 128 * S + 128), A("D16b", 16 * S, 16 * S + 16), S == 0, S == 1)
+        ts(A("gi", 32, 64), A("bi"), 10, SHR, 15, AND)
+        cp(A("Kt", 12, 512, 16), A("gi", 0, 32))
+        cp(A("Kt", 13, 512, 16), A("gi", 32, 64))
+        for h in range(2):
+            mm(P(5, 0, 256), A("Kt", 256 * h, 256 * h + 128), A("PJb", 256 * h, 256 * h + 256), h == 0, h == 1)
+        cl = A("CL", 48 * nr, 48 * nr + 16)
+        cp(cl, P(4, 0, 16))
+        act(A("Kp"), P(5, 0, 256), bias=fc(37))
+        act(A("La"), IND(A("Bw"), cl))
+        if k < 5:
+            ts(A("gi", 64, 96), A("bi"), 0xFFFC00, AND)
+            cp(A("ctf"), P(4, 0, 16))
+            tt(A("Kk", 0, 512, 16), A("gi", 64, 96), A("idc"), ADD)
+            for h in range(2):
+                mm(P(4, 256 + 128 * h, 384 + 128 * h), A("Kt", 256 * h, 256 * h + 128), A("Ib"), True, False)
+                mm(P(4, 256 + 128 * h, 384 + 128 * h), A("Kk", 256 * h, 256 * h + 128), A("I"), False, True)
+        else:
+            ts(A("t1", 0, 80), A("val"), 4096.0, OP.is_ge)
+            ts(A("t2", 0, 80), A("val"), 0.0, OP.max)
+            cp(A("gi", 0, 80), A("t2", 0, 80))
+            ts(A("gi", 0, 80), A("gi", 0, 80), 4095, AND)
+            ts(A("t2", 0, 80), A("gi", 0, 80), 1.0, ADD)
+        tt(A("R"), IND(A("Bw"), cl), A("Kp"), ADD)
+        act(A("Lo"), A("La"), scale=ODD)
+        for h in range(2):
+            mm(P(4, 128 + h, 176, 2), A("R", 128 * h, 128 * h + 128), A("SS"))
+        if 1 < k < 5:
+            ts(A("ge"), A("val"), 0.0, OP.is_lt, -BIG, MUL)
+            ts(A("VX", 0, 80), A("val"), 0.0, OP.max)
+            tt(A("NK"), A("NK"), A("ge"), OP.min)
+        if k == 1: late(2)
+        if k == 5: late(3)
+        act(A("st", 16, 48), P(4, 144, 176))
+        act(A("st", 0, 16), P(4, 128, 144), bias=2047.5)
+        n = 0
+        for gg in (0, 2, 4, 6, 1, 3, 5, 7):
+            p0 = 16 * (gg - gg % 2); p1 = 16 * gg + 16
+            for h in range(2):
+                b = (0, 1, 2)[n % 3] if h == 0 else (3, 6, 7)[n % 3]
+                mm(P(b, 0, 256), A("Lo" if gg % 2 else "La", 128 * h, 128 * h + 128, 1, p0, p1), A("R", 0, 256, 1, p0, p1))
+                col = A("acc", 2 * gg + h, 2 * gg + h + 1)
+                if h == 0: red(col, P(b, 0, 256), OP.max)
+                else: act(A("CD", 256 * n, 256 * n + 256), P(b, 0, 256), AF.Relu, bias=A("st", 33 + 2 * gg, 34 + 2 * gg), acc=col)
+            n += 1
+            if n == 2:
+                ts(A("tz", 0, 16, 2), A("st", 32, 48, 2), -1.0, MUL)
+                ts(A("st", 48, 64), A("st", 16, 32), -(2.0 ** 25), OP.is_le, -1.0, ADD)
+                tt(A("st", 64, 80), A("st", 0, 16), A("dP"), OP.subtract)
+                tt(A("st", 48, 64), A("st", 48, 64), A("tz"), ADD)
+        if k < 5:
+            for t in range(2):
+                mm(P(5, 16 * t, 16 + 16 * t), A("Sh", 128 * t, 128 * t + 128), A("ctf"))
+            act(A("Va"), P(4, 256, 512))
+        else:
+            act(A("o2", 16, 32), A("st", 16, 32), scale=-(2.0 ** -15))
+        act(A("st", 80, 96), A("st", 0, 16), bias=4096.0 * k if k < 5 else 1.0)
+        if k == 5: clear(2); clear(3)
+        tt(A("al"), A("acc"), A("st", 48, 64), EQL)
+        tt(A("ow", 0, 16), A("al"), A("st", 64, 80), MUL)
+        if k < 5:
+            ts(A("sm", 0, 16), A("al"), -1.0, ADD, BIG, MUL)
+            tt(A("XW"), IND(A("ow"), A("E2")), A("DX", 0, 128), ADD)
+            mm(P(4, 48, 64), A("XW"), A("D16"))
+            tt(A("NK", k, 80, 5), A("sm", 0, 16), A("st", 16, 32), ADD)
+            cp(A("CL", 48 * nr + 16, 48 * nr + 48), P(5, 0, 32))
+            tt(A("VX", k, 80, 5), A("al"), A("st", 80, 96), MUL)
+            for t in range(3):
+                act(A("NK3", t, 240, 3), A("NK"))
+            act(A("NK3", 3 * k, 240, 15), A("sm", 0, 16))
+            act(A("ZD", k, 80, 5), A("st", 64, 80), bias=-256.0 * nr)
+            cp(A("Wu"), P(4, 48, 64))
+            if k == 1: spread("Fw", far[1], ["lf"], (6, 7))
+            mm(P(5, 256, 496), A("I"), A("NK3"), True, False)
+            cp(IND(A("Wo"), A("Wu")), A("Va"))
+            gr = "w%d" % k
+            dma("s", A("Wl", 0, 4096, 1, 0, 128, 16), A("Wo", 0, 4096, 1, 0, 128, 16), gr)
+            dma("s", A("Wl", 0, 4096, 1, 17, 128, 16), A("Wo", 0, 4096, 1, 0, 112, 16), gr)
+            dma("s", A("Wl", 0, 4096, 1, 3, 112, 16), A("Wo", 0, 4096, 1, 16, 128, 16), gr)
+            dma("s", A("Wl", 0, 4096, 1, 2, 128, 64), A("Wo", 0, 4096, 1, 48, 128, 64), gr)
+            dma("s", A("Wl", 0, 4096, 1, 52, 128, 64), A("Wo", 0, 4096, 1, 0, 128, 64), gr)
+            if k == 4:
+                for r in order:
+                    dma("s", ("!", T.ts[r]), A("Wo", 0, 4096, 1, 16 * r, 128, 64), "ts")
+                dma("s", A("Wf", 0, 4096, 1, 32 * q, 32 * q + 32, 16), A("Wo", 0, 4096, 1, 16 * q, 128, 64), "tf")
+                send(lambda r: T.ts[r], T.tl[q], "at", [], [("@ts", 0)])
+                for s in order:
+                    dma("s", A("Wf", 0, 4096, 1, 32 * s, 32 * s + 32, 16), ("!", T.tl[s]), "tf", [("at", gotall)])
+            if k == 1: late(1)
+
+    tt(A("o2", 0, 16), A("ow", 0, 16), A("dP"), ADD)
+    cp(A("t1", 5, 81, 5), A("al"))
+    cp(A("s1"), IND(A("o2"), A("FS1")))
+    send(lambda r: T.s1[:, 8 * r:8 * r + 8], T.l1[:, 8 * q:8 * q + 8], "a1", [A("s1")])
+    scan(A("t0", 0, 80), A("r5", 0, 80), A("t1", 1, 81), 0.0, MUL, ADD)
+    cp(A("t2", 5, 81, 5), A("st", 80, 96))
+    tt(A("t0", 0, 80), A("t0", 0, 80), A("t1", 1, 81), MUL)
+    for s in range(4):
+        ts(A("t3", 80 * s, 80 * s + 80), A("t0", 0, 80), float(s + 1), EQL)
+    for s in range(4):
+        tt(A("t4", 80 * s, 80 * s + 80), A("t3", 80 * s, 80 * s + 80), A("t2", 1, 81), MUL)
+    scan(A("t5", 0, 320), A("r5"), A("t4", 0, 320), 0.0, MUL, ADD)
+    cp(A("l1", 8 * q, 8 * q + 8), A("s1", 8 * q, 8 * q + 8))
+    ts(A("s2"), IND(A("t5", 0, 320), A("FS2")), -1.0, ADD)
+    send(lambda r: T.s2[:, 16 * r:16 * r + 16], T.l2[:, 16 * q:16 * q + 16], "a2", [A("s2")])
+    cp(A("l2", 16 * q, 16 * q + 16), A("s2", 16 * q, 16 * q + 16))
+    tt(A("XL"), IND(A("l1"), A("FR", 0, 16)), A("mD"), MUL, [("a1", gotall)])
+    act(A("cG"), IND(A("l1"), A("FR", 16, 32)), w=[("a1", gotall)])
+    for h in range(2):
+        mm(P(4, 8 * h, 8 * h + 8), A("XL", 128 * h, 128 * h + 128), BD)
+    for h in range(2):
+        mm(P(5, 128 * h, 128 * h + 128), A("cG", 128 * h, 128 * h + 128), A("I"))
+    cp(A("Wu"), P(4, 0, 16))
+    act(A("Va"), P(5, 0, 256))
+    cp(IND(A("Wf"), A("Wu")), A("Va"))
+    dma("s", ("!", T.yt[:, :]), A("Wf", 0, 4096, 1, 0, 128, 16), "yt")
+    for h in range(2):
+        mm(P(0, 0, 256, 1, 0, 32), A("l2", h, 64, 2), A("PJ", 256 * h, 256 * h + 256), h == 0, h == 1, [("a2", gotall)])
+    act(A("yo", 0, 256, 1, 0, 32), P(0, 0, 256, 1, 0, 32))
+    dma("a", ("!", T.yb[:, :]), A("yo", 0, 256, 1, 0, 32), "yb")
+
+    gsem = {n: "d%d" % i for i, n in enumerate(groups)}
+    needs = []; hist = {}; clock = {qu: {} for qu in "vatgs"}; snap = []; member = {}
+    for i, (qu, _, rd, wr, grp, _w) in enumerate(ops):
+        last = {}; known = clock[qu]
+        cand = sorted(set(j for a in rd + wr for j in hist.get(a[0], ())), reverse=True)
+        for a in rd + wr: hist.setdefault(a[0], set()).add(i)
+        for j in cand:
+            q2, _, rd2, wr2, grp2, _w2 = ops[j]
+            key = q2 if grp2 is None else "@" + grp2
+            if (key in last or known.get(key, -1) >= j or grp2 == "remote" or (grp2 is not None and grp2 == grp)
+                    or (qu == "t" and q2 == "t")):
+                continue
+            if (any(_hit(a, b) for a in rd + wr for b in wr2) or any(_hit(a, b) for a in wr for b in rd2)
+                    or (q2 != qu and any(a[0] == b[0] and a[0] not in SB for a in rd + wr for b in rd2 + wr2))):
+                last[key] = j
+        for key, j in sorted(last.items(), key=lambda e: -e[1]):
+            if known.get(key, -1) >= j:
+                del last[key]; continue
+            for jj in (member[key[1:]] if key[0] == "@" else [j]):
+                for k2, v2 in snap[jj].items():
+                    if known.get(k2, -1) < v2: known[k2] = v2
+            known[key] = len(ops) if key[0] == "@" else j
+        needs.append(last); snap.append(dict(known))
+        if grp is not None: member.setdefault(grp, []).append(i)
+    marked = set(j for last in needs for key, j in last.items() if key[0] != "@")
+    for qu in "vatg":
+        marked.add(max(i for i, o in enumerate(ops) if o[0] == qu and o[4] is None))
+    count, number = {}, {}
+    for i, o in enumerate(ops):
+        if i in marked:
+            count[o[0]] = count.get(o[0], 0) + 1; number[i] = count[o[0]]
+    eng = {"v": g.vector, "a": g.scalar, "t": g.tensor, "g": g, "s": g.sync}
+    seen = {}
+
+    def wait(qu, sem, n):
+        if seen.get((qu, sem), 0) < n:
+            seen[(qu, sem)] = n; eng[qu].wait_ge(T.sem[sem], n)
+    for i, (qu, emit, rd, wr, grp, ws) in enumerate(ops):
+        for key, j in needs[i].items():
+            if key[0] == "@": wait(qu, gsem[key[1:]], 16 * groups[key[1:]])
+            else: wait(qu, "q" + key, number[j])
+        for sem, n in ws:
+            if sem[0] == "@": wait(qu, gsem[sem[1:]], 16 * groups[sem[1:]])
+            else: wait(qu, sem, n)
+        ins = emit()
+        if grp is not None and grp != "remote": ins.then_inc(T.sem[gsem[grp]], 16)
+        elif i in marked: ins.then_inc(T.sem["q" + qu], 1)
+    for qu in "vatg":
+        wait("g", "q" + qu, count[qu])
+    for n in groups:
+        wait("g", gsem[n], 16 * groups[n])
+    wait("g", "sent", nsent[0])

@@ -1,28 +1,28 @@
 from concourse.bass import DstId, RemoteDMATransfer
 from concourse.mybir import AluOpType as OP, AxisListType as AX, ActivationFunctionType as AF
 
-F32, BF, I32, U16 = "float32", "bfloat16", "int32", "uint16"
+F32, BF, I32, U16, F16 = "float32", "bfloat16", "int32", "uint16", "float16"
 SB = {
     "Fw": (4352, BF), "Nw": (4096, F32), "Wo": (5120, F32), "Wl": (4096, F32), "Bw": (4096, BF), "Wf": (5120, F32),
     "Fd": (4096, BF), "Vd": (4096, F32), "CD": (3072, BF), "PM": (1536, BF), "M": (512, BF),
-    "sh": (16, I32), "lh": (64, I32), "sn": (1024, I32), "sf": (1024, BF), "ln": (1024, I32), "lf": (1024, BF),
-    "nh": (1024, BF), "nl": (1024, BF), "hf": (64, F32), "hx": (512, F32),
-    "ip": (1, I32), "ic": (16, I32), "fc": (56, F32), "iof": (256, F32), "D16": (16, F32), "D16b": (32, BF), "BD": (16, F32),
+    "sh": (16, I32), "lh": (64, I32), "sn": (1024, I32), "sf": (1024, BF), "sx": (1280, F16), "lx": (1280, F16), "lf": (1024, BF),
+    "hf": (64, F32), "hx": (512, F32),
+    "ic": (8, I32), "fc": (56, F32), "iof": (16, F32), "D16": (16, F32), "D16b": (32, BF), "BD": (16, F32),
     "I": (128, F32), "t0": (512, F32), "t1": (512, F32), "t2": (512, F32), "t3": (512, F32), "t4": (512, F32),
-    "t5": (512, F32), "pw": (16, F32), "sg": (16, F32), "inc": (16, F32), "EU": (336, U16),
-    "mL": (256, F32), "DX": (512, F32), "dP": (16, F32), "on": (320, F32), "onb": (256, BF),
-    "r15": (240, F32), "r5": (320, F32), "r8": (128, F32), "PJ": (512, F32), "PJb": (512, BF), "Kt": (512, BF),
-    "Kk": (512, F32), "idc": (32, F32), "CI": (256, BF), "CW": (640, BF), "SF": (40, BF), "SM": (320, BF), "SV": (56, F32),
-    "SU": (32, BF), "SC": (24, BF), "Sh": (256, F32), "SS": (24, BF), "SQ": (512, BF), "mH": (128, F32), "RH": (4, F32),
-    "mD": (256, F32), "Ib": (128, BF), "D256": (16, F32), "zr": (256, F32),
-    "VX": (88, F32), "NK": (80, F32), "NK3": (240, F32), "cum": (240, F32), "val": (80, F32), "sv": (80, F32), "vi": (16, I32),
+    "t5": (512, F32), "tb": (128, BF), "pw": (24, F32), "sg": (16, F32), "inc": (16, F32), "EU": (336, U16),
+    "mL": (256, F32), "DX": (512, F32), "dP": (32, F32), "on": (256, F32), "onb": (320, BF),
+    "r15": (240, F32), "r5": (320, F32), "r12": (192, F32), "r4": (128, F32), "PJ": (512, F16), "PJb": (512, BF), "Kt": (512, BF),
+    "Kk": (512, F32), "idc": (32, F32), "CI": (256, BF), "CW": (1152, BF), "SF": (24, BF), "SM": (384, BF), "SV": (56, F32),
+    "SU": (32, BF), "SC": (24, BF), "Sh": (256, F32), "SS": (64, BF), "SQ": (512, F16), "mH": (128, F32), "RH": (4, F32),
+    "mD": (256, F32), "Ib": (128, BF), "D256": (16, F32), "zr": (256, F32), "zb": (240, BF), "NI": (128, BF), "DW": (128, BF),
+    "VX": (88, F32), "NK": (80, F32), "DD": (80, BF), "cum": (240, F32), "val": (80, F32), "sv": (80, F32), "vi": (16, I32),
     "Li": (24, I32), "Rf": (24, F32), "XL": (256, F32), "XR": (128, F32), "cG": (256, F32),
-    "cT": (256, F32), "cu": (256, U16), "ge": (80, F32), "zq": (88, F32), "ZD": (80, F32), "XZ": (512, F32),
-    "am": (256, F32), "ss": (512, F32), "sc": (512, F32), "bi": (32, I32), "I1": (40, I32), "gi": (96, I32), "X1": (256, BF),
-    "CL": (240, U16), "ctf": (16, F32), "Kp": (256, F32), "La": (256, BF), "Lo": (256, BF), "R": (256, BF),
-    "st": (96, F32), "tz": (16, F32), "acc": (16, F32), "al": (16, F32), "ow": (24, F32), "XW": (128, F32),
+    "cT": (256, F32), "cu": (256, U16), "zq": (88, F32), "ZD": (80, F32), "XZ": (512, F32),
+    "pen": (1280, BF), "sc": (512, F32), "bi": (32, I32), "I1": (40, I32), "gi": (96, I32), "X1": (256, BF),
+    "CL": (240, U16), "ctf": (16, F32), "La": (256, BF), "Lo": (256, BF), "R": (256, BF),
+    "st": (96, F32), "acc": (16, F32), "al": (16, F32), "ow": (24, F32), "XW": (128, F32),
     "Va": (256, F32), "sm": (96, F32),
-    "o2": (32, F32), "s1": (32, F32), "l1": (32, F32), "s2": (64, F32), "l2": (64, F32), "yo": (256, F32),
+    "o2": (32, F32), "s1": (32, F32), "l1": (32, F32), "s2": (64, F16), "l2": (64, F16), "yo": (256, F32),
     "s3": (64, F32), "l3": (72, F32),
 }
 LISTS = {"E1": (0, 16), "E2": (16, 8), "EL": (32, 16), "EZ": (48, 32), "PC": (80, 16), "EH": (96, 32), "FS1": (128, 2),
@@ -33,10 +33,11 @@ for _i in range(8):
     SCRATCH["p%d" % _i] = ("psum", [128, 512], F32)
 SCRATCH["ts"] = ("dram", [4, 128, 64], F32)
 SCRATCH["tl"] = ("dram", [4, 128, 64], F32)
-NDMA = 20
+NDMA = 30
 SEMAPHORES = (["qv", "qa", "qt", "qg", "sent", "ah", "at", "a1", "a2", "a3"] + ["an%d" % i for i in range(4)]
               + ["af%d" % i for i in range(4)] + ["d%d" % i for i in range(NDMA)])
 BIG = float(2 ** 40)
+PH = ((0, 12), (12, 4))
 
 
 def A(name, c0=0, c1=None, cs=1, p0=0, p1=128, ps=1):
@@ -119,15 +120,18 @@ def rank_program(g, core, T, topo):
         else:
             add("g", lambda: g.iota(ap(o), pat, base, cm, allow_small_or_imprecise_dtypes=True), [o], [])
 
-    def sel(o, pat, op, base, cm, src=None):
+    def sel(o, pat, op, base, cm, src=None, fill=0.0):
         if src is None:
             n = 1
             for _s, c in pat: n *= c
             src = A("onb" if SB[o[0]][1] == BF else "on", 0, n)
-        add("g", lambda: g.affine_select(ap(o), ap(src), pat, op, 0.0, base, cm), [o], [src])
+        add("g", lambda: g.affine_select(ap(o), ap(src), pat, op, fill, base, cm), [o], [src])
 
     def zero(o):
         iota(o, [[0, len(range(o[1], o[2], o[3]))]])
+
+    def own(o, pat):
+        sel(o, [[-16 * s, c] for s, c in pat], OP.is_ge, 0, 1, o); sel(o, [[16 * s, c] for s, c in pat], OP.is_ge, 15, -1, o)
 
     def dma(qu, o, i, grp, w=()):
         groups[grp] = groups.get(grp, 0) + 1
@@ -161,426 +165,443 @@ def rank_program(g, core, T, topo):
                 nsent[0] += len(mine[c])
         add("g", lambda: g.remote_dma_fused(trs, local_sem=T.sem.sent), [], reads, "remote", w)
 
-    order = [(q + 1 + i) % 4 for i in range(3)]
+    def fc(k): return A("fc", k, k + 1)
+    AND, SHR, MUL, ADD, SUB = OP.bitwise_and, OP.logical_shift_right, OP.mult, OP.add, OP.subtract
+    EQL, GT, NE = OP.is_equal, OP.is_gt, OP.not_equal
+    blk = lambda n, s: A(n, 256 * s, 256 * s + 256)
+    near = [s for s in range(4) if s != q and topo.chip(T.cores[s]) == topo.chip(core)]
+    far = [s for s in range(4) if s != q and s not in near]
+    order = far + near
+
     dma("s", A("sh"), ("!", T.home[:, :]), "ldh")
     for r in order:
-        dma("s", A("sn", 256 * r, 256 * r + 256), ("!", T.nb[32 * r:32 * r + 32, :]), "ldn")
-    dma("s", A("ln", 256 * q, 256 * q + 256), ("!", T.nb[32 * q:32 * q + 32, :]), "own")
-    for r in order:
-        dma("s", A("sf", 256 * r, 256 * r + 256), ("!", T.feat[32 * r:32 * r + 32, :]), "ldf")
-    dma("s", A("lf", 256 * q, 256 * q + 256), ("!", T.feat[32 * q:32 * q + 32, :]), "owf")
-    iota(A("ip"), [[0, 1]], 0, 1)
-    iota(A("iof"), [[1, 256]])
-    iota(A("t0", 0, 128), [[64, 2], [0, 4], [4, 16]])
+        dma("a", blk("sf", r), ("!", T.feat[32 * r:32 * r + 32, :]), "ldf")
+    for r in order + [q]:
+        dma("s", blk("sn", r), ("!", T.nb[32 * r:32 * r + 32, :]), "ln%d" % r)
+    dma("a", blk("lf", q), ("!", T.feat[32 * q:32 * q + 32, :]), "owf")
+    PF = fc(8)
+    iota(PF, [[0, 1]], 0, 1)
+    iota(A("iof"), [[1, 16]])
+    iota(A("tb"), [[64, 2], [0, 4], [4, 16]])
     iota(A("t3", 0, 16), [[2, 2], [4, 4], [0, 2]], -16)
     iota(A("t3", 16, 48), [[16, 4], [0, 8]])
     iota(A("mH"), [[1, 8], [0, 16]])
     iota(A("t4", 0, 32), [[4, 2], [0, 4], [1, 4]])
+    zero(A("Li")); zero(A("I1"))
     send(lambda r: T.sh[:, :], T.lh[:, 16 * q:16 * q + 16], "ah", [A("sh")])
     iota(A("mL"), [[0, 8], [1, 2], [0, 16]])
-    zero(A("Li")); zero(A("VX"))
-    send(lambda r: T.sn[:, 256 * r:256 * r + 256], T.ln[:, 256 * q:256 * q + 256], "an%d" % q, [A("sn")])
-    send(lambda r: T.sf[:, 256 * r:256 * r + 256], T.lf[:, 256 * q:256 * q + 256], "af%d" % q, [A("sf")])
+    zero(A("VX")); iota(A("dP", 0, 16), [[0, 8], [8, 2]], 4096)
 
-    EQL, GT = OP.is_equal, OP.is_gt
+    P64, P32, G, P8, P4, P2 = [fc(k) for k in range(1, 7)]
+    X, X8, HX, RK, ODD, X1, X6, X13, EQ, XG = [fc(k) for k in range(9, 19)]
+    io = lambda a, b: A("iof", a, b)
+    d16 = lambda k: A("D16", k, k + 1)
+    BD, D8 = A("BD", 0, 8), A("BD", 8, 16)
+    ms(A("zr"), 0.0); ms(A("t1", 0, 24), 2.0)
+    scan(A("pw"), A("t1", 0, 24), A("zr", 0, 24), 2.0 ** -8, MUL, ADD)
+    ts(A("ic"), A("pw", 0, 8), PF, MUL, -0.496, ADD)
+    ms(A("onb"), 1.0)
+    cp(A("fc", 0, 8), A("ic"))
+    ms(A("on"), 1.0)
+    ts(X, G, -16.0, MUL, PF, ADD); ts(X8, P8, -8.0, MUL, PF, ADD); ts(HX, G, -2.0, MUL, P8, ADD)
+    ts(A("D16"), io(0, 16), X, EQL)
+    ts(BD, io(0, 8), G, EQL)
+    for c in range(2):
+        act(A("Wo", 256 * c, 256 * c + 256), A("zr"), AF.Silu)
+    act(A("inc", 0, 6), A("pw", 7, 13), scale=d16(7)); act(A("inc", 6, 12), A("pw", 7, 13), scale=d16(6))
+    act(A("Wl", 0, 1), A("zr", 0, 1))
+    act(A("sg"), A("D16"), scale=-2.0, bias=1.0)
+    small = [(fc(41), P4, -4.0, PF), (RK, P64, -4.0, G), (fc(43), P64, 4.0, fc(41)), (ODD, P32, -2.0, G), (X1, P2, -2.0, PF),
+             (X13, P8, -4.0, P2), (X6, X1, -1.0, X8), (XG, X, 16.0, G)]
+    for k in range(12):
+        act(A("Wl", 1 << k, 2 << k), A("Wl", 0, 1 << k), bias=A("inc", k, k + 1))
+        if k < len(small):
+            o, i, s, b = small[k]; act(o, i, scale=s, bias=b)
+    ts(fc(30), X, 14.5, OP.is_lt)
+    ts(fc(32), X, 11.5, OP.is_lt)
+    for qt in range(4):
+        ts(A("SQ", 128 * qt, 128 * qt + 128), A("tb"), float(qt), ADD, PF, EQL)
+    ts(A("Bw", 0, 1), fc(32), 2047.0, MUL, fc(30), ADD)
+    tt(fc(37), fc(32), fc(30), SUB)
+    ts(D8, io(0, 8), X8, EQL); tt(EQ, X8, G, EQL)
+    ts(A("EH"), A("t3", 16, 48), X, ADD); ts(A("mH"), A("mH"), X8, EQL)
+
+    def lst(name, src, col, zcol, c):
+        n = LISTS[name][1]
+        return [lambda: ts(A("t5", c, c + n), src, col, ADD, EQ, MUL), lambda: ts(A(name), A("t5", c, c + n), float(zcol), ADD)]
+    el, e1, e2 = lst("EL", A("t3", 0, 16), HX, 16, 0), lst("E1", io(0, 16), fc(21), 32, 16), lst("E2", A("t1", 48, 56), HX, 16, 32)
+    fill = [lambda: ts(fc(19), X8, 32.0, MUL), lambda: ts(fc(20), HX, 16.0, MUL), el[0],
+            lambda: ts(A("PC"), io(0, 16), fc(19), ADD, fc(20), ADD), el[1],
+            lambda: ts(fc(34), d16(14), -0.75, MUL, fc(37), SUB), lambda: ts(fc(21), fc(20), -32.0, ADD),
+            lambda: ts(A("t1", 48, 56), io(0, 8), 2.0, MUL, -16.0, ADD), e1[0], e2[0]]
+
+    def bits(k0, k1):
+        for k in range(k0, k1):
+            ts(A("Bw", 1 << k, 2 << k), A("Bw", 0, 1 << k), A("sg", k, k + 1), MUL)
+            if k < len(fill): fill[k]()
+    sel(A("Ib"), [[1, 128]], EQL, 0, -1)
+    ts(A("SU"), A("t4", 0, 32), fc(43), EQL)
+    for i, r in enumerate(order):
+        for c in range(2):
+            mm(P(4, 64 * i + 32 * c, 64 * i + 32 * c + 32), A("sf", 256 * r + 128 * c, 256 * r + 128 * c + 128), A("SU"))
+    for i, r in enumerate(order):
+        bits(3 * i, 3 * i + 3)
+        ts(A("sx", 320 * r, 320 * r + 256), blk("sn", r), -2048.0, ADD)
+        if i == 1:
+            for j, s in enumerate(order): ts(A("sx", 320 * s + 256, 320 * s + 320), P(4, 64 * j, 64 * j + 64), -2048.0, ADD)
+    send(lambda r: T.sx[:, 320 * r:320 * r + 320], T.lx[:, 320 * q:320 * q + 320], "an%d" % q,
+         [A("sx", 320 * r, 320 * r + 320) for r in order])
+    send(lambda r: T.sf[:, 256 * r:256 * r + 256], T.lf[:, 256 * q:256 * q + 256], "af%d" % q, [blk("sf", r) for r in order])
+    bits(9, 10)
+    ts(A("sx", 320 * q, 320 * q + 256), blk("sn", q), -2048.0, ADD)
 
     def spare(rho):
         dx = A("DX", 128 * rho, 128 * rho + 128)
         iota(dx, [[0, 8], [8, 2], [-255, 8]], 4096 + 256 * rho, 16)
-        sel(dx, [[0, 16], [-16, 8]], OP.is_ge, 0, 1, dx); sel(dx, [[0, 16], [16, 8]], OP.is_ge, 15, -1, dx)
-    iota(A("t0", 128, 320), [[0, 6], [-1, 4], [0, 8]], 3)
-    iota(A("t0", 320, 448), [[0, 16], [-64, 8]], 960)
-    iota(A("dP"), [[0, 8], [8, 2]], 4096)
-    iota(A("on"), [[0, 320]], 1)
-    sel(A("r8"), [[0, 16], [1, 8]], GT, 0, 0)
-    iota(A("onb"), [[0, 256]], 1)
-    zero(A("I1"))
+        own(dx, [[0, 16], [1, 8]])
+    sel(A("SV", 40, 56), [[1, 2], [16, 8]], EQL, 6, -1)
+    sel(A("SV", 40, 56), [[0, 2], [16, 8]], NE, 5, -1, A("SV", 40, 56), 1024.0)
+    iota(A("CW", 640, 832, 1, 0, 1), [[0, 16], [-64, 12]], 960); iota(A("CW", 832, 960, 1, 0, 1), [[0, 32], [-64, 4]], 192)
+    iota(A("t2", 64, 96), [[1, 4], [10, 8]], 1 - 80)
+    iota(A("t2", 128, 144), [[1, 2], [8, 4], [2, 2]])
+    iota(A("t2", 160, 192), [[2, 4], [8, 8]], -64)
+    iota(A("t1", 256, 264), [[1, 8]])
+    iota(A("t1", 264, 272, 4), [[4, 2]], 3); iota(A("t1", 275, 280, 4), [[4, 2]], 0)
+    for m in range(2):
+        iota(A("t1", 265 + 4 * m, 268 + 4 * m), [[1, 3]], 4 * m); iota(A("t1", 272 + 4 * m, 275 + 4 * m), [[1, 3]], 4 * m + 1)
+    sel(A("r12"), [[0, 16], [1, 12]], GT, 0, 0)
+    sel(A("r4"), [[0, 32], [1, 4]], GT, 0, 0)
     for h in range(2):
         zero(A("Kt", 256 * h, 256 * h + 128))
-    iota(A("Kt", 15, 512, 16), [[0, 32]], 1)
-    iota(A("Kt", 14, 512, 16), [[-128, 2], [0, 16]], 255, -1)
+    iota(A("Kt", 14, 512, 16), [[-512, 2], [0, 16]], 1020, -4)
     for h in range(2):
         sel(A("PJb", 256 * h, 256 * h + 256), [[1, 16], [128, 2], [16, 8]], EQL, -128 * h, -1)
-    sel(A("Ib"), [[1, 128]], EQL, 0, -1)
     iota(A("idc"), [[-128, 2], [0, 4], [-256, 4]], 1023, -1)
     for h in range(2):
         zero(A("Kk", 256 * h, 256 * h + 128))
-    iota(A("t2", 128, 144), [[1, 2], [8, 4], [2, 2]])
-    iota(A("t2", 160, 192), [[2, 4], [8, 8]], -64)
-    zero(A("tz")); zero(A("ow"))
+    sel(A("I"), [[1, 128]], EQL, 0, -1)
+    zero(A("ow"))
+    spare(0)
     for m in range(2):
         sel(A("Sh", 64 * m, 64 * m + 48), [[1, 48]], EQL, 64 * m + 16, -1)
         sel(A("Sh", 64 * m + 48, 64 * m + 64), [[1, 16]], EQL, 64 * m, -1)
         sel(A("Sh", 128 + 64 * m, 144 + 64 * m), [[1, 16]], EQL, 64 * m + 48, -1)
         sel(A("Sh", 144 + 64 * m, 192 + 64 * m), [[1, 48]], EQL, 64 * m, -1)
-    spare(0)
-    zero(A("ZD"))
-    iota(A("t1", 256, 264), [[1, 8]])
-    iota(A("t1", 264, 272, 4), [[4, 2]], 3); iota(A("t1", 275, 280, 4), [[4, 2]], 0)
-    for m in range(2):
-        iota(A("t1", 265 + 4 * m, 268 + 4 * m), [[1, 3]], 4 * m); iota(A("t1", 272 + 4 * m, 275 + 4 * m), [[1, 3]], 4 * m + 1)
-    iota(A("t3", 64, 384), [[0, 5], [1, 8], [0, 8]])
-    iota(A("t2", 64, 96), [[1, 4], [10, 8]], 1 - 80)
+    zero(A("ZD")); zero(A("zb"))
     zero(A("Fw", 4096, 4352)); zero(A("PM", 0, 256))
     sel(A("r15"), [[0, 16], [1, 15]], GT, 0, 0)
-    sel(A("r5"), [[0, 64], [1, 5]], GT, 0, 0)
+    for c in range(2):
+        sel(A("r5", 160 * c, 160 * c + 160), [[0, 32], [1, 5]], GT, 0, 0)
+    iota(A("CI", 0, 256, 1, 0, 1), [[-1, 256]], 255)
+    for ph, (f, n) in enumerate(PH):
+        iota(A("CW", 480 * ph, 480 * ph + 24 * n, 1, 0, 1), [[0, 6], [-256, 4], [0, n]], 768)
+        iota(A("CW", 480 * ph + 24 * n, 480 * ph + 40 * n, 1, 0, 1), [[0, 16 * n]], 1)
     zero(A("zq")); zero(A("Rf"))
+    for ph, (f, n) in enumerate(PH):
+        sm = A("SM", 288 * ph, 288 * ph + 24 * n)
+        iota(sm, [[0, 24 * n]], -1024); own(sm, [[0, 3], [1, 8], [0, n]])
+    iota(A("SF"), [[0, 24]], 1024); own(A("SF"), [[0, 3], [1, 8]])
+    zero(A("SV", 0, 40))
+    sel(A("SV", 0, 24), [[2, 3], [16, 8]], NE, 0, -1, A("SV", 0, 24), -1.0)
+    for m in range(2):
+        sel(A("SV", 9 + 4 * m, 12 + 4 * m), [[16, 3]], NE, 64 * m + 17, -1, A("SV", 9 + 4 * m, 12 + 4 * m), -1.0)
+        sel(A("SV", 16 + 4 * m, 19 + 4 * m), [[16, 3]], NE, 64 * m + 3, -1, A("SV", 16 + 4 * m, 19 + 4 * m), -1.0)
+    sel(A("SV", 24, 40), [[1, 2], [16, 8]], NE, 6, -1, A("SV", 24, 40), -1.0)
     for rho in range(1, 4):
         spare(rho)
     iota(A("PM", 1280, 1536), [[0, 256]], 255)
-    zero(A("l3", 64, 72))
+    zero(A("l3", 64, 72)); iota(A("fc", 52, 56), [[-8192, 4]], -12288)
     iota(A("mD"), [[0, 16], [1, 16]])
-    for h in range(2):
-        sel(A("PJ", 256 * h, 256 * h + 256), [[1, 16], [128, 2], [16, 8]], EQL, -128 * h, -1)
 
-    def fc(k): return A("fc", k, k + 1)
-    AND, SHR, MUL, ADD = OP.bitwise_and, OP.logical_shift_right, OP.mult, OP.add
-    for k, (s, m) in enumerate([(0, 15), (4, 7), (0, 7), (3, 1), (4, 3), (4, 1), (3, 15), (0, 6), (0, 1), (1, 3), (0, 127),
-                                (0, 3), (6, 1)]):
-        ts(A("ic", k, k + 1), A("ip"), s, SHR, m, AND)
-    ms(A("t1", 0, 16), 2.0); ms(A("zr"), 0.0)
-    cp(A("fc", 0, 11), A("ic", 0, 11)); cp(A("fc", 41, 43), A("ic", 11, 13))
-    X, G, X8, HX, RK, ODD, P8, X6, X1, X13, PF = [fc(k) for k in range(11)]
-    io = lambda a, b: A("iof", a, b)
-    d16 = lambda k: A("D16", k, k + 1)
-    BD, D8 = A("BD", 0, 8), A("BD", 8, 16)
-    scan(A("pw"), A("t1", 0, 16), A("zr", 0, 16), 0.5, MUL, ADD)
-    ts(A("D16"), io(0, 16), X, EQL)
-    ts(BD, io(0, 8), G, EQL)
-    ts(A("inc", 0, 6), A("pw", 0, 6), d16(7), MUL)
-    ts(A("inc", 6, 12), A("pw", 0, 6), d16(6), MUL)
-    act(A("Wl", 0, 1), A("zr", 0, 1))
-    for c in range(2):
-        act(A("Wo", 256 * c, 256 * c + 256), A("zr"), AF.Silu)
-    for k in range(12):
-        act(A("Wl", 1 << k, 2 << k), A("Wl", 0, 1 << k), bias=A("inc", k, k + 1))
-    ts(A("sg"), A("D16"), -2.0, MUL, 1.0, ADD)
-    ts(fc(30), d16(12), 4096.0, MUL, d16(14), ADD)
-    ts(fc(33), d16(12), 2.0 ** 29, MUL)
-    ts(fc(22), RK, -(2.0 ** 23), MUL, 3 * 2.0 ** 23, ADD)
-    ts(fc(31), d16(13), 256.0, MUL, fc(30), ADD)
-    ts(fc(34), d16(13), 2.0 ** 25, MUL, fc(33), ADD)
-    ts(fc(32), X, 11.5, OP.is_lt, 1024.0, MUL)
-    ts(fc(35), d16(14), 2.0 ** 15, MUL, fc(34), ADD)
-    tt(A("Bw", 0, 1), fc(31), fc(32), ADD)
-    ts(fc(36), fc(22), d16(15), MUL, fc(35), ADD)
-    ts(fc(37), fc(31), -1.0, MUL)
-    fill = [lambda qt=qt: ts(A("SQ", 128 * qt, 128 * qt + 128), A("t0", 0, 128), float(qt), ADD, PF, EQL) for qt in range(4)]
-    fill += [lambda: ts(D8, io(0, 8), X8, EQL), lambda: tt(fc(11), X8, G, EQL), lambda: ts(fc(12), X, 16.0, MUL, G, ADD),
-             lambda: ts(A("I"), io(0, 128), PF, EQL), lambda: ts(A("EH"), A("t3", 16, 48), X, ADD),
-             lambda: ts(A("mH"), A("mH"), X8, EQL)]
-    for k in range(10):
-        ts(A("Bw", 1 << k, 2 << k), A("Bw", 0, 1 << k), A("sg", k, k + 1), MUL)
-        fill[k]()
-    EQ, XG = fc(11), fc(12)
-
-    def lst(name, src, col, zcol):
-        n = LISTS[name][1]
-        ts(A("t2", 0, n), src, col, ADD, EQ, MUL)
-        ts(A(name), A("t2", 0, n), float(zcol), ADD)
-
-    near = [s for s in range(4) if s != q and topo.chip(T.cores[s]) == topo.chip(core)]
-    far = [s for s in range(4) if s != q and s not in near]
     bank = [0]; nsum = [0]
-    wf = lambda s: [("af%d" % s, got[s])]
+    wf = lambda s: [("af%d" % s, got[s])] if s != q else []
+    wn = lambda s: [("an%d" % s, got[s])] if s != q else []
 
-    def split(s):
-        raw = A("ln", 256 * s, 256 * s + 256); hi = A("nh", 256 * s, 256 * s + 256)
-        cp(hi, raw, [("an%d" % s, got[s])] if s != q else [])
-        tt(A("nl", 256 * s, 256 * s + 256), raw, hi, OP.subtract)
-
-    def spread(win, s, parts, banks=(0, 1, 2, 3, 6, 7)):
+    def spread(s, engs="aa"):
         for half in range(2):
-            b = banks[bank[0] % len(banks)]; bank[0] += 1
+            b = (0, 1, 2, 3, 6, 7)[bank[0] % 6]; bank[0] += 1
             for j in range(2):
-                sq = A("SQ", 128 * (2 * half + j), 128 * (2 * half + j) + 128)
-                for i, src in enumerate(parts):
-                    mm(P(b, 256 * j, 256 * j + 256), sq, A(src, 256 * s, 256 * s + 256), i == 0, i == len(parts) - 1)
-            act(A(win, 1024 * s + 512 * half, 1024 * s + 512 * half + 512), P(b, 0, 512))
+                mm(P(b, 256 * j, 256 * j + 256), A("SQ", 128 * (2 * half + j), 128 * (2 * half + j) + 128),
+                   A("sx" if s == q else "lx", 320 * s, 320 * s + 256), w=wn(s))
+            o = A("Nw", 1024 * s + 512 * half, 1024 * s + 512 * half + 512)
+            if engs[half] == "a": act(o, P(b, 0, 512), bias=2048.0)
+            else: ts(o, P(b, 0, 512), 2048.0, ADD)
 
     def sums(ss, eng, b=5):
         for i, s in enumerate(ss):
-            mm(P(b, 256 * i, 256 * i + 256, 1, 0, 32), A("SU"), A("lf", 256 * s, 256 * s + 256), w=wf(s) if s != q else ())
-        c0 = 256 * nsum[0]; n = 256 * len(ss); nsum[0] += len(ss)
-        if eng == "a": act(A("Vd", c0, c0 + n, 1, 0, 32), P(b, 0, n, 1, 0, 32))
-        else: cp(A("Vd", c0, c0 + n, 1, 0, 32), P(b, 0, n, 1, 0, 32))
+            if s == q: mm(P(b, 256 * i, 256 * i + 256, 1, 0, 32), A("SU"), blk("lf", s))
+            for c in range(2 if s != q else 0):
+                mm(P(b, 256 * i + 128 * c, 256 * i + 128 * c + 128, 1, 0, 32),
+                   A("lx", 320 * s + 256 + 32 * c, 320 * s + 288 + 32 * c), A("Ib"), w=wn(s))
+        c0 = 256 * nsum[0]; n = 256 * len(ss); nsum[0] += len(ss); off = 0.0 if ss == [q] else 2048.0
+        if eng == "a": act(A("Vd", c0, c0 + n, 1, 0, 32), P(b, 0, n, 1, 0, 32), bias=off)
+        else: ts(A("Vd", c0, c0 + n, 1, 0, 32), P(b, 0, n, 1, 0, 32), off, ADD)
         for i, s in enumerate(ss):
             dma("s", A("Wl", 1024 * s, 1024 * s + 1024, 1, 5, 128, 16), A("Vd", c0 + 256 * i, c0 + 256 * i + 256, 1, 0, 32), "su")
-    ts(fc(43), fc(42), 4.0, MUL, fc(41), ADD)
-    for S in range(2):
-        ts(fc(46 + S), d16(5), 1024.0, MUL, d16(6 + S), ADD)
-    ts(A("SU"), A("t4", 0, 32), fc(43), EQL)
-    for S in range(2):
-        ts(A("SV", 40 + 8 * S, 48 + 8 * S), BD, fc(46 + S), MUL)
-    NP = ["nh", "nl"]
-    split(q); spread("Nw", q, NP)
-    lst("EL", A("t3", 0, 16), HX, 16)
     ts(A("RH"), io(0, 4), float(4 * q), ADD, P8, EQL)
     ts(A("mL"), A("mL"), HX, EQL)
     cp(A("lh", 16 * q, 16 * q + 16), A("sh"))
+    e1[1](); e2[1]()
+    tt(A("t1", 32, 48), A("pw", 7, 23), A("D16"), MUL)
+    bits(10, 11)
+    red(fc(38), A("t1", 32, 48), ADD)
+    spread(q); sums([q], "a")
+    act(A("Wo", 512, 1024), A("Wo", 0, 512))
+    for o, i, s, b in [(fc(22), RK, -(2.0 ** 23), 3 * 2.0 ** 23), (fc(24), HX, 5.0, None), (fc(35), d16(15), fc(22), None),
+                       (fc(49), A("sg", 10, 11), A("sg", 11, 12), None), (fc(36), fc(34), 2.0 ** 15, fc(35)),
+                       (fc(40), d16(15), -12.0 * 2 ** 22, fc(37)), (fc(25), X6, 4.0, X1), (fc(27), X1, 5.0, 4.0),
+                       (fc(50), fc(36), -1.0, None), (fc(26), HX, 2.0, fc(25)), (fc(28), HX, 40.0, fc(27)),
+                       (fc(51), fc(32), -(2.0 ** -12), None), (fc(29), X13, 80.0, fc(28)), (fc(47), X13, 1.0, fc(28)),
+                       (fc(39), fc(38), fc(51), None), (fc(48), fc(47), 1.0, -3.0)]:
+        act(o, i, scale=s, bias=b)
     cp(A("hf"), A("lh"), [("ah", gotall)])
     for r in range(4):
         tt(A("hx", 128 * r, 128 * r + 128), IND(A("hf"), A("EH", 8 * r, 8 * r + 8)), A("mH"), MUL)
         for m in range(2):
             mm(P(4, 8 * m + 2 * r, 8 * m + 2 * r + 2), A("hx", 128 * r, 128 * r + 128), A("RH", 2 * m, 2 * m + 2))
-    sums([q], "a"); spread("Fw", q, ["lf"])
-    act(A("Bw", 1024, 2048), A("Bw", 0, 1024), scale=A("sg", 10, 11))
-    ts(fc(13), X8, 32.0, MUL); ts(fc(14), HX, 16.0, MUL)
-    e0, e1 = A("I", 0, 1), A("I", 1, 2)
-    ts(fc(15), e0, 2.0 ** 30, MUL); ts(fc(16), e1, 2.0 ** 22, MUL)
-    ts(A("PC"), io(0, 16), fc(13), ADD, fc(14), ADD)
-    ts(A("t1", 0, 256), io(0, 256), -1.0, MUL, 255.0, ADD)
-    ts(fc(17), RK, 0.5, GT, d16(1), MUL); ts(fc(18), RK, 2.5, OP.is_lt, d16(3), MUL)
-    ts(A("CI"), A("t1", 0, 256), e1, MUL, e0, ADD)
-    tt(fc(19), fc(17), d16(2), ADD); tt(fc(20), fc(18), d16(4), ADD)
-    for t in range(5):
-        ts(A("SF", 8 * t, 8 * t + 8), BD, 2.0 ** 32 if t < 3 else 1024.0, MUL)
-    for t, col in enumerate([d16(0), fc(19), fc(20), d16(6), d16(7)]):
-        ts(A("SV", 8 * t, 8 * t + 8), BD, col, MUL, -2.0 ** 22 if t < 3 else 1.0, MUL)
-    cp(A("Li", 0, 16), P(4, 0, 16)); cp(A("VX", 0, 80, 5), P(4, 0, 16))
-    tt(fc(49), A("sg", 10, 11), A("sg", 11, 12), MUL)
+    cp(A("Li", 0, 16), P(4, 0, 16)); act(A("VX", 0, 80, 5), P(4, 0, 16))
     tt(A("XL"), IND(A("Li"), A("EL")), A("mL"), MUL)
+    sums(near, "a"); spread(near[0])
     for u in range(2):
         mm(P(4, 16 + u, 32, 2), A("XL", 128 * u, 128 * u + 128), D8)
     ts(A("Bw", 2048, 3072), A("Bw", 0, 1024), A("sg", 11, 12), MUL)
-    ts(A("Bw", 3072, 4096), A("Bw", 0, 1024), fc(49), MUL)
-    split(near[0]); spread("Nw", near[0], NP)
     cp(A("Lu"), P(4, 16, 32))
-    split(far[0]); spread("Nw", far[0], NP)
-    split(far[1])
-    ts(fc(25), X6, 4.0, MUL, X1, ADD); ts(fc(27), X1, 5.0, MUL, 4.0, ADD)
-    ts(fc(26), HX, 2.0, MUL, fc(25), ADD); ts(fc(28), HX, 40.0, MUL, fc(27), ADD)
-    ts(A("FS1"), io(0, 2), 4.0, MUL, fc(26), ADD); ts(fc(29), X13, 80.0, MUL, fc(28), ADD)
-    ts(fc(48), X13, -3.0, ADD, fc(28), ADD)
-    ts(A("FS2"), io(0, 4), 10.0, MUL, fc(29), ADD); ts(A("FS3"), io(0, 4), 10.0, MUL, fc(48), ADD)
-    sums(far, "v"); sums(near, "v", 4)
-    spread("Nw", far[1], NP)
-    for ph in range(2):
-        ts(A("CW", 320 * ph, 320 * ph + 192), A("t0", 128, 320), fc(15), MUL, fc(16), ADD)
-        ts(A("CW", 320 * ph + 192, 320 * ph + 320), A("t0", 320, 448), -512.0 * ph, ADD, e0, MUL)
-    spread("Fw", near[0], ["lf"])
+    sums(far, "v")
+    spread(far[0], "av"); spread(far[1], "av")
+    for s in [q] + near + far:
+        dma("s", A("Fd", 1024 * s, 1024 * s + 1024, 1, 0, 32), blk("lf", s), "f1", wf(s))
+    for c in range(1, 4):
+        dma("s", A("Wo", 1024 * c, 1024 * c + 1024), A("Wo", 0, 1024), "wz")
+    for gg in range(8):
+        dma("s", A("Fw", 0, 4096, 1, 16 * gg, 16 * gg + 16), A("Fd", 0, 4096, 1, 16 * (gg // 4), 16 * (gg // 4) + 16), "f2")
 
     def late(k):
         if k == 0:
-            ts(fc(21), fc(14), -32.0, ADD); ts(fc(24), HX, 5.0, MUL)
-            tt(A("t1", 16, 32), A("pw"), A("D16"), MUL)
-            lst("E1", io(0, 16), fc(21), 32)
-            red(fc(38), A("t1", 16, 32), ADD)
-            ts(A("t1", 0, 8), io(0, 8), 2.0, MUL, -16.0, ADD)
-            ts(fc(39), fc(38), fc(32), MUL, -(2.0 ** -21), MUL)
-            lst("E2", A("t1", 0, 8), HX, 16)
-            ts(fc(40), d16(15), -12.0 * 2 ** 20, MUL, fc(37), ADD)
-            ts(A("D16b", 0, 16), A("D16"), 64.0, MUL); cp(A("D16b", 16, 32), A("D16")); ts(A("D256"), A("D16"), 1.0 / 16, MUL)
-            ts(A("SS", 0, 8), BD, fc(39), MUL)
-            ts(A("SS", 8, 16), BD, fc(36), MUL, -1.0, MUL)
-            ts(A("SS", 16, 24), BD, fc(40), MUL)
-            ts(A("dP"), A("dP"), XG, ADD)
-            ms(A("NK"), -BIG)
+            act(A("Bw", 3072, 4096), A("Bw", 0, 1024), scale=fc(49))
+            act(A("D16b", 0, 16), A("D16"), scale=64.0); act(A("D16b", 16, 32), A("D16"))
         if k == 1:
-            ts(A("SC"), A("t1", 256, 280), G, EQL, fc(36), MUL)
-            ts(A("SM", 0, 192), A("t3", 64, 256), G, EQL, -2.0 ** 32, MUL)
-            ts(A("SM", 192, 320), A("t3", 256, 384), G, EQL, -1024.0, MUL)
-            lst("EZ", A("t2", 64, 96), fc(24), 80)
+            act(A("DW"), A("Ib"), scale=fc(37))
+            act(A("dP", 0, 16), A("dP", 0, 16), bias=XG)
+            act(A("SS", 0, 8), BD, scale=fc(39)); act(A("SS", 8, 16), BD, scale=fc(50)); act(A("SS", 16, 24), BD, scale=fc(40))
+            act(A("dP", 16, 32), A("dP", 0, 16), bias=-2047.5)
+            act(A("SS", 24, 32), A("SS", 16, 24), scale=-1.0)
+            act(A("SS", 32, 56), A("SS", 0, 24)); act(A("SS", 56, 64), A("zr", 0, 8))
+            act(A("NI"), A("Ib"), scale=-(2.0 ** 23)); act(A("D256"), A("D16"), scale=1.0 / 16)
+            act(A("NK"), A("zr", 0, 80)); act(A("DD"), A("zr", 0, 80), bias=2.0 ** 17)
+            act(A("NK", 0, 80, 5), A("zr", 0, 16), bias=-BIG)
         if k == 2:
-            cp(A("FR", 0, 16), A("t2", 128, 144)); ts(A("FR", 16, 32), A("t2", 128, 144), 4.0, ADD)
-            lst("EY", A("t2", 160, 192), HX, 64)
+            ez, ey = lst("EZ", A("t2", 64, 96), fc(24), 80, 48), lst("EY", A("t2", 160, 192), HX, 64, 80)
+            ts(A("SC"), A("t1", 256, 280), G, EQL, fc(36), MUL)
+            ez[0](); ey[0]()
+            ts(A("FS1"), io(0, 2), 4.0, MUL, fc(26), ADD)
+            ez[1](); ey[1]()
         if k == 3:
-            ts(A("mD"), A("mD"), X, EQL)
+            ts(A("FS2"), io(0, 4), 10.0, MUL, fc(29), ADD); ts(A("FS3"), io(0, 4), 10.0, MUL, fc(48), ADD)
+            cp(A("FR", 0, 16), A("t2", 128, 144)); ts(A("FR", 16, 32), A("t2", 128, 144), 4.0, ADD)
 
-    def open_scores():
-        for b in range(4):
-            mm(P(b, 0, 320), A("CI", 128 * (b % 2), 128 * (b % 2) + 128, 1, 0, 2),
-               A("CW", 320 * (b // 2), 320 * (b // 2) + 320, 1, 0, 2), True, False)
+    def SCO(ph, h, c0, c1, cs=1):
+        return P(5 + h, c0, c1, cs) if ph == 0 else P(7, 64 * h + c0, 64 * h + c1, cs)
+
+    def open_scores(k, part):
+        one = A("onb", 0, 128, 1, 0, 1)
+        if part == 1:
+            mm(SCO(0, 0, 0, 192), one, A("CW", 640, 832, 1, 0, 1), True, False)
+            return
+        mm(SCO(0, 1, 0, 192), one, A("CW", 640, 832, 1, 0, 1), True, False)
+        mm(P(7, 0, 128), one, A("CW", 832, 960, 1, 0, 1), True, False)
+        for ph, (f, n) in enumerate(PH):
+            for h in range(2 if k > 1 else 0):
+                mm(P(2 * ph + h, 0, 40 * n), one, A("CW", 480 * ph, 480 * ph + 40 * n, 1, 0, 1), True, False)
+                mm(P(2 * ph + h, 0, 24 * n), A("CI", 128 * h, 128 * h + 128, 1, 0, 1), A("onb", 0, 24 * n, 1, 0, 1), False, False)
     WO = A("Wo", 0, 4096)
 
     for k in range(1, 6):
         nr = k - 1
         if k > 1:
-            tt(A("PM", 256 * nr, 256 * nr + 256), IND(A("Fw"), A("Wu")), A("M", 0, 256) if k > 2 else A("PM", 0, 256), OP.max)
             blocks = [i for i in range(3 * nr) if i != 3 * nr - 3]
             for n, i in enumerate(blocks):
                 rho, t = i // 3 + 1, i % 3
                 o = A("CD", 256 * i, 256 * i + 256); src = IND(WO, A("CL", 16 * i, 16 * i + 16))
-                if n % 2 == 0 or k == 2: act(o, src)
+                if n % 2 == 0: act(o, src)
                 else: cp(o, src)
                 for h in range(2):
                     c0 = 256 + 15 * h + 3 * rho + t
                     mm(P(5, c0, 496, 30), A("CD", 256 * i + 128 * h, 256 * i + 128 * h + 128), A("SC", 8 * t, 8 * t + 8), False,
                        i == blocks[-1] and h == 1)
-            open_scores()
+            pm = lambda: tt(blk("PM", nr), IND(A("Fw"), A("Wu")), A("M", 0, 256) if k > 2 else A("PM", 0, 256), OP.max)
+            if len(blocks) % 2: pm()
+            open_scores(k, 0)
             scan(A("cum"), A("r15"), P(5, 256, 496), 0.0, MUL, OP.max)
-            tt(A("val"), A("VX", 0, 80), A("cum", 2, 240, 3), OP.subtract)
+            tt(A("val"), A("VX", 0, 80), A("cum", 2, 240, 3), SUB)
             scan(A("sv"), A("r5", 0, 80), A("val"), 0.0, MUL, OP.max)
             cp(A("vi"), A("sv", 4, 80, 5))
             ts(A("Li", 0, 16), A("vi"), 4095, AND)
-            tt(A("XL"), IND(A("Li"), A("EL")), A("mL"), MUL)
             for u in range(2):
+                tt(A("XL", 128 * u, 128 * u + 128), IND(A("Li"), A("EL", 8 * u, 8 * u + 8)), A("mL", 128 * u, 128 * u + 128), MUL)
                 mm(P(4, 16 + u, 32, 2), A("XL", 128 * u, 128 * u + 128), D8)
-            tt(A("Rf", 0, 16), A("sv", 4, 80, 5), A("Li", 0, 16), OP.subtract)
+            act(A("VX", 0, 80), A("val"), AF.Relu)
+            tt(A("Rf", 0, 16), A("sv", 4, 80, 5), A("Li", 0, 16), SUB)
             if k == 5:
                 ts(A("sm", 0, 80), A("val"), 4096.0, OP.is_ge)
                 scan(A("sv"), A("r5", 0, 80), A("sm", 0, 80), 0.0, MUL, ADD)
                 ts(A("sm", 80, 96), A("sv", 4, 80, 5), 4.0, EQL, 4096.0, MUL)
                 tt(A("Rf", 0, 16), A("Rf", 0, 16), A("sm", 80, 96), ADD)
             act(A("XR"), IND(A("Rf"), A("E2")))
-            ts(A("ge"), A("val"), 0.0, OP.is_ge)
-            tt(A("zq", 0, 80), P(5, 256, 496, 3), A("ge"), EQL)
+            tt(A("zq", 0, 80), P(5, 256, 496, 3), A("VX", 0, 80), EQL)
             cp(A("Lu"), P(4, 16, 32))
             mm(P(4, 32, 48), A("DX", 0, 128), A("D16"), True, False)
             mm(P(4, 32, 48), A("XR"), A("D256"), False, True)
             act(A("cG"), IND(A("Nw"), A("Lu")))
-            tt(A("zq", 0, 80), A("zq", 0, 80), A("ZD"), MUL)
+            if len(blocks) % 2 == 0: pm()
             ts(A("Mu"), P(4, 32, 48), -4096.0, ADD)
+            open_scores(k, 1)
+            if k == 5: tt(A("zq", 0, 80), A("zq", 0, 80), A("ZD"), MUL)
             act(A("M", 0, 256), IND(A("PM", 0, 256 * k if k < 5 else 1536), A("Mu")))
         else:
             cp(A("cG"), IND(A("Nw"), A("Lu")))
-            open_scores()
-            for c in range(1, 8):
-                dma("s", A("Wo", 512 * c, 512 * c + 512), A("Wo", 0, 512), "wz", wf(far[1]))
+            open_scores(k, 0); open_scores(k, 1)
+            late(0)
         tr(A("cT"), A("cG"))
         cp(A("cu"), IND(A("cT"), A("PC")))
         if k > 1:
-            if k < 5:
-                cp(A("XZ", 0, 128 * nr), IND(A("zq"), A("EZ", 0, 8 * nr)))
-            else:
+            if k == 5:
                 cp(A("s3"), IND(A("zq"), A("FS3")))
                 send(lambda r: T.s3[:, 16 * r:16 * r + 16], T.l3[:, 16 * q:16 * q + 16], "a3", [A("s3")])
             for b in range(4):
-                mm(P(b, 0, 320), A("M", 128 * (b % 2), 128 * (b % 2) + 128), A("SM"), False, False)
+                ph, h = b // 2, b % 2; n = PH[ph][1]; mh = A("M", 128 * h, 128 * h + 128)
+                mm(P(b, 0, 24 * n), mh, A("SM", 288 * ph, 288 * ph + 24 * n), False, False)
+                mm(SCO(ph, h, 0, 16 * n), mh, A("SM", 288 * ph, 288 * ph + 16 * n), False, False)
 
-        def post(ph):
-            bs = (2 * ph, 2 * ph + 1)
-            if k == 1:
-                for b in bs:
-                    scan(A("sc", 128 * b, 128 * b + 128), A("r8"), P(b, 192, 320), 0.0, MUL, OP.max)
-                return
-            for b in bs:
-                if ph == 1: cp(A("am", 64 * b, 64 * b + 64), P(b, 0, 64))
-            for t in (1, 2):
-                for b in bs:
-                    tt(A("am", 64 * b, 64 * b + 64), P(b, 64 * t, 64 * t + 64), A("am", 64 * b, 64 * b + 64), OP.min)
-            for b in bs:
-                for S in range(2):
-                    tt(A("ss", 128 * b + 64 * S, 128 * b + 64 * S + 64), P(b, 192 + 64 * S, 256 + 64 * S),
-                       A("am", 64 * b, 64 * b + 64), OP.min)
-            for b in bs:
-                scan(A("sc", 128 * b, 128 * b + 128), A("r8"), A("ss", 128 * b, 128 * b + 128), 0.0, MUL, OP.max)
-        for p in range(16):
-            if k == 1:
-                o = A("Vd", 256 * p, 256 * p + 256); src = IND(A("Wl"), A("cu", 16 * p, 16 * p + 16))
-                if p % 2 == 0 or p == 15: act(o, src)
-                else: cp(o, src)
-                for h in range(2):
-                    mm(P(2 * (p // 8) + h, 192 + p % 8, 320, 8), A("Vd", 256 * p + 128 * h, 256 * p + 128 * h + 128), A("SV", 40, 56),
-                       False, p % 8 == 7)
-                if p == 15:
-                    late(0); spread("Fw", far[0], ["lf"], (6, 7)); post(0)
-                continue
-            w = 1 if p < 2 else 2 - 2 * (p % 2)
-            if p == 0: act(A("M", 256, 512), A("M", 0, 256))
-            if p % 2 == 0:
-                act(A("Vd", 256 * p, 256 * p + 512), IND(A("Wl"), A("cu", 16 * p, 16 * p + 32)))
-            if w:
-                tt(A("Fd", 256 * p, 256 * (p + w)), IND(A("Fw", 0, 4096), A("cu", 16 * p, 16 * (p + w))), A("M", 0, 256 * w), OP.max)
-            for h in range(2):
-                o = P(2 * (p // 8) + h, p % 8, 320, 8); c0 = 256 * p + 128 * h
-                mm(o, A("Vd", c0, c0 + 128), A("SV", 0, 40), False, False)
-                mm(o, A("Fd", c0, c0 + 128), A("SF"), False, p % 8 == 7)
-            if p == 0 and k == 5: cp(A("l3", 16 * q, 16 * q + 16), A("s3", 16 * q, 16 * q + 16))
-            if p == 6 and k == 5: cp(A("XZ"), IND(A("l3"), A("EY")), [("a3", gotall)])
-            if p == (1 if k < 5 else 7):
-                for rho in range(nr):
-                    mm(P(4, 64 + 16 * rho, 80 + 16 * rho), A("DX", 128 * rho, 128 * rho + 128), A("D16"), True, False)
-                    mm(P(4, 64 + 16 * rho, 80 + 16 * rho), A("XZ", 128 * rho, 128 * rho + 128), A("D16"), False, True)
-            if p == 12: cp(A("Zu", 0, 16 * nr), P(4, 64, 64 + 16 * nr))
-            if p == 10:
-                for b in range(2): act(A("am", 64 * b, 64 * b + 64), P(b, 0, 64))
-            if p == 15: post(0)
+        def short(ph, h):
+            n = PH[ph][1]; c = 960 * ph + 40 * n * h
+            act(A("pen", c, c + 40 * n), P(2 * ph + h, 0, 40 * n), AF.Relu, bias=1.0, scale=-1.0)
+
+        def bar(ph, h):
+            n = PH[ph][1]; c = 960 * ph + 40 * n * h
+            mm(SCO(ph, h, 0, 16 * n), A("Ib"), A("pen", c + 24 * n, c + 40 * n), False, False)
+            for o0, o1, t in ((0, 16, 0), (0, 16, 1), (0, 8, 2), (8, 16, 0)):
+                mm(SCO(ph, h, o0 * n, o1 * n), A("NI"), A("pen", c + 8 * n * t, c + n * (8 * t + o1 - o0)), False,
+                   o0 == 8 and (ph == 0 or h == 1))
+
+        def best(ph, h):
+            if ph == 0: scan(A("sc", 192 * h, 192 * h + 192), A("r12"), SCO(0, h, 0, 192), 0.0, MUL, OP.max)
+            else: scan(A("sc", 384, 512), A("r4"), P(7, 0, 128), 0.0, MUL, OP.max)
+
+        def zlist():
+            for rho in range(nr):
+                mm(P(0, 16 * rho, 16 + 16 * rho), A("XZ", 128 * rho, 128 * rho + 128), A("D16"))
 
         def clear(rho):
             act(IND(A("Wo" if k < 5 else "Wf"), A("Zu", 16 * rho, 16 * rho + 16)), A("zr"), AF.Silu)
-        for rho in range(nr if k < 5 else 2):
-            clear(rho)
-        post(1)
-        tt(A("bi"), A("sc", 7, 256, 8), A("sc", 263, 512, 8), OP.max)
+        for p in range(16):
+            ph = int(p >= PH[1][0]); f, n = PH[ph]
+            if k == 1:
+                o = blk("Vd", p); src = IND(A("Wl"), A("cu", 16 * p, 16 * p + 16))
+                if p % 2 == 0: act(o, src)
+                else: cp(o, src)
+                for h in range(2):
+                    mm(SCO(ph, h, p - f, 16 * n, n), A("Vd", 256 * p + 128 * h, 256 * p + 128 * h + 128),
+                       A("SV", 40, 56), False, p == f + n - 1 and (ph == 0 or h == 1))
+                continue
+            w = 1 if p < 2 else 2 - 2 * (p % 2)
+            if p == 0: act(A("M", 256, 512), A("M", 0, 256))
+            if p % 2 == 0 and p < 14:
+                act(A("Vd", 256 * p, 256 * p + 512), IND(A("Wl"), A("cu", 16 * p, 16 * p + 32)))
+            if p == 14: short(0, 0); act(blk("Vd", p), IND(A("Wl"), A("cu", 16 * p, 16 * p + 16))); short(0, 1); bar(0, 0)
+            if w:
+                tt(A("Fd", 256 * p, 256 * (p + w)), IND(A("Fw", 0, 4096), A("cu", 16 * p, 16 * (p + w))), A("M", 0, 256 * w), OP.max)
+            if p == 15: cp(blk("Vd", p), IND(A("Wl"), A("cu", 16 * p, 16 * p + 16)))
+            for h in range(2):
+                c0 = 256 * p + 128 * h
+                mm(SCO(ph, h, p - f, 16 * n, n), A("Fd", c0, c0 + 128), A("SF", 0, 16), False, False)
+                mm(P(2 * ph + h, p - f, 24 * n, n), A("Fd", c0, c0 + 128), A("SF"), False, False)
+                mm(P(2 * ph + h, p - f, 40 * n, n), A("Vd", c0, c0 + 128), A("SV", 0, 40), False, p == f + n - 1)
+            if p == 0 and k == 5: cp(A("l3", 16 * q, 16 * q + 16), A("s3", 16 * q, 16 * q + 16))
+        if k > 1:
+            short(1, 0); short(1, 1); bar(0, 1); bar(1, 0); bar(1, 1)
+        best(0, 0)
+        if 1 < k < 5:
+            tt(A("zq", 0, 80), A("zq", 0, 80), A("ZD"), MUL)
+            tt(A("XZ", 0, 128 * nr), IND(A("zq"), A("EZ", 0, 8 * nr)), A("DX", 0, 128 * nr), ADD)
+        if k == 5:
+            tt(A("XZ"), IND(A("l3"), A("EY")), A("DX"), ADD, [("a3", gotall)])
+        best(0, 1)
+        if k == 1: late(1); late(2)
+        if k == 2: late(3)
+        best(1, 0)
+        tt(A("bi"), A("sc", 11, 384, 12), A("sc", 387, 512, 4), OP.max)
+        zlist()
+        mm(P(5, 0, 256), A("DW"), A("onb", 0, 256), True, False)
         ts(A("I1", 0, 32), A("bi"), 63, AND)
-        ts(A("gi", 0, 32), A("bi"), 14, SHR)
+        if k > 1:
+            cp(A("Zu", 0, 16 * nr), P(0, 0, 16 * nr))
+            if k < 5: act(A("DD"), A("val"), AF.Relu, bias=2.0 ** 17, scale=-(2.0 ** 17))
+            for rho in range(min(nr, 2)):
+                clear(rho)
+        else:
+            ts(A("gi", 0, 32), A("bi"), 0xFFFC00, AND)
         cp(A("X1"), IND(A("I1"), A("E1")))
         for S in range(2):
             mm(P(4, 0, 16), A("X1", 128 * S, 128 * S + 128), A("D16b", 16 * S, 16 * S + 16), S == 0, S == 1)
-        ts(A("gi", 32, 64), A("bi"), 10, SHR, 15, AND)
+        if k > 1: ts(A("gi", 0, 32), A("bi"), 0xFFFC00, AND)
+        ts(A("Kt", 15, 512, 16), A("bi"), 1023.5, GT)
         cp(A("Kt", 12, 512, 16), A("gi", 0, 32))
-        cp(A("Kt", 13, 512, 16), A("gi", 32, 64))
-        for h in range(2):
-            mm(P(5, 0, 256), A("Kt", 256 * h, 256 * h + 128), A("PJb", 256 * h, 256 * h + 256), h == 0, h == 1)
         cl = A("CL", 48 * nr, 48 * nr + 16)
         cp(cl, P(4, 0, 16))
-        act(A("Kp"), P(5, 0, 256), bias=fc(37))
-        act(A("La"), IND(A("Bw"), cl))
-        if k < 5:
-            ts(A("gi", 64, 96), A("bi"), 0xFFFC00, AND)
-            cp(A("ctf"), P(4, 0, 16))
-            tt(A("Kk", 0, 512, 16), A("gi", 64, 96), A("idc"), ADD)
-            for h in range(2):
-                mm(P(4, 256 + 128 * h, 384 + 128 * h), A("Kt", 256 * h, 256 * h + 128), A("Ib"), True, False)
-                mm(P(4, 256 + 128 * h, 384 + 128 * h), A("Kk", 256 * h, 256 * h + 128), A("I"), False, True)
-        else:
-            ts(A("t1", 0, 80), A("val"), 4096.0, OP.is_ge)
-            ts(A("t2", 0, 80), A("val"), 0.0, OP.max)
-            cp(A("gi", 0, 80), A("t2", 0, 80))
-            ts(A("gi", 0, 80), A("gi", 0, 80), 4095, AND)
-            ts(A("t2", 0, 80), A("gi", 0, 80), 1.0, ADD)
-        tt(A("R"), IND(A("Bw"), cl), A("Kp"), ADD)
-        act(A("Lo"), A("La"), scale=ODD)
+        tt(A("Kt", 13, 512, 16), A("gi", 0, 32), A("Kt", 12, 512, 16), SUB)
         for h in range(2):
-            mm(P(4, 128 + h, 176, 2), A("R", 128 * h, 128 * h + 128), A("SS"))
-        if 1 < k < 5:
-            ts(A("ge"), A("val"), 0.0, OP.is_lt, -BIG, MUL)
-            ts(A("VX", 0, 80), A("val"), 0.0, OP.max)
-            tt(A("NK"), A("NK"), A("ge"), OP.min)
-        if k == 1: late(2)
-        if k == 5: late(3)
-        act(A("st", 16, 48), P(4, 144, 176))
-        act(A("st", 0, 16), P(4, 128, 144), bias=2047.5)
+            mm(P(5, 0, 256), A("Kt", 256 * h, 256 * h + 128), A("PJb", 256 * h, 256 * h + 256), False, h == 1)
+        cp(A("La"), IND(A("Bw"), cl))
+        tt(A("R"), P(5, 0, 256), A("La"), ADD)
+        for h in range(2):
+            mm(P(7, 128 + h, 192, 2), A("R", 128 * h, 128 * h + 128), A("SS", 32 * h, 32 * h + 32))
+        if nr < 2: act(A("Lo"), A("La"), scale=ODD)
+        act(A("st", 16, 64), P(7, 144, 192))
+        if k < 5:
+            tt(A("Kk", 0, 512, 16), A("gi", 0, 32), A("idc"), ADD)
+            cp(A("ctf"), P(4, 0, 16))
         n = 0
         for gg in (0, 2, 4, 6, 1, 3, 5, 7):
             p0 = 16 * (gg - gg % 2); p1 = 16 * gg + 16
             for h in range(2):
-                b = (0, 1, 2)[n % 3] if h == 0 else (3, 6, 7)[n % 3]
+                b = (0, 1, 2)[n % 3] if h == 0 else (3, 6, 5)[n % 3]
                 mm(P(b, 0, 256), A("Lo" if gg % 2 else "La", 128 * h, 128 * h + 128, 1, p0, p1), A("R", 0, 256, 1, p0, p1))
                 col = A("acc", 2 * gg + h, 2 * gg + h + 1)
                 if h == 0: red(col, P(b, 0, 256), OP.max)
-                else: act(A("CD", 256 * n, 256 * n + 256), P(b, 0, 256), AF.Relu, bias=A("st", 33 + 2 * gg, 34 + 2 * gg), acc=col)
+                else: act(blk("CD", n), P(b, 0, 256), AF.Relu, bias=A("st", 33 + 2 * gg, 34 + 2 * gg), acc=col)
             n += 1
-            if n == 2:
-                ts(A("tz", 0, 16, 2), A("st", 32, 48, 2), -1.0, MUL)
-                ts(A("st", 48, 64), A("st", 16, 32), -(2.0 ** 25), OP.is_le, -1.0, ADD)
-                tt(A("st", 64, 80), A("st", 0, 16), A("dP"), OP.subtract)
-                tt(A("st", 48, 64), A("st", 48, 64), A("tz"), ADD)
+            if n == 2: tt(A("st", 64, 80), P(7, 128, 144), A("dP", 16, 32), SUB)
+            if n == 2 and nr >= 2: ts(A("Lo"), A("La"), ODD, MUL)
         if k < 5:
+            for h in range(2):
+                mm(P(4, 256 + 128 * h, 384 + 128 * h), A("Kt", 256 * h, 256 * h + 128), A("Ib"), True, False)
+                mm(P(4, 256 + 128 * h, 384 + 128 * h), A("Kk", 256 * h, 256 * h + 128), A("I"), False, True)
             for t in range(2):
                 mm(P(5, 16 * t, 16 + 16 * t), A("Sh", 128 * t, 128 * t + 128), A("ctf"))
             act(A("Va"), P(4, 256, 512))
         else:
             act(A("o2", 16, 32), A("st", 16, 32), scale=-(2.0 ** -15))
-        act(A("st", 80, 96), A("st", 0, 16), bias=4096.0 * k if k < 5 else 1.0)
-        if k == 5: clear(2); clear(3)
+        act(A("st", 80, 96), P(7, 128, 144), bias=2047.5 + (4096.0 * k if k < 5 else 1.0))
         tt(A("al"), A("acc"), A("st", 48, 64), EQL)
         tt(A("ow", 0, 16), A("al"), A("st", 64, 80), MUL)
         if k < 5:
-            ts(A("sm", 0, 16), A("al"), -1.0, ADD, BIG, MUL)
             tt(A("XW"), IND(A("ow"), A("E2")), A("DX", 0, 128), ADD)
             mm(P(4, 48, 64), A("XW"), A("D16"))
-            tt(A("NK", k, 80, 5), A("sm", 0, 16), A("st", 16, 32), ADD)
+            act(A("NK", k, 80, 5), A("st", 16, 32))
+            act(A("DD", k, 80, 5), A("al"), bias=2.0 ** 17, scale=-(2.0 ** 17))
+            for rho in range(2, nr):
+                clear(rho)
+            act(A("ZD", k, 80, 5), A("st", 64, 80), bias=-256.0 * nr)
             cp(A("CL", 48 * nr + 16, 48 * nr + 48), P(5, 0, 32))
             tt(A("VX", k, 80, 5), A("al"), A("st", 80, 96), MUL)
-            for t in range(3):
-                act(A("NK3", t, 240, 3), A("NK"))
-            act(A("NK3", 3 * k, 240, 15), A("sm", 0, 16))
-            act(A("ZD", k, 80, 5), A("st", 64, 80), bias=-256.0 * nr)
             cp(A("Wu"), P(4, 48, 64))
-            if k == 1: spread("Fw", far[1], ["lf"], (6, 7))
-            mm(P(5, 256, 496), A("I"), A("NK3"), True, False)
+            mm(P(5, 256, 496), A("Ib"), A("zb"), True, False)
+            for t in (1, 2):
+                mm(P(5, 256 + t, 496, 3), A("I"), A("NK"), False, False)
+            for rho in range(k):
+                mm(P(5, 256 + 3 * rho, 496, 15), A("I"), A("NK", rho, 80, 5), False, False)
+            for t in range(3):
+                mm(P(5, 256 + t, 496, 3), A("NI"), A("DD"), False, False)
             cp(IND(A("Wo"), A("Wu")), A("Va"))
             gr = "w%d" % k
             dma("s", A("Wl", 0, 4096, 1, 0, 128, 16), A("Wo", 0, 4096, 1, 0, 128, 16), gr)
@@ -595,37 +616,43 @@ def rank_program(g, core, T, topo):
                 send(lambda r: T.ts[r], T.tl[q], "at", [], [("@ts", 0)])
                 for s in order:
                     dma("s", A("Wf", 0, 4096, 1, 32 * s, 32 * s + 32, 16), ("!", T.tl[s]), "tf", [("at", gotall)])
-            if k == 1: late(1)
 
-    tt(A("o2", 0, 16), A("ow", 0, 16), A("dP"), ADD)
-    cp(A("t1", 5, 81, 5), A("al"))
+    tt(A("o2", 0, 16), A("ow", 0, 16), A("dP", 0, 16), ADD)
     cp(A("s1"), IND(A("o2"), A("FS1")))
     send(lambda r: T.s1[:, 8 * r:8 * r + 8], T.l1[:, 8 * q:8 * q + 8], "a1", [A("s1")])
+    clear(2)
+    cp(A("gi", 0, 80), A("VX", 0, 80))
+    ts(A("t1", 0, 80), A("val"), 4096.0, OP.is_ge, 8192.0, MUL)
+    ts(A("gi", 0, 80), A("gi", 0, 80), 4095, AND)
+    ts(A("t1", 5, 81, 5), A("al"), 8192.0, MUL)
+    tt(A("t2", 0, 80), A("gi", 0, 80), A("sm", 0, 80), ADD)
     scan(A("t0", 0, 80), A("r5", 0, 80), A("t1", 1, 81), 0.0, MUL, ADD)
-    cp(A("t2", 5, 81, 5), A("st", 80, 96))
-    tt(A("t0", 0, 80), A("t0", 0, 80), A("t1", 1, 81), MUL)
-    for s in range(4):
-        ts(A("t3", 80 * s, 80 * s + 80), A("t0", 0, 80), float(s + 1), EQL)
-    for s in range(4):
-        tt(A("t4", 80 * s, 80 * s + 80), A("t3", 80 * s, 80 * s + 80), A("t2", 1, 81), MUL)
-    scan(A("t5", 0, 320), A("r5"), A("t4", 0, 320), 0.0, MUL, ADD)
+    tt(A("t2", 5, 81, 5), A("al"), A("st", 80, 96), MUL)
     cp(A("l1", 8 * q, 8 * q + 8), A("s1", 8 * q, 8 * q + 8))
-    ts(A("s2"), IND(A("t5", 0, 320), A("FS2")), -1.0, ADD)
+    tt(A("t0", 0, 80), A("t0", 0, 80), A("t2", 1, 81), ADD)
+    for s in range(4):
+        act(A("t4", 80 * s, 80 * s + 80), A("t0", 0, 80), AF.Abs, bias=A("fc", 52 + s, 53 + s))
+    clear(3)
+    ts(A("t3", 0, 320), A("r5"), -8192.0, MUL, 8192.0, ADD)
+    scan(A("t5", 0, 320), A("t3", 0, 320), A("t4", 0, 320), 0.0, ADD, OP.min)
+    ts(A("s2"), IND(A("t5", 0, 320), A("FS2")), 4096.0, OP.min, -2048.0, ADD)
     send(lambda r: T.s2[:, 16 * r:16 * r + 16], T.l2[:, 16 * q:16 * q + 16], "a2", [A("s2")])
+    ts(A("mD"), A("mD"), X, EQL)
     cp(A("l2", 16 * q, 16 * q + 16), A("s2", 16 * q, 16 * q + 16))
     tt(A("XL"), IND(A("l1"), A("FR", 0, 16)), A("mD"), MUL, [("a1", gotall)])
     act(A("cG"), IND(A("l1"), A("FR", 16, 32)), w=[("a1", gotall)])
     for h in range(2):
-        mm(P(4, 8 * h, 8 * h + 8), A("XL", 128 * h, 128 * h + 128), BD)
-    for h in range(2):
         mm(P(5, 128 * h, 128 * h + 128), A("cG", 128 * h, 128 * h + 128), A("I"))
-    cp(A("Wu"), P(4, 0, 16))
+    for h in range(2):
+        mm(P(4, 8 * h, 8 * h + 8), A("XL", 128 * h, 128 * h + 128), BD)
+    cp(A("PJ"), A("PJb"))
     act(A("Va"), P(5, 0, 256))
+    cp(A("Wu"), P(4, 0, 16))
     cp(IND(A("Wf"), A("Wu")), A("Va"))
     dma("s", ("!", T.yt[:, :]), A("Wf", 0, 4096, 1, 0, 128, 16), "yt")
     for h in range(2):
         mm(P(0, 0, 256, 1, 0, 32), A("l2", h, 64, 2), A("PJ", 256 * h, 256 * h + 256), h == 0, h == 1, [("a2", gotall)])
-    act(A("yo", 0, 256, 1, 0, 32), P(0, 0, 256, 1, 0, 32))
+    act(A("yo", 0, 256, 1, 0, 32), P(0, 0, 256, 1, 0, 32), bias=2047.0, scale=-1.0)
     dma("a", ("!", T.yb[:, :]), A("yo", 0, 256, 1, 0, 32), "yb")
 
     gsem = {n: "d%d" % i for i, n in enumerate(groups)}

@@ -4,29 +4,29 @@ from concourse.mybir import AluOpType as OP, AxisListType as AX, ActivationFunct
 F32, BF, I32, U16, F16 = "float32", "bfloat16", "int32", "uint16", "float16"
 SB = {
     "Fw": (4352, BF), "Nw": (4096, F32), "Wo": (5120, F32), "Wl": (4096, F32), "Bw": (4096, BF), "Wf": (5120, F32),
-    "Fd": (4096, BF), "Vd": (4096, F32), "CD": (3072, BF), "PM": (1536, BF), "M": (512, BF),
-    "sh": (16, I32), "lh": (64, I32), "sn": (1024, I32), "sf": (1024, BF), "sx": (1280, F16), "lx": (1280, F16), "lf": (1024, BF),
-    "hf": (64, F32), "hx": (512, F32),
+    "Fd": (4096, BF), "Vd": (4096, F32), "CD": (4096, BF), "PM": (1536, BF), "M": (512, BF),
+    "sh": (16, I32), "lh": (64, I32), "sn": (1024, I32), "sf": (1024, BF), "sx": (1152, F16), "lx": (1152, F16), "lf": (1024, BF),
+    "hf": (64, F32), "hx": (512, F16),
     "ic": (8, I32), "fc": (56, F32), "iof": (16, F32), "D16": (16, F32), "D16b": (32, BF), "BD": (16, F32),
     "I": (128, F32), "t0": (512, F32), "t1": (512, F32), "t2": (512, F32), "t3": (512, F32), "t4": (512, F32),
     "t5": (512, F32), "tb": (128, BF), "pw": (24, F32), "sg": (16, F32), "inc": (16, F32), "EU": (336, U16),
-    "mL": (256, F32), "DX": (512, F32), "dP": (32, F32), "on": (256, F32), "onb": (320, BF),
-    "r15": (240, F32), "r5": (320, F32), "r12": (192, F32), "r4": (128, F32), "PJ": (512, F16), "PJb": (512, BF), "Kt": (512, BF),
-    "Kk": (512, F32), "idc": (32, F32), "CI": (256, BF), "CW": (1152, BF), "SF": (24, BF), "SM": (384, BF), "SV": (56, F32),
-    "SU": (32, BF), "SC": (24, BF), "Sh": (256, F32), "SS": (64, BF), "SQ": (512, F16), "mH": (128, F32), "RH": (4, F32),
-    "mD": (256, F32), "Ib": (128, BF), "D256": (16, F32), "zr": (256, F32), "zb": (240, BF), "NI": (128, BF), "DW": (128, BF),
+    "mL": (256, F32), "DX": (512, F32), "dP": (48, F32), "on": (256, F32), "onb": (320, BF),
+    "r15": (240, F32), "r5": (80, F32), "r12": (192, F32), "r4": (128, F32), "PJ": (512, F16), "PJb": (512, BF), "Kt": (512, BF),
+    "Kk": (512, F32), "idc": (32, F32), "CI": (256, BF), "CW": (1152, BF), "SF": (40, BF), "SM": (384, BF), "SV": (40, F32),
+    "SU": (8, BF), "SC": (24, BF), "Sh": (256, F32), "SS": (64, BF), "SQ": (512, F16), "mH": (128, F32), "RH": (4, F16),
+    "mD": (128, F32), "Ib": (128, BF), "D256": (16, F32), "zr": (256, F32), "zb": (240, BF), "NI": (128, BF), "DW": (128, BF),
     "VX": (88, F32), "NK": (80, F32), "DD": (80, BF), "cum": (240, F32), "val": (80, F32), "sv": (80, F32), "vi": (16, I32),
     "Li": (24, I32), "Rf": (24, F32), "XL": (256, F32), "XR": (128, F32), "cG": (256, F32),
     "cT": (256, F32), "cu": (256, U16), "zq": (88, F32), "ZD": (80, F32), "XZ": (512, F32),
-    "pen": (1280, BF), "sc": (512, F32), "bi": (32, I32), "I1": (40, I32), "gi": (96, I32), "X1": (256, BF),
+    "pen": (1280, BF), "sc": (512, F32), "bi": (32, I32), "I1": (40, I32), "gi": (112, I32), "X1": (256, BF),
     "CL": (240, U16), "ctf": (16, F32), "La": (256, BF), "Lo": (256, BF), "R": (256, BF),
-    "st": (96, F32), "acc": (16, F32), "al": (16, F32), "ow": (24, F32), "XW": (128, F32),
+    "st": (96, F32), "acc": (16, F32), "al": (24, F32), "ow": (32, F32), "XW": (128, F32),
     "Va": (256, F32), "sm": (96, F32),
     "o2": (32, F32), "s1": (32, F32), "l1": (32, F32), "s2": (64, F16), "l2": (64, F16), "yo": (256, F32),
     "s3": (64, F32), "l3": (72, F32),
 }
 LISTS = {"E1": (0, 16), "E2": (16, 8), "EL": (32, 16), "EZ": (48, 32), "PC": (80, 16), "EH": (96, 32), "FS1": (128, 2),
-         "FS2": (132, 4), "FR": (144, 32), "FS3": (176, 4), "EY": (192, 32), "Lu": (224, 16), "Mu": (240, 16), "Wu": (256, 16),
+         "FS2": (132, 4), "FR": (144, 16), "FS3": (176, 4), "EY": (192, 32), "Lu": (224, 16), "Mu": (240, 16), "Wu": (256, 16),
          "Zu": (272, 64)}
 SCRATCH = {k: ("sbuf", [128, n], d) for k, (n, d) in SB.items()}
 for _i in range(8):
@@ -98,9 +98,9 @@ def rank_program(g, core, T, topo):
     def scan(o, a, b, i0, o0, o1): add("v", lambda: g.vector.tensor_tensor_scan(ap(o), ap(a), ap(b), i0, o0, o1), [o], [a, b])
     def tr(o, i): add("v", lambda: g.vector.transpose(ap(o), ap(i)), [o], [i])
 
-    def ts(o, a, s1, o0, s2=None, o1=None):
+    def ts(o, a, s1, o0, s2=None, o1=None, w=()):
         if s2 is None:
-            add("v", lambda: g.vector.tensor_scalar(ap(o), ap(a), ap(s1), None, o0), [o], [a, s1])
+            add("v", lambda: g.vector.tensor_scalar(ap(o), ap(a), ap(s1), None, o0), [o], [a, s1], None, w)
         else:
             add("v", lambda: g.vector.tensor_scalar(ap(o), ap(a), ap(s1), ap(s2), o0, o1), [o], [a, s1, s2])
 
@@ -186,7 +186,6 @@ def rank_program(g, core, T, topo):
     iota(A("t3", 0, 16), [[2, 2], [4, 4], [0, 2]], -16)
     iota(A("t3", 16, 48), [[16, 4], [0, 8]])
     iota(A("mH"), [[1, 8], [0, 16]])
-    iota(A("t4", 0, 32), [[4, 2], [0, 4], [1, 4]])
     zero(A("Li")); zero(A("I1"))
     send(lambda r: T.sh[:, :], T.lh[:, 16 * q:16 * q + 16], "ah", [A("sh")])
     iota(A("mL"), [[0, 8], [1, 2], [0, 16]])
@@ -206,15 +205,16 @@ def rank_program(g, core, T, topo):
     ts(X, G, -16.0, MUL, PF, ADD); ts(X8, P8, -8.0, MUL, PF, ADD); ts(HX, G, -2.0, MUL, P8, ADD)
     ts(A("D16"), io(0, 16), X, EQL)
     ts(BD, io(0, 8), G, EQL)
-    for c in range(2):
-        act(A("Wo", 256 * c, 256 * c + 256), A("zr"), AF.Silu)
+    act(A("Wo", 0, 256), A("zr"), AF.Silu)
+    zero(A("Wo", 256, 1024))
     act(A("inc", 0, 6), A("pw", 7, 13), scale=d16(7)); act(A("inc", 6, 12), A("pw", 7, 13), scale=d16(6))
     act(A("Wl", 0, 1), A("zr", 0, 1))
     act(A("sg"), A("D16"), scale=-2.0, bias=1.0)
     small = [(fc(41), P4, -4.0, PF), (RK, P64, -4.0, G), (fc(43), P64, 4.0, fc(41)), (ODD, P32, -2.0, G), (X1, P2, -2.0, PF),
-             (X13, P8, -4.0, P2), (X6, X1, -1.0, X8), (XG, X, 16.0, G)]
+             (X13, P8, -4.0, P2), (X6, P2, 16.0, X1), (XG, X, 16.0, G)]
     for k in range(12):
-        act(A("Wl", 1 << k, 2 << k), A("Wl", 0, 1 << k), bias=A("inc", k, k + 1))
+        n = min(1 << k, 1024)
+        act(A("Wl", 1 << k, (1 << k) + n), A("Wl", 0, n), bias=A("inc", k, k + 1))
         if k < len(small):
             o, i, s, b = small[k]; act(o, i, scale=s, bias=b)
     ts(fc(30), X, 14.5, OP.is_lt)
@@ -240,30 +240,45 @@ def rank_program(g, core, T, topo):
             ts(A("Bw", 1 << k, 2 << k), A("Bw", 0, 1 << k), A("sg", k, k + 1), MUL)
             if k < len(fill): fill[k]()
     sel(A("Ib"), [[1, 128]], EQL, 0, -1)
-    ts(A("SU"), A("t4", 0, 32), fc(43), EQL)
+    ts(A("SU"), io(0, 8), fc(43), EQL)
+
+    def pieces(ss, b):
+        for i, r in enumerate(ss):
+            for c in range(2):
+                for m in range(2):
+                    mm(P(b, 16 * i + 2 * c + m, 16 * i + 16, 4), A("sf" if r != q else "lf", 256 * r + 128 * c, 256 * r + 128 * c + 128),
+                       A("SU", 4 * m, 4 * m + 4))
+        yield
+        cp(A("X1", 0, 16 * len(ss)), P(b, 0, 16 * len(ss)))
+        yield
+        for i, r in enumerate(ss):
+            cp(A("sx", 288 * r + 256, 288 * r + 288, 2), A("X1", 16 * i, 16 * i + 16))
+            tt(A("sx", 288 * r + 257, 288 * r + 288, 2), P(b, 16 * i, 16 * i + 16), A("X1", 16 * i, 16 * i + 16), SUB)
+        yield
+    step = pieces(order, 4); next(step)
     for i, r in enumerate(order):
-        for c in range(2):
-            mm(P(4, 64 * i + 32 * c, 64 * i + 32 * c + 32), A("sf", 256 * r + 128 * c, 256 * r + 128 * c + 128), A("SU"))
-    for i, r in enumerate(order):
-        bits(3 * i, 3 * i + 3)
-        ts(A("sx", 320 * r, 320 * r + 256), blk("sn", r), -2048.0, ADD)
-        if i == 1:
-            for j, s in enumerate(order): ts(A("sx", 320 * s + 256, 320 * s + 320), P(4, 64 * j, 64 * j + 64), -2048.0, ADD)
-    send(lambda r: T.sx[:, 320 * r:320 * r + 320], T.lx[:, 320 * q:320 * q + 320], "an%d" % q,
-         [A("sx", 320 * r, 320 * r + 320) for r in order])
+        bits(3 * i, 3 * i + 3 if i < 2 else 7)
+        if i == 1: next(step)
+        ts(A("sx", 288 * r, 288 * r + 256), blk("sn", r), -2048.0, ADD)
+        if i == 1: next(step)
+    send(lambda r: T.sx[:, 288 * r:288 * r + 288], T.lx[:, 288 * q:288 * q + 288], "an%d" % q,
+         [A("sx", 288 * r, 288 * r + 288) for r in order])
     send(lambda r: T.sf[:, 256 * r:256 * r + 256], T.lf[:, 256 * q:256 * q + 256], "af%d" % q, [blk("sf", r) for r in order])
-    bits(9, 10)
-    ts(A("sx", 320 * q, 320 * q + 256), blk("sn", q), -2048.0, ADD)
+    step = pieces([q], 5); next(step); next(step)
+    bits(7, 8); next(step)
+    ts(A("sx", 288 * q, 288 * q + 256), blk("sn", q), -2048.0, ADD)
+    bits(8, 10)
 
     def spare(rho):
         dx = A("DX", 128 * rho, 128 * rho + 128)
         iota(dx, [[0, 8], [8, 2], [-255, 8]], 4096 + 256 * rho, 16)
         own(dx, [[0, 16], [1, 8]])
-    sel(A("SV", 40, 56), [[1, 2], [16, 8]], EQL, 6, -1)
-    sel(A("SV", 40, 56), [[0, 2], [16, 8]], NE, 5, -1, A("SV", 40, 56), 1024.0)
+    sel(A("SF", 24, 40), [[1, 2], [16, 8]], EQL, 6, -1)
+    for row in (5, 8):
+        sel(A("SF", 24, 40), [[0, 2], [16, 8]], NE, row, -1, A("SF", 24, 40), 1024.0)
     iota(A("CW", 640, 832, 1, 0, 1), [[0, 16], [-64, 12]], 960); iota(A("CW", 832, 960, 1, 0, 1), [[0, 32], [-64, 4]], 192)
     iota(A("t2", 64, 96), [[1, 4], [10, 8]], 1 - 80)
-    iota(A("t2", 128, 144), [[1, 2], [8, 4], [2, 2]])
+    iota(A("t2", 128, 144), [[1, 2], [8, 4], [4, 2]], 2)
     iota(A("t2", 160, 192), [[2, 4], [8, 8]], -64)
     iota(A("t1", 256, 264), [[1, 8]])
     iota(A("t1", 264, 272, 4), [[4, 2]], 3); iota(A("t1", 275, 280, 4), [[4, 2]], 0)
@@ -280,7 +295,7 @@ def rank_program(g, core, T, topo):
     for h in range(2):
         zero(A("Kk", 256 * h, 256 * h + 128))
     sel(A("I"), [[1, 128]], EQL, 0, -1)
-    zero(A("ow"))
+    zero(A("al", 16, 24)); zero(A("st", 80, 88))
     spare(0)
     for m in range(2):
         sel(A("Sh", 64 * m, 64 * m + 48), [[1, 48]], EQL, 64 * m + 16, -1)
@@ -290,8 +305,7 @@ def rank_program(g, core, T, topo):
     zero(A("ZD")); zero(A("zb"))
     zero(A("Fw", 4096, 4352)); zero(A("PM", 0, 256))
     sel(A("r15"), [[0, 16], [1, 15]], GT, 0, 0)
-    for c in range(2):
-        sel(A("r5", 160 * c, 160 * c + 160), [[0, 32], [1, 5]], GT, 0, 0)
+    sel(A("r5"), [[0, 16], [1, 5]], GT, 0, 0)
     iota(A("CI", 0, 256, 1, 0, 1), [[-1, 256]], 255)
     for ph, (f, n) in enumerate(PH):
         iota(A("CW", 480 * ph, 480 * ph + 24 * n, 1, 0, 1), [[0, 6], [-256, 4], [0, n]], 768)
@@ -300,18 +314,22 @@ def rank_program(g, core, T, topo):
     for ph, (f, n) in enumerate(PH):
         sm = A("SM", 288 * ph, 288 * ph + 24 * n)
         iota(sm, [[0, 24 * n]], -1024); own(sm, [[0, 3], [1, 8], [0, n]])
-    iota(A("SF"), [[0, 24]], 1024); own(A("SF"), [[0, 3], [1, 8]])
+    iota(A("SF", 0, 24), [[0, 24]], 1024); own(A("SF", 0, 24), [[0, 3], [1, 8]])
     zero(A("SV", 0, 40))
     sel(A("SV", 0, 24), [[2, 3], [16, 8]], NE, 0, -1, A("SV", 0, 24), -1.0)
     for m in range(2):
         sel(A("SV", 9 + 4 * m, 12 + 4 * m), [[16, 3]], NE, 64 * m + 17, -1, A("SV", 9 + 4 * m, 12 + 4 * m), -1.0)
         sel(A("SV", 16 + 4 * m, 19 + 4 * m), [[16, 3]], NE, 64 * m + 3, -1, A("SV", 16 + 4 * m, 19 + 4 * m), -1.0)
     sel(A("SV", 24, 40), [[1, 2], [16, 8]], NE, 6, -1, A("SV", 24, 40), -1.0)
-    for rho in range(1, 4):
-        spare(rho)
-    iota(A("PM", 1280, 1536), [[0, 256]], 255)
-    zero(A("l3", 64, 72)); iota(A("fc", 52, 56), [[-8192, 4]], -12288)
-    iota(A("mD"), [[0, 16], [1, 16]])
+
+    def rest():
+        iota(A("mD"), [[0, 8], [1, 16]])
+        for rho in range(1, 4):
+            spare(rho)
+        iota(A("PM", 1280, 1536), [[0, 256]], 255)
+        iota(A("ow", 0, 16), [[0, 16]], 1); iota(A("tb", 0, 16, 1, 0, 1), [[1, 16]])
+        zero(A("l3", 64, 72)); iota(A("fc", 52, 56), [[-8192, 4]], -12288)
+        zero(A("t3", 0, 320)); sel(A("t3", 0, 320), [[0, 64], [1, 5]], NE, 0, 0, A("t3", 0, 320), 8192.0)
 
     bank = [0]; nsum = [0]
     wf = lambda s: [("af%d" % s, got[s])] if s != q else []
@@ -319,55 +337,48 @@ def rank_program(g, core, T, topo):
 
     def spread(s, engs="aa"):
         for half in range(2):
-            b = (0, 1, 2, 3, 6, 7)[bank[0] % 6]; bank[0] += 1
+            b = (0, 1, 2, 3, 6, 7, 2, 3)[bank[0]]; bank[0] += 1
             for j in range(2):
                 mm(P(b, 256 * j, 256 * j + 256), A("SQ", 128 * (2 * half + j), 128 * (2 * half + j) + 128),
-                   A("sx" if s == q else "lx", 320 * s, 320 * s + 256), w=wn(s))
+                   A("sx" if s == q else "lx", 288 * s, 288 * s + 256), w=wn(s))
             o = A("Nw", 1024 * s + 512 * half, 1024 * s + 512 * half + 512)
             if engs[half] == "a": act(o, P(b, 0, 512), bias=2048.0)
             else: ts(o, P(b, 0, 512), 2048.0, ADD)
 
     def sums(ss, eng, b=5):
-        for i, s in enumerate(ss):
-            if s == q: mm(P(b, 256 * i, 256 * i + 256, 1, 0, 32), A("SU"), blk("lf", s))
-            for c in range(2 if s != q else 0):
-                mm(P(b, 256 * i + 128 * c, 256 * i + 128 * c + 128, 1, 0, 32),
-                   A("lx", 320 * s + 256 + 32 * c, 320 * s + 288 + 32 * c), A("Ib"), w=wn(s))
-        c0 = 256 * nsum[0]; n = 256 * len(ss); nsum[0] += len(ss); off = 0.0 if ss == [q] else 2048.0
-        if eng == "a": act(A("Vd", c0, c0 + n, 1, 0, 32), P(b, 0, n, 1, 0, 32), bias=off)
-        else: ts(A("Vd", c0, c0 + n, 1, 0, 32), P(b, 0, n, 1, 0, 32), off, ADD)
-        for i, s in enumerate(ss):
-            dma("s", A("Wl", 1024 * s, 1024 * s + 1024, 1, 5, 128, 16), A("Vd", c0 + 256 * i, c0 + 256 * i + 256, 1, 0, 32), "su")
+        s = ss[0]
+        for r in range(4):
+            mm(P(b, 0, 128, 1, 32 * r, 32 * r + 32), A("sx" if s == q else "lx", 288 * s + 256, 288 * s + 288), A("Ib"), w=wn(s))
+        (act if eng == "a" else cp)(A("Vd", 128 * s, 128 * s + 128), P(b, 0, 128))
+        for m in range(2):
+            for e, row in enumerate((5, 8)):
+                dma("s", A("Wl", 1024 * s, 1024 * s + 1024, 1, 64 * m + row, 64 * m + 64, 16),
+                    A("Vd", 128 * s, 128 * s + 128, 1, 2 * m + e, 128, 4), "su")
     ts(A("RH"), io(0, 4), float(4 * q), ADD, P8, EQL)
     ts(A("mL"), A("mL"), HX, EQL)
     cp(A("lh", 16 * q, 16 * q + 16), A("sh"))
     e1[1](); e2[1]()
     tt(A("t1", 32, 48), A("pw", 7, 23), A("D16"), MUL)
-    bits(10, 11)
+    ts(A("Wl", 3072, 4096), A("Wl", 1024, 2048), A("inc", 11, 12), ADD)
     red(fc(38), A("t1", 32, 48), ADD)
     spread(q); sums([q], "a")
-    act(A("Wo", 512, 1024), A("Wo", 0, 512))
-    for o, i, s, b in [(fc(22), RK, -(2.0 ** 23), 3 * 2.0 ** 23), (fc(24), HX, 5.0, None), (fc(35), d16(15), fc(22), None),
-                       (fc(49), A("sg", 10, 11), A("sg", 11, 12), None), (fc(36), fc(34), 2.0 ** 15, fc(35)),
-                       (fc(40), d16(15), -12.0 * 2 ** 22, fc(37)), (fc(25), X6, 4.0, X1), (fc(27), X1, 5.0, 4.0),
-                       (fc(50), fc(36), -1.0, None), (fc(26), HX, 2.0, fc(25)), (fc(28), HX, 40.0, fc(27)),
-                       (fc(51), fc(32), -(2.0 ** -12), None), (fc(29), X13, 80.0, fc(28)), (fc(47), X13, 1.0, fc(28)),
-                       (fc(39), fc(38), fc(51), None), (fc(48), fc(47), 1.0, -3.0)]:
-        act(o, i, scale=s, bias=b)
-    cp(A("hf"), A("lh"), [("ah", gotall)])
+    act(A("Bw", 1024, 2048), A("Bw", 0, 1024), scale=A("sg", 10, 11))
+    ts(A("Bw", 2048, 3072), A("Bw", 0, 1024), A("sg", 11, 12), MUL)
+    ts(A("hf"), A("lh"), -2048.0, ADD, w=[("ah", gotall)])
+    sums(near, "a"); spread(near[0])
     for r in range(4):
         tt(A("hx", 128 * r, 128 * r + 128), IND(A("hf"), A("EH", 8 * r, 8 * r + 8)), A("mH"), MUL)
         for m in range(2):
             mm(P(4, 8 * m + 2 * r, 8 * m + 2 * r + 2), A("hx", 128 * r, 128 * r + 128), A("RH", 2 * m, 2 * m + 2))
-    cp(A("Li", 0, 16), P(4, 0, 16)); act(A("VX", 0, 80, 5), P(4, 0, 16))
+    ts(A("Li", 0, 16), P(4, 0, 16), 2048.0, ADD); act(A("VX", 0, 80, 5), P(4, 0, 16), bias=2048.0)
     tt(A("XL"), IND(A("Li"), A("EL")), A("mL"), MUL)
-    sums(near, "a"); spread(near[0])
+    act(A("Bw", 3072, 4096), A("Bw", 2048, 3072), scale=A("sg", 10, 11))
+    sums(far[:1], "v", 0); sums(far[1:], "v", 1)
+    spread(far[0], "va")
     for u in range(2):
         mm(P(4, 16 + u, 32, 2), A("XL", 128 * u, 128 * u + 128), D8)
-    ts(A("Bw", 2048, 3072), A("Bw", 0, 1024), A("sg", 11, 12), MUL)
     cp(A("Lu"), P(4, 16, 32))
-    sums(far, "v")
-    spread(far[0], "av"); spread(far[1], "av")
+    spread(far[1], "va")
     for s in [q] + near + far:
         dma("s", A("Fd", 1024 * s, 1024 * s + 1024, 1, 0, 32), blk("lf", s), "f1", wf(s))
     for c in range(1, 4):
@@ -377,27 +388,36 @@ def rank_program(g, core, T, topo):
 
     def late(k):
         if k == 0:
-            act(A("Bw", 3072, 4096), A("Bw", 0, 1024), scale=fc(49))
-            act(A("D16b", 0, 16), A("D16"), scale=64.0); act(A("D16b", 16, 32), A("D16"))
+            for o, i, s, b in [(fc(22), RK, -(2.0 ** 23), 3 * 2.0 ** 23), (fc(24), HX, 5.0, None), (fc(51), fc(32), -(2.0 ** -12), None),
+                               (fc(35), d16(15), fc(22), None), (fc(40), d16(15), -12.0 * 2 ** 22, fc(37)),
+                               (fc(39), fc(38), fc(51), None), (fc(36), fc(34), 2.0 ** 15, fc(35)),
+                               (A("D16b", 0, 16), A("D16"), 64.0, None), (A("D16b", 16, 32), A("D16"), None, None),
+                               (fc(50), fc(36), -1.0, None)]:
+                act(o, i, scale=s, bias=b)
+        if k == 7:
+            for o, i, s, b in [(fc(31), P4, -24.0, X6), (fc(27), X1, 5.0, 4.0), (fc(23), X, 16.0, 4096.0), (fc(25), P8, -16.0, fc(31)),
+                               (fc(28), HX, 40.0, fc(27)), (fc(26), HX, 2.0, fc(25)), (fc(47), X13, 1.0, fc(28)),
+                               (fc(29), X13, 80.0, fc(28)), (fc(48), fc(47), 1.0, -3.0)]:
+                act(o, i, scale=s, bias=b)
         if k == 1:
             act(A("DW"), A("Ib"), scale=fc(37))
             act(A("dP", 0, 16), A("dP", 0, 16), bias=XG)
             act(A("SS", 0, 8), BD, scale=fc(39)); act(A("SS", 8, 16), BD, scale=fc(50)); act(A("SS", 16, 24), BD, scale=fc(40))
-            act(A("dP", 16, 32), A("dP", 0, 16), bias=-2047.5)
+            act(A("dP", 16, 32), A("dP", 0, 16), bias=-2047.5); act(A("dP", 32, 48), A("dP", 0, 16), bias=-65536.0, scale=16.0)
             act(A("SS", 24, 32), A("SS", 16, 24), scale=-1.0)
             act(A("SS", 32, 56), A("SS", 0, 24)); act(A("SS", 56, 64), A("zr", 0, 8))
             act(A("NI"), A("Ib"), scale=-(2.0 ** 23)); act(A("D256"), A("D16"), scale=1.0 / 16)
             act(A("NK"), A("zr", 0, 80)); act(A("DD"), A("zr", 0, 80), bias=2.0 ** 17)
             act(A("NK", 0, 80, 5), A("zr", 0, 16), bias=-BIG)
-        if k == 2:
-            ez, ey = lst("EZ", A("t2", 64, 96), fc(24), 80, 48), lst("EY", A("t2", 160, 192), HX, 64, 80)
-            ts(A("SC"), A("t1", 256, 280), G, EQL, fc(36), MUL)
-            ez[0](); ey[0]()
-            ts(A("FS1"), io(0, 2), 4.0, MUL, fc(26), ADD)
-            ez[1](); ey[1]()
+        ez, ey = lst("EZ", A("t2", 64, 96), fc(24), 80, 48), lst("EY", A("t2", 160, 192), HX, 64, 80)
         if k == 3:
-            ts(A("FS2"), io(0, 4), 10.0, MUL, fc(29), ADD); ts(A("FS3"), io(0, 4), 10.0, MUL, fc(48), ADD)
-            cp(A("FR", 0, 16), A("t2", 128, 144)); ts(A("FR", 16, 32), A("t2", 128, 144), 4.0, ADD)
+            ez[0](); ts(A("SC"), A("t1", 256, 280), G, EQL, fc(36), MUL); cp(A("FR"), A("t2", 128, 144)); ez[1]()
+        if k == 4:
+            ey[0](); ts(A("FS1"), io(0, 2), 4.0, MUL, fc(26), ADD); ts(A("FS3"), io(0, 4), 10.0, MUL, fc(48), ADD); ey[1]()
+        if k == 5:
+            ts(A("mD"), A("mD"), X, EQL); ts(A("FS2"), io(0, 4), 10.0, MUL, fc(29), ADD)
+        if k == 6:
+            cp(A("PJ"), A("PJb"))
 
     def SCO(ph, h, c0, c1, cs=1):
         return P(5 + h, c0, c1, cs) if ph == 0 else P(7, 64 * h + c0, 64 * h + c1, cs)
@@ -430,39 +450,43 @@ def rank_program(g, core, T, topo):
                        i == blocks[-1] and h == 1)
             pm = lambda: tt(blk("PM", nr), IND(A("Fw"), A("Wu")), A("M", 0, 256) if k > 2 else A("PM", 0, 256), OP.max)
             if len(blocks) % 2: pm()
+            if nr >= 3: tt(A("VX", nr, 80, 5), al, A("st", 80, 96), MUL)
             open_scores(k, 0)
             scan(A("cum"), A("r15"), P(5, 256, 496), 0.0, MUL, OP.max)
             tt(A("val"), A("VX", 0, 80), A("cum", 2, 240, 3), SUB)
             scan(A("sv"), A("r5", 0, 80), A("val"), 0.0, MUL, OP.max)
+            if k == 5: ts(A("sm", 0, 80), A("val"), 4096.0, OP.is_ge)
             cp(A("vi"), A("sv", 4, 80, 5))
+            tt(A("sm", 80, 96), A("sv", 4, 80, 5), A("dP", 32, 48), ADD)
+            if k == 5: scan(A("t0", 0, 80), A("r5", 0, 80), A("sm", 0, 80), 0.0, MUL, ADD)
             ts(A("Li", 0, 16), A("vi"), 4095, AND)
+            if k == 5: ts(A("t0", 80, 96), A("t0", 4, 80, 5), 4.0, EQL, 4096.0, MUL)
             for u in range(2):
                 tt(A("XL", 128 * u, 128 * u + 128), IND(A("Li"), A("EL", 8 * u, 8 * u + 8)), A("mL", 128 * u, 128 * u + 128), MUL)
                 mm(P(4, 16 + u, 32, 2), A("XL", 128 * u, 128 * u + 128), D8)
             act(A("VX", 0, 80), A("val"), AF.Relu)
-            tt(A("Rf", 0, 16), A("sv", 4, 80, 5), A("Li", 0, 16), SUB)
             if k == 5:
-                ts(A("sm", 0, 80), A("val"), 4096.0, OP.is_ge)
-                scan(A("sv"), A("r5", 0, 80), A("sm", 0, 80), 0.0, MUL, ADD)
-                ts(A("sm", 80, 96), A("sv", 4, 80, 5), 4.0, EQL, 4096.0, MUL)
-                tt(A("Rf", 0, 16), A("Rf", 0, 16), A("sm", 80, 96), ADD)
+                tt(A("sm", 80, 96), A("sm", 80, 96), A("t0", 80, 96), ADD)
+            if k == 5: tt(A("zq", 0, 80), P(5, 256, 496, 3), A("VX", 0, 80), EQL)
+            tt(A("Rf", 0, 16), A("sm", 80, 96), A("Li", 0, 16), SUB)
             act(A("XR"), IND(A("Rf"), A("E2")))
-            tt(A("zq", 0, 80), P(5, 256, 496, 3), A("VX", 0, 80), EQL)
+            if k < 5: tt(A("zq", 0, 80), P(5, 256, 496, 3), A("VX", 0, 80), EQL)
             cp(A("Lu"), P(4, 16, 32))
-            mm(P(4, 32, 48), A("DX", 0, 128), A("D16"), True, False)
-            mm(P(4, 32, 48), A("XR"), A("D256"), False, True)
+            mm(P(5, 200, 216), A("XR"), A("D256"))
             act(A("cG"), IND(A("Nw"), A("Lu")))
             if len(blocks) % 2 == 0: pm()
-            ts(A("Mu"), P(4, 32, 48), -4096.0, ADD)
+            cp(A("Mu"), P(5, 200, 216))
+            tt(A("zq", 0, 80), A("zq", 0, 80), A("ZD"), MUL)
             open_scores(k, 1)
-            if k == 5: tt(A("zq", 0, 80), A("zq", 0, 80), A("ZD"), MUL)
             act(A("M", 0, 256), IND(A("PM", 0, 256 * k if k < 5 else 1536), A("Mu")))
+            sel(A("M", 256, 512), [[0, 256]], OP.is_ge, 0, 0, A("M", 0, 256))
+            if k == 2: rest()
         else:
             cp(A("cG"), IND(A("Nw"), A("Lu")))
             open_scores(k, 0); open_scores(k, 1)
             late(0)
         tr(A("cT"), A("cG"))
-        cp(A("cu"), IND(A("cT"), A("PC")))
+        cp(A("cu", 0, 64), IND(A("cT"), A("PC", 0, 4))); cp(A("cu", 64, 256), IND(A("cT"), A("PC", 4, 16)))
         if k > 1:
             if k == 5:
                 cp(A("s3"), IND(A("zq"), A("FS3")))
@@ -496,105 +520,110 @@ def rank_program(g, core, T, topo):
         for p in range(16):
             ph = int(p >= PH[1][0]); f, n = PH[ph]
             if k == 1:
-                o = blk("Vd", p); src = IND(A("Wl"), A("cu", 16 * p, 16 * p + 16))
-                if p % 2 == 0: act(o, src)
-                else: cp(o, src)
+                w = 1 if p < 4 or p >= 12 else (2, 0, 2, 0)[p % 4]
+                if w: (act if (p if w == 1 else p // 2) % 2 == 0 else cp)(A("CD", 256 * p, 256 * (p + w)),
+                                                                          IND(A("Wl"), A("cu", 16 * p, 16 * (p + w))))
                 for h in range(2):
-                    mm(SCO(ph, h, p - f, 16 * n, n), A("Vd", 256 * p + 128 * h, 256 * p + 128 * h + 128),
-                       A("SV", 40, 56), False, p == f + n - 1 and (ph == 0 or h == 1))
+                    mm(SCO(ph, h, p - f, 16 * n, n), A("CD", 256 * p + 128 * h, 256 * p + 128 * h + 128),
+                       A("SF", 24, 40), False, p == f + n - 1 and (ph == 0 or h == 1))
                 continue
             w = 1 if p < 2 else 2 - 2 * (p % 2)
-            if p == 0: act(A("M", 256, 512), A("M", 0, 256))
             if p % 2 == 0 and p < 14:
                 act(A("Vd", 256 * p, 256 * p + 512), IND(A("Wl"), A("cu", 16 * p, 16 * p + 32)))
-            if p == 14: short(0, 0); act(blk("Vd", p), IND(A("Wl"), A("cu", 16 * p, 16 * p + 16))); short(0, 1); bar(0, 0)
+            if p == 14: short(0, 0); act(blk("Vd", p), IND(A("Wl"), A("cu", 16 * p, 16 * p + 16))); bar(0, 0)
             if w:
                 tt(A("Fd", 256 * p, 256 * (p + w)), IND(A("Fw", 0, 4096), A("cu", 16 * p, 16 * (p + w))), A("M", 0, 256 * w), OP.max)
-            if p == 15: cp(blk("Vd", p), IND(A("Wl"), A("cu", 16 * p, 16 * p + 16)))
+            if p == 15:
+                cp(A("Vd", 3840, 3968), IND(A("Wl"), A("cu", 240, 248))); act(A("Vd", 3968, 4096), IND(A("Wl"), A("cu", 248, 256)))
+                short(0, 1)
             for h in range(2):
                 c0 = 256 * p + 128 * h
                 mm(SCO(ph, h, p - f, 16 * n, n), A("Fd", c0, c0 + 128), A("SF", 0, 16), False, False)
-                mm(P(2 * ph + h, p - f, 24 * n, n), A("Fd", c0, c0 + 128), A("SF"), False, False)
+                mm(P(2 * ph + h, p - f, 24 * n, n), A("Fd", c0, c0 + 128), A("SF", 0, 24), False, False)
                 mm(P(2 * ph + h, p - f, 40 * n, n), A("Vd", c0, c0 + 128), A("SV", 0, 40), False, p == f + n - 1)
-            if p == 0 and k == 5: cp(A("l3", 16 * q, 16 * q + 16), A("s3", 16 * q, 16 * q + 16))
+            if p == 14 and k == 5: act(A("l3", 16 * q, 16 * q + 16), A("s3", 16 * q, 16 * q + 16))
         if k > 1:
             short(1, 0); short(1, 1); bar(0, 1); bar(1, 0); bar(1, 1)
         best(0, 0)
         if 1 < k < 5:
-            tt(A("zq", 0, 80), A("zq", 0, 80), A("ZD"), MUL)
             tt(A("XZ", 0, 128 * nr), IND(A("zq"), A("EZ", 0, 8 * nr)), A("DX", 0, 128 * nr), ADD)
         if k == 5:
             tt(A("XZ"), IND(A("l3"), A("EY")), A("DX"), ADD, [("a3", gotall)])
         best(0, 1)
-        if k == 1: late(1); late(2)
-        if k == 2: late(3)
+        if k == 1: late(1)
         best(1, 0)
         tt(A("bi"), A("sc", 11, 384, 12), A("sc", 387, 512, 4), OP.max)
         zlist()
         mm(P(5, 0, 256), A("DW"), A("onb", 0, 256), True, False)
+        if 1 < k < 4: cp(A("Zu", 0, 16 * nr), P(0, 0, 16 * nr))
         ts(A("I1", 0, 32), A("bi"), 63, AND)
+        ts(A("gi", 0, 32), A("bi"), 0xFFFC00, AND)
+        if k >= 4: cp(A("Zu", 0, 16 * nr), P(0, 0, 16 * nr))
         if k > 1:
-            cp(A("Zu", 0, 16 * nr), P(0, 0, 16 * nr))
             if k < 5: act(A("DD"), A("val"), AF.Relu, bias=2.0 ** 17, scale=-(2.0 ** 17))
-            for rho in range(min(nr, 2)):
-                clear(rho)
-        else:
-            ts(A("gi", 0, 32), A("bi"), 0xFFFC00, AND)
+            clear(0)
         cp(A("X1"), IND(A("I1"), A("E1")))
         for S in range(2):
             mm(P(4, 0, 16), A("X1", 128 * S, 128 * S + 128), A("D16b", 16 * S, 16 * S + 16), S == 0, S == 1)
-        if k > 1: ts(A("gi", 0, 32), A("bi"), 0xFFFC00, AND)
-        ts(A("Kt", 15, 512, 16), A("bi"), 1023.5, GT)
         cp(A("Kt", 12, 512, 16), A("gi", 0, 32))
+        ts(A("Kt", 15, 512, 16), A("bi"), 1023.5, GT)
+        if k < 5: tt(A("Kk", 0, 512, 16), A("gi", 0, 32), A("idc"), ADD)
+        else: cp(A("gi", 32, 112), A("VX", 0, 80))
+        tt(A("Kt", 13, 512, 16), A("gi", 0, 32), A("Kt", 12, 512, 16), SUB)
         cl = A("CL", 48 * nr, 48 * nr + 16)
         cp(cl, P(4, 0, 16))
-        tt(A("Kt", 13, 512, 16), A("gi", 0, 32), A("Kt", 12, 512, 16), SUB)
         for h in range(2):
             mm(P(5, 0, 256), A("Kt", 256 * h, 256 * h + 128), A("PJb", 256 * h, 256 * h + 256), False, h == 1)
-        cp(A("La"), IND(A("Bw"), cl))
+        if k == 5:
+            ts(A("gi", 32, 112), A("gi", 32, 112), 4095, AND); act(A("t1", 0, 80), A("sm", 0, 80), scale=8192.0)
+        if k < 5:
+            cp(A("ctf"), P(4, 0, 16))
+            for t in range(2):
+                mm(P(4, 16 + 16 * t, 32 + 16 * t), A("Sh", 128 * t, 128 * t + 128), A("ctf"))
+        cp(A("La", 0, 128), IND(A("Bw"), A("CL", 48 * nr, 48 * nr + 8)))
+        act(A("La", 128, 256), IND(A("Bw"), A("CL", 48 * nr + 8, 48 * nr + 16)))
         tt(A("R"), P(5, 0, 256), A("La"), ADD)
         for h in range(2):
             mm(P(7, 128 + h, 192, 2), A("R", 128 * h, 128 * h + 128), A("SS", 32 * h, 32 * h + 32))
-        if nr < 2: act(A("Lo"), A("La"), scale=ODD)
+        if nr == 3: clear(1)
+        ts(A("Lo"), A("La"), ODD, MUL)
+        if k < 5: cp(A("CL", 48 * nr + 16, 48 * nr + 48), P(4, 16, 48)); late(k + 2)
         act(A("st", 16, 64), P(7, 144, 192))
-        if k < 5:
-            tt(A("Kk", 0, 512, 16), A("gi", 0, 32), A("idc"), ADD)
-            cp(A("ctf"), P(4, 0, 16))
+        al = A("al", 0, 16) if k < 5 else A("ow", 16, 32)
+        if k == 5: tt(A("t2", 0, 80), A("gi", 32, 112), A("sm", 0, 80), ADD)
         n = 0
         for gg in (0, 2, 4, 6, 1, 3, 5, 7):
             p0 = 16 * (gg - gg % 2); p1 = 16 * gg + 16
-            for h in range(2):
+            for h in ((0, 1) if n < 2 else (1, 0)):
                 b = (0, 1, 2)[n % 3] if h == 0 else (3, 6, 5)[n % 3]
                 mm(P(b, 0, 256), A("Lo" if gg % 2 else "La", 128 * h, 128 * h + 128, 1, p0, p1), A("R", 0, 256, 1, p0, p1))
                 col = A("acc", 2 * gg + h, 2 * gg + h + 1)
                 if h == 0: red(col, P(b, 0, 256), OP.max)
                 else: act(blk("CD", n), P(b, 0, 256), AF.Relu, bias=A("st", 33 + 2 * gg, 34 + 2 * gg), acc=col)
             n += 1
-            if n == 2: tt(A("st", 64, 80), P(7, 128, 144), A("dP", 16, 32), SUB)
-            if n == 2 and nr >= 2: ts(A("Lo"), A("La"), ODD, MUL)
+            if n == 1: tt(A("st", 64, 80) if k < 5 else A("o2", 16, 32), P(7, 128, 144), A("dP", 16, 32), SUB)
+            if n == 1 and k == 5: ts(A("o2", 0, 16), A("st", 16, 32), -(2.0 ** -15), MUL)
+            if n == 3 and k < 5: cp(A("XR"), IND(A("st", 64, 88), A("E2")))
+            if n == 3 and k == 5: cp(A("t4", 400, 432), IND(A("o2"), A("FS1")))
         if k < 5:
             for h in range(2):
                 mm(P(4, 256 + 128 * h, 384 + 128 * h), A("Kt", 256 * h, 256 * h + 128), A("Ib"), True, False)
                 mm(P(4, 256 + 128 * h, 384 + 128 * h), A("Kk", 256 * h, 256 * h + 128), A("I"), False, True)
-            for t in range(2):
-                mm(P(5, 16 * t, 16 + 16 * t), A("Sh", 128 * t, 128 * t + 128), A("ctf"))
-            act(A("Va"), P(4, 256, 512))
-        else:
-            act(A("o2", 16, 32), A("st", 16, 32), scale=-(2.0 ** -15))
+            mm(P(2, 0, 16), A("DX", 0, 128), A("D16"), True, False)
+            if nr >= 2: clear(nr - 1)
+            else: act(A("Va"), P(4, 256, 512))
         act(A("st", 80, 96), P(7, 128, 144), bias=2047.5 + (4096.0 * k if k < 5 else 1.0))
-        tt(A("al"), A("acc"), A("st", 48, 64), EQL)
-        tt(A("ow", 0, 16), A("al"), A("st", 64, 80), MUL)
+        tt(al, A("acc"), A("st", 48, 64), EQL)
         if k < 5:
-            tt(A("XW"), IND(A("ow"), A("E2")), A("DX", 0, 128), ADD)
-            mm(P(4, 48, 64), A("XW"), A("D16"))
+            tt(A("XW"), IND(A("al"), A("E2")), A("XR"), MUL)
+            mm(P(2, 0, 16), A("XW"), A("D16"), False, True)
+            if nr >= 2: cp(A("Va"), P(4, 256, 512))
             act(A("NK", k, 80, 5), A("st", 16, 32))
-            act(A("DD", k, 80, 5), A("al"), bias=2.0 ** 17, scale=-(2.0 ** 17))
-            for rho in range(2, nr):
-                clear(rho)
+            act(A("DD", k, 80, 5), al, bias=2.0 ** 17, scale=-(2.0 ** 17))
             act(A("ZD", k, 80, 5), A("st", 64, 80), bias=-256.0 * nr)
-            cp(A("CL", 48 * nr + 16, 48 * nr + 48), P(5, 0, 32))
-            tt(A("VX", k, 80, 5), A("al"), A("st", 80, 96), MUL)
-            cp(A("Wu"), P(4, 48, 64))
+            if nr < 2: tt(A("VX", k, 80, 5), al, A("st", 80, 96), MUL)
+            cp(A("Wu"), P(2, 0, 16))
+            if k == 1: late(7)
             mm(P(5, 256, 496), A("Ib"), A("zb"), True, False)
             for t in (1, 2):
                 mm(P(5, 256 + t, 496, 3), A("I"), A("NK"), False, False)
@@ -617,37 +646,30 @@ def rank_program(g, core, T, topo):
                 for s in order:
                     dma("s", A("Wf", 0, 4096, 1, 32 * s, 32 * s + 32, 16), ("!", T.tl[s]), "tf", [("at", gotall)])
 
-    tt(A("o2", 0, 16), A("ow", 0, 16), A("dP", 0, 16), ADD)
-    cp(A("s1"), IND(A("o2"), A("FS1")))
+    tt(A("s1"), IND(A("ow"), A("FS1")), A("t4", 400, 432), MUL)
     send(lambda r: T.s1[:, 8 * r:8 * r + 8], T.l1[:, 8 * q:8 * q + 8], "a1", [A("s1")])
-    clear(2)
-    cp(A("gi", 0, 80), A("VX", 0, 80))
-    ts(A("t1", 0, 80), A("val"), 4096.0, OP.is_ge, 8192.0, MUL)
-    ts(A("gi", 0, 80), A("gi", 0, 80), 4095, AND)
-    ts(A("t1", 5, 81, 5), A("al"), 8192.0, MUL)
-    tt(A("t2", 0, 80), A("gi", 0, 80), A("sm", 0, 80), ADD)
+    clear(1)
+    ts(A("t1", 5, 81, 5), al, 8192.0, MUL)
+    tt(A("t2", 5, 81, 5), al, A("st", 80, 96), MUL)
     scan(A("t0", 0, 80), A("r5", 0, 80), A("t1", 1, 81), 0.0, MUL, ADD)
-    tt(A("t2", 5, 81, 5), A("al"), A("st", 80, 96), MUL)
     cp(A("l1", 8 * q, 8 * q + 8), A("s1", 8 * q, 8 * q + 8))
     tt(A("t0", 0, 80), A("t0", 0, 80), A("t2", 1, 81), ADD)
     for s in range(4):
         act(A("t4", 80 * s, 80 * s + 80), A("t0", 0, 80), AF.Abs, bias=A("fc", 52 + s, 53 + s))
-    clear(3)
-    ts(A("t3", 0, 320), A("r5"), -8192.0, MUL, 8192.0, ADD)
+    clear(2); clear(3)
+    mm(P(4, 0, 16), A("onb", 0, 128, 1, 0, 1), A("tb", 0, 16, 1, 0, 1), True, False)
     scan(A("t5", 0, 320), A("t3", 0, 320), A("t4", 0, 320), 0.0, ADD, OP.min)
     ts(A("s2"), IND(A("t5", 0, 320), A("FS2")), 4096.0, OP.min, -2048.0, ADD)
     send(lambda r: T.s2[:, 16 * r:16 * r + 16], T.l2[:, 16 * q:16 * q + 16], "a2", [A("s2")])
-    ts(A("mD"), A("mD"), X, EQL)
     cp(A("l2", 16 * q, 16 * q + 16), A("s2", 16 * q, 16 * q + 16))
-    tt(A("XL"), IND(A("l1"), A("FR", 0, 16)), A("mD"), MUL, [("a1", gotall)])
-    act(A("cG"), IND(A("l1"), A("FR", 16, 32)), w=[("a1", gotall)])
     for h in range(2):
-        mm(P(5, 128 * h, 128 * h + 128), A("cG", 128 * h, 128 * h + 128), A("I"))
+        cp(A("Kk", 256 * h, 256 * h + 128, 8), A("l1", h, 32, 2), [("a1", gotall)])
+        mm(P(5, 128 * h, 128 * h + 128), A("Kk", 256 * h, 256 * h + 128), A("I"))
     for h in range(2):
-        mm(P(4, 8 * h, 8 * h + 8), A("XL", 128 * h, 128 * h + 128), BD)
-    cp(A("PJ"), A("PJb"))
+        tt(A("XL", 128 * h, 128 * h + 128), IND(A("l1"), A("FR", 8 * h, 8 * h + 8)), A("mD", 0, 128), MUL)
+        mm(P(4, 8 * h, 8 * h + 8), A("XL", 128 * h, 128 * h + 128), BD, False, h == 1)
     act(A("Va"), P(5, 0, 256))
-    cp(A("Wu"), P(4, 0, 16))
+    ts(A("Wu"), P(4, 0, 16), fc(23), ADD)
     cp(IND(A("Wf"), A("Wu")), A("Va"))
     dma("s", ("!", T.yt[:, :]), A("Wf", 0, 4096, 1, 0, 128, 16), "yt")
     for h in range(2):

@@ -4,18 +4,18 @@ from concourse.mybir import AluOpType as OP, AxisListType as AX, ActivationFunct
 F32, BF, I32, U16, F16 = "float32", "bfloat16", "int32", "uint16", "float16"
 SB = {
     "Fw": (4352, BF), "Nw": (4096, F32), "Wo": (5120, F32), "Wl": (4096, F32), "Bw": (4096, BF), "Wf": (5120, F32),
-    "Fd": (4096, BF), "Vd": (4096, F32), "CD": (4096, BF), "PM": (1536, BF), "M": (512, BF),
+    "Fd": (4096, BF), "Vd": (4096, F16), "CD": (3072, BF), "PM": (1536, BF), "M": (512, BF),
     "sh": (16, I32), "lh": (64, I32), "sn": (1024, I32), "sf": (1024, BF), "sx": (1152, F16), "lx": (1152, F16), "lf": (1024, BF),
     "hf": (64, F32), "hx": (512, F16),
     "ic": (8, I32), "fc": (56, F32), "iof": (16, F32), "D16": (16, F32), "D16b": (32, BF), "BD": (16, F32),
     "I": (128, F32), "t0": (512, F32), "t1": (512, F32), "t2": (512, F32), "t3": (512, F32), "t4": (512, F32),
     "t5": (512, F32), "tb": (128, BF), "pw": (24, F32), "sg": (16, F32), "inc": (16, F32), "EU": (336, U16),
-    "mL": (256, F32), "DX": (512, F32), "dP": (48, F32), "on": (256, F32), "onb": (320, BF),
-    "r15": (240, F32), "r5": (80, F32), "r12": (192, F32), "r4": (128, F32), "PJ": (512, F16), "PJb": (512, BF), "Kt": (512, BF),
-    "Kk": (512, F32), "idc": (32, F32), "CI": (256, BF), "CW": (1152, BF), "SF": (40, BF), "SM": (384, BF), "SV": (40, F32),
+    "mL": (256, F32), "DX": (512, F32), "dP": (80, F32), "on": (256, F32), "onb": (320, BF),
+    "r5": (80, F32), "r12": (192, F32), "r4": (128, F32), "PJ": (512, F16), "PJb": (512, BF), "Kt": (512, BF),
+    "Kk": (512, F32), "idc": (32, F32), "CI": (256, BF), "CW": (1152, BF), "SF": (40, BF), "SM": (384, BF), "SV": (40, BF),
     "SU": (8, BF), "SC": (24, BF), "Sh": (256, F32), "SS": (64, BF), "SQ": (512, F16), "mH": (128, F32), "RH": (4, F16),
-    "mD": (128, F32), "Ib": (128, BF), "D256": (16, F32), "zr": (256, F32), "zb": (240, BF), "NI": (128, BF), "DW": (128, BF),
-    "VX": (88, F32), "NK": (80, F32), "DD": (80, BF), "cum": (240, F32), "val": (80, F32), "sv": (80, F32), "vi": (16, I32),
+    "mD": (128, F32), "Ib": (128, BF), "D256": (16, F32), "zr": (256, F32), "NI": (128, BF), "DW": (128, BF),
+    "VX": (240, F32), "NK": (80, F32), "DD": (80, BF), "cum": (240, F32), "val": (80, F32), "sv": (240, I32), "vi": (32, I32),
     "Li": (24, I32), "Rf": (24, F32), "XL": (256, F32), "XR": (128, F32), "cG": (256, F32),
     "cT": (256, F32), "cu": (256, U16), "zq": (88, F32), "ZD": (80, F32), "XZ": (512, F32),
     "pen": (1280, BF), "sc": (512, F32), "bi": (32, I32), "I1": (40, I32), "gi": (112, I32), "X1": (256, BF),
@@ -206,41 +206,40 @@ def rank_program(g, core, T, topo):
     ts(A("D16"), io(0, 16), X, EQL)
     ts(BD, io(0, 8), G, EQL)
     act(A("Wo", 0, 256), A("zr"), AF.Silu)
-    zero(A("Wo", 256, 1024))
     act(A("inc", 0, 6), A("pw", 7, 13), scale=d16(7)); act(A("inc", 6, 12), A("pw", 7, 13), scale=d16(6))
     act(A("Wl", 0, 1), A("zr", 0, 1))
     act(A("sg"), A("D16"), scale=-2.0, bias=1.0)
-    small = [(fc(41), P4, -4.0, PF), (RK, P64, -4.0, G), (fc(43), P64, 4.0, fc(41)), (ODD, P32, -2.0, G), (X1, P2, -2.0, PF),
-             (X13, P8, -4.0, P2), (X6, P2, 16.0, X1), (XG, X, 16.0, G)]
+    ts(fc(41), P4, -4.0, MUL, PF, ADD)
+    ts(fc(30), X, 14.5, OP.is_lt)
+    ts(fc(32), X, 11.5, OP.is_lt)
+    ts(D8, io(0, 8), X8, EQL); tt(EQ, X8, G, EQL)
+    ts(fc(43), P64, 4.0, MUL, fc(41), ADD)
+    ts(A("Bw", 0, 1), fc(32), 2047.0, MUL, fc(30), ADD)
+    tt(fc(37), fc(32), fc(30), SUB)
+    ts(A("EH"), A("t3", 16, 48), X, ADD)
+    ts(A("SU"), io(0, 8), fc(43), EQL)
+    for qt in range(4):
+        ts(A("SQ", 128 * qt, 128 * qt + 128), A("tb"), float(qt), ADD, PF, EQL)
+    ts(A("mH"), A("mH"), X8, EQL)
+    small = [(RK, P64, -4.0, G), (ODD, P32, -2.0, G), (X1, P2, -2.0, PF), (X13, P8, -4.0, P2), (X6, P2, 16.0, X1), (XG, X, 16.0, G),
+             (A("dP", 64, 80), io(0, 16), 2.0 ** 19, 2048.0)]
     for k in range(12):
         n = min(1 << k, 1024)
         act(A("Wl", 1 << k, (1 << k) + n), A("Wl", 0, n), bias=A("inc", k, k + 1))
+        if k < 8: act(A("Bw", 1 << k, 2 << k), A("Bw", 0, 1 << k), scale=A("sg", k, k + 1))
         if k < len(small):
             o, i, s, b = small[k]; act(o, i, scale=s, bias=b)
-    ts(fc(30), X, 14.5, OP.is_lt)
-    ts(fc(32), X, 11.5, OP.is_lt)
-    for qt in range(4):
-        ts(A("SQ", 128 * qt, 128 * qt + 128), A("tb"), float(qt), ADD, PF, EQL)
-    ts(A("Bw", 0, 1), fc(32), 2047.0, MUL, fc(30), ADD)
-    tt(fc(37), fc(32), fc(30), SUB)
-    ts(D8, io(0, 8), X8, EQL); tt(EQ, X8, G, EQL)
-    ts(A("EH"), A("t3", 16, 48), X, ADD); ts(A("mH"), A("mH"), X8, EQL)
 
     def lst(name, src, col, zcol, c):
         n = LISTS[name][1]
         return [lambda: ts(A("t5", c, c + n), src, col, ADD, EQ, MUL), lambda: ts(A(name), A("t5", c, c + n), float(zcol), ADD)]
     el, e1, e2 = lst("EL", A("t3", 0, 16), HX, 16, 0), lst("E1", io(0, 16), fc(21), 32, 16), lst("E2", A("t1", 48, 56), HX, 16, 32)
     fill = [lambda: ts(fc(19), X8, 32.0, MUL), lambda: ts(fc(20), HX, 16.0, MUL), el[0],
-            lambda: ts(A("PC"), io(0, 16), fc(19), ADD, fc(20), ADD), el[1],
-            lambda: ts(fc(34), d16(14), -0.75, MUL, fc(37), SUB), lambda: ts(fc(21), fc(20), -32.0, ADD),
-            lambda: ts(A("t1", 48, 56), io(0, 8), 2.0, MUL, -16.0, ADD), e1[0], e2[0]]
-
-    def bits(k0, k1):
-        for k in range(k0, k1):
-            ts(A("Bw", 1 << k, 2 << k), A("Bw", 0, 1 << k), A("sg", k, k + 1), MUL)
-            if k < len(fill): fill[k]()
+            lambda: ts(A("t1", 48, 56), io(0, 8), 2.0, MUL, -16.0, ADD), lambda: ts(fc(34), d16(14), -0.75, MUL, fc(37), SUB),
+            lambda: ts(A("PC"), io(0, 16), fc(19), ADD, fc(20), ADD), lambda: ts(fc(21), fc(20), -32.0, ADD), el[1], e2[0],
+            lambda: ts(A("RH"), io(0, 4), float(4 * q), ADD, P8, EQL), lambda: tt(A("t1", 32, 48), A("pw", 7, 23), A("D16"), MUL),
+            e1[0], e2[1], lambda: cp(A("lh", 16 * q, 16 * q + 16), A("sh")), lambda: red(fc(38), A("t1", 32, 48), ADD), e1[1]]
     sel(A("Ib"), [[1, 128]], EQL, 0, -1)
-    ts(A("SU"), io(0, 8), fc(43), EQL)
 
     def pieces(ss, b):
         for i, r in enumerate(ss):
@@ -257,7 +256,7 @@ def rank_program(g, core, T, topo):
         yield
     step = pieces(order, 4); next(step)
     for i, r in enumerate(order):
-        bits(3 * i, 3 * i + 3 if i < 2 else 7)
+        for f in fill[(0, 8, 16)[i]:(8, 16, 16)[i]]: f()
         if i == 1: next(step)
         ts(A("sx", 288 * r, 288 * r + 256), blk("sn", r), -2048.0, ADD)
         if i == 1: next(step)
@@ -265,18 +264,21 @@ def rank_program(g, core, T, topo):
          [A("sx", 288 * r, 288 * r + 288) for r in order])
     send(lambda r: T.sf[:, 256 * r:256 * r + 256], T.lf[:, 256 * q:256 * q + 256], "af%d" % q, [blk("sf", r) for r in order])
     step = pieces([q], 5); next(step); next(step)
-    bits(7, 8); next(step)
     ts(A("sx", 288 * q, 288 * q + 256), blk("sn", q), -2048.0, ADD)
-    bits(8, 10)
+    next(step)
+    ts(A("Bw", 256, 512), A("Bw", 0, 256), A("sg", 8, 9), MUL)
+    ts(A("mL"), A("mL"), HX, EQL)
+    ts(A("Bw", 512, 1024), A("Bw", 0, 512), A("sg", 9, 10), MUL)
 
     def spare(rho):
         dx = A("DX", 128 * rho, 128 * rho + 128)
         iota(dx, [[0, 8], [8, 2], [-255, 8]], 4096 + 256 * rho, 16)
         own(dx, [[0, 16], [1, 8]])
     sel(A("SF", 24, 40), [[1, 2], [16, 8]], EQL, 6, -1)
-    for row in (5, 8):
+    for row in (5, 13):
         sel(A("SF", 24, 40), [[0, 2], [16, 8]], NE, row, -1, A("SF", 24, 40), 1024.0)
     iota(A("CW", 640, 832, 1, 0, 1), [[0, 16], [-64, 12]], 960); iota(A("CW", 832, 960, 1, 0, 1), [[0, 32], [-64, 4]], 192)
+    zero(A("Wo", 256, 1024))
     iota(A("t2", 64, 96), [[1, 4], [10, 8]], 1 - 80)
     iota(A("t2", 128, 144), [[1, 2], [8, 4], [4, 2]], 2)
     iota(A("t2", 160, 192), [[2, 4], [8, 8]], -64)
@@ -297,33 +299,24 @@ def rank_program(g, core, T, topo):
     sel(A("I"), [[1, 128]], EQL, 0, -1)
     zero(A("al", 16, 24)); zero(A("st", 80, 88))
     spare(0)
-    for m in range(2):
-        sel(A("Sh", 64 * m, 64 * m + 48), [[1, 48]], EQL, 64 * m + 16, -1)
-        sel(A("Sh", 64 * m + 48, 64 * m + 64), [[1, 16]], EQL, 64 * m, -1)
-        sel(A("Sh", 128 + 64 * m, 144 + 64 * m), [[1, 16]], EQL, 64 * m + 48, -1)
-        sel(A("Sh", 144 + 64 * m, 192 + 64 * m), [[1, 48]], EQL, 64 * m, -1)
-    zero(A("ZD")); zero(A("zb"))
-    zero(A("Fw", 4096, 4352)); zero(A("PM", 0, 256))
-    sel(A("r15"), [[0, 16], [1, 15]], GT, 0, 0)
-    sel(A("r5"), [[0, 16], [1, 5]], GT, 0, 0)
+    for ph, (f, n) in enumerate(PH):
+        iota(A("SM", 288 * ph, 288 * ph + 24 * n), [[0, 3], [1, 8], [0, n]])
+    zero(A("ZD")); zero(A("PM", 0, 256))
     iota(A("CI", 0, 256, 1, 0, 1), [[-1, 256]], 255)
     for ph, (f, n) in enumerate(PH):
         iota(A("CW", 480 * ph, 480 * ph + 24 * n, 1, 0, 1), [[0, 6], [-256, 4], [0, n]], 768)
-        iota(A("CW", 480 * ph + 24 * n, 480 * ph + 40 * n, 1, 0, 1), [[0, 16 * n]], 1)
     zero(A("zq")); zero(A("Rf"))
-    for ph, (f, n) in enumerate(PH):
-        sm = A("SM", 288 * ph, 288 * ph + 24 * n)
-        iota(sm, [[0, 24 * n]], -1024); own(sm, [[0, 3], [1, 8], [0, n]])
     iota(A("SF", 0, 24), [[0, 24]], 1024); own(A("SF", 0, 24), [[0, 3], [1, 8]])
-    zero(A("SV", 0, 40))
-    sel(A("SV", 0, 24), [[2, 3], [16, 8]], NE, 0, -1, A("SV", 0, 24), -1.0)
-    for m in range(2):
-        sel(A("SV", 9 + 4 * m, 12 + 4 * m), [[16, 3]], NE, 64 * m + 17, -1, A("SV", 9 + 4 * m, 12 + 4 * m), -1.0)
-        sel(A("SV", 16 + 4 * m, 19 + 4 * m), [[16, 3]], NE, 64 * m + 3, -1, A("SV", 16 + 4 * m, 19 + 4 * m), -1.0)
-    sel(A("SV", 24, 40), [[1, 2], [16, 8]], NE, 6, -1, A("SV", 24, 40), -1.0)
+    zero(A("SV", 0, 24))
+    for row, wt in ((0, -2048.0), (8, -1.0)):
+        sel(A("SV", 0, 24), [[2, 3], [16, 8]], NE, row, -1, A("SV", 0, 24), wt)
+        for m in range(2):
+            sel(A("SV", 9 + 4 * m, 12 + 4 * m), [[16, 3]], NE, 64 * m + 17 + row, -1, A("SV", 9 + 4 * m, 12 + 4 * m), wt)
+            sel(A("SV", 16 + 4 * m, 19 + 4 * m), [[16, 3]], NE, 64 * m + 3 + row, -1, A("SV", 16 + 4 * m, 19 + 4 * m), wt)
+    sel(A("SV", 24, 40), [[1, 2], [16, 8]], EQL, 6, -1)
 
     def rest():
-        iota(A("mD"), [[0, 8], [1, 16]])
+        iota(A("mD"), [[0, 8], [1, 16]]); sel(A("r5"), [[0, 16], [1, 5]], GT, 0, 0)
         for rho in range(1, 4):
             spare(rho)
         iota(A("PM", 1280, 1536), [[0, 256]], 255)
@@ -349,36 +342,29 @@ def rank_program(g, core, T, topo):
         s = ss[0]
         for r in range(4):
             mm(P(b, 0, 128, 1, 32 * r, 32 * r + 32), A("sx" if s == q else "lx", 288 * s + 256, 288 * s + 288), A("Ib"), w=wn(s))
-        (act if eng == "a" else cp)(A("Vd", 128 * s, 128 * s + 128), P(b, 0, 128))
+        (act if eng == "a" else cp)(A("t0", 128 * s, 128 * s + 128), P(b, 0, 128))
         for m in range(2):
-            for e, row in enumerate((5, 8)):
+            for e, row in enumerate((5, 13)):
                 dma("s", A("Wl", 1024 * s, 1024 * s + 1024, 1, 64 * m + row, 64 * m + 64, 16),
-                    A("Vd", 128 * s, 128 * s + 128, 1, 2 * m + e, 128, 4), "su")
-    ts(A("RH"), io(0, 4), float(4 * q), ADD, P8, EQL)
-    ts(A("mL"), A("mL"), HX, EQL)
-    cp(A("lh", 16 * q, 16 * q + 16), A("sh"))
-    e1[1](); e2[1]()
-    tt(A("t1", 32, 48), A("pw", 7, 23), A("D16"), MUL)
-    ts(A("Wl", 3072, 4096), A("Wl", 1024, 2048), A("inc", 11, 12), ADD)
-    red(fc(38), A("t1", 32, 48), ADD)
-    spread(q); sums([q], "a")
-    act(A("Bw", 1024, 2048), A("Bw", 0, 1024), scale=A("sg", 10, 11))
+                    A("t0", 128 * s, 128 * s + 128, 1, 2 * m + e, 128, 4), "su")
     ts(A("Bw", 2048, 3072), A("Bw", 0, 1024), A("sg", 11, 12), MUL)
+    ts(A("Wl", 3072, 4096), A("Wl", 1024, 2048), A("inc", 11, 12), ADD)
+    spread(q); sums([q], "a")
     ts(A("hf"), A("lh"), -2048.0, ADD, w=[("ah", gotall)])
     sums(near, "a"); spread(near[0])
     for r in range(4):
         tt(A("hx", 128 * r, 128 * r + 128), IND(A("hf"), A("EH", 8 * r, 8 * r + 8)), A("mH"), MUL)
         for m in range(2):
             mm(P(4, 8 * m + 2 * r, 8 * m + 2 * r + 2), A("hx", 128 * r, 128 * r + 128), A("RH", 2 * m, 2 * m + 2))
-    ts(A("Li", 0, 16), P(4, 0, 16), 2048.0, ADD); act(A("VX", 0, 80, 5), P(4, 0, 16), bias=2048.0)
+    ts(A("Bw", 3072, 4096), A("Bw", 2048, 3072), A("sg", 10, 11), MUL)
+    ts(A("Li", 0, 16), P(4, 0, 16), 2048.0, ADD); tt(A("VX", 0, 240, 15), P(4, 0, 16), A("dP", 64, 80), ADD)
     tt(A("XL"), IND(A("Li"), A("EL")), A("mL"), MUL)
-    act(A("Bw", 3072, 4096), A("Bw", 2048, 3072), scale=A("sg", 10, 11))
-    sums(far[:1], "v", 0); sums(far[1:], "v", 1)
-    spread(far[0], "va")
+    sums(far[:1], "a", 0); sums(far[1:], "a", 1)
+    spread(far[0], "av"); spread(far[1], "av")
     for u in range(2):
         mm(P(4, 16 + u, 32, 2), A("XL", 128 * u, 128 * u + 128), D8)
     cp(A("Lu"), P(4, 16, 32))
-    spread(far[1], "va")
+    act(A("Bw", 1024, 2048), A("Bw", 0, 1024), scale=A("sg", 10, 11))
     for s in [q] + near + far:
         dma("s", A("Fd", 1024 * s, 1024 * s + 1024, 1, 0, 32), blk("lf", s), "f1", wf(s))
     for c in range(1, 4):
@@ -395,12 +381,16 @@ def rank_program(g, core, T, topo):
                                (fc(50), fc(36), -1.0, None)]:
                 act(o, i, scale=s, bias=b)
         if k == 7:
+            act(A("Fw", 4096, 4352), A("zr"))
             for o, i, s, b in [(fc(31), P4, -24.0, X6), (fc(27), X1, 5.0, 4.0), (fc(23), X, 16.0, 4096.0), (fc(25), P8, -16.0, fc(31)),
                                (fc(28), HX, 40.0, fc(27)), (fc(26), HX, 2.0, fc(25)), (fc(47), X13, 1.0, fc(28)),
                                (fc(29), X13, 80.0, fc(28)), (fc(48), fc(47), 1.0, -3.0)]:
                 act(o, i, scale=s, bias=b)
         if k == 1:
             act(A("DW"), A("Ib"), scale=fc(37))
+            for m in range(2):
+                for o, i, n in ((0, 16, 48), (48, 0, 16), (128, 48, 16), (144, 0, 48)):
+                    act(A("Sh", 64 * m + o, 64 * m + o + n), A("I", 64 * m + i, 64 * m + i + n))
             act(A("dP", 0, 16), A("dP", 0, 16), bias=XG)
             act(A("SS", 0, 8), BD, scale=fc(39)); act(A("SS", 8, 16), BD, scale=fc(50)); act(A("SS", 16, 24), BD, scale=fc(40))
             act(A("dP", 16, 32), A("dP", 0, 16), bias=-2047.5); act(A("dP", 32, 48), A("dP", 0, 16), bias=-65536.0, scale=16.0)
@@ -411,13 +401,11 @@ def rank_program(g, core, T, topo):
             act(A("NK", 0, 80, 5), A("zr", 0, 16), bias=-BIG)
         ez, ey = lst("EZ", A("t2", 64, 96), fc(24), 80, 48), lst("EY", A("t2", 160, 192), HX, 64, 80)
         if k == 3:
-            ez[0](); ts(A("SC"), A("t1", 256, 280), G, EQL, fc(36), MUL); cp(A("FR"), A("t2", 128, 144)); ez[1]()
+            ez[0](); ts(A("SC"), A("t1", 256, 280), G, EQL, fc(36), MUL); ts(A("SM"), A("SM"), G, EQL, -1024.0, MUL); ez[1]()
         if k == 4:
             ey[0](); ts(A("FS1"), io(0, 2), 4.0, MUL, fc(26), ADD); ts(A("FS3"), io(0, 4), 10.0, MUL, fc(48), ADD); ey[1]()
         if k == 5:
             ts(A("mD"), A("mD"), X, EQL); ts(A("FS2"), io(0, 4), 10.0, MUL, fc(29), ADD)
-        if k == 6:
-            cp(A("PJ"), A("PJb"))
 
     def SCO(ph, h, c0, c1, cs=1):
         return P(5 + h, c0, c1, cs) if ph == 0 else P(7, 64 * h + c0, 64 * h + c1, cs)
@@ -431,47 +419,56 @@ def rank_program(g, core, T, topo):
         mm(P(7, 0, 128), one, A("CW", 832, 960, 1, 0, 1), True, False)
         for ph, (f, n) in enumerate(PH):
             for h in range(2 if k > 1 else 0):
-                mm(P(2 * ph + h, 0, 40 * n), one, A("CW", 480 * ph, 480 * ph + 40 * n, 1, 0, 1), True, False)
+                mm(P(2 * ph + h, 0, 24 * n), one, A("CW", 480 * ph, 480 * ph + 24 * n, 1, 0, 1), True, False)
                 mm(P(2 * ph + h, 0, 24 * n), A("CI", 128 * h, 128 * h + 128, 1, 0, 1), A("onb", 0, 24 * n, 1, 0, 1), False, False)
     WO = A("Wo", 0, 4096)
+    VX = A("VX", 2, 240, 3)
 
     for k in range(1, 6):
         nr = k - 1
         if k > 1:
             blocks = [i for i in range(3 * nr) if i != 3 * nr - 3]
-            for n, i in enumerate(blocks):
-                rho, t = i // 3 + 1, i % 3
-                o = A("CD", 256 * i, 256 * i + 256); src = IND(WO, A("CL", 16 * i, 16 * i + 16))
-                if n % 2 == 0: act(o, src)
-                else: cp(o, src)
-                for h in range(2):
-                    c0 = 256 + 15 * h + 3 * rho + t
-                    mm(P(5, c0, 496, 30), A("CD", 256 * i + 128 * h, 256 * i + 128 * h + 128), A("SC", 8 * t, 8 * t + 8), False,
-                       i == blocks[-1] and h == 1)
+            calls = {1: ((cp, 1, 1), (act, 2, 1)), 2: ((cp, 0, 2), (act, 4, 2), (act, 2, 1)),
+                     3: ((cp, 0, 3), (act, 4, 2), (act, 7, 1), (cp, 3, 1), (act, 8, 1)),
+                     4: ((cp, 0, 4), (act, 5, 4), (act, 10, 1), (cp, 4, 1), (act, 11, 1))}[nr]
+            for n, (f, i0, w) in enumerate(calls):
+                f(A("CD", 256 * i0, 256 * (i0 + w)), IND(WO, A("CL", 16 * i0, 16 * (i0 + w))))
+                for i in range(i0, i0 + w):
+                    rho, t = i // 3 + 1, i % 3
+                    for h in range(2):
+                        c0 = 256 + 15 * h + 3 * rho + t
+                        mm(P(5, c0, 496, 30), A("CD", 256 * i + 128 * h, 256 * i + 128 * h + 128), A("SC", 8 * t, 8 * t + 8), False,
+                           n == len(calls) - 1 and h == 1)
             pm = lambda: tt(blk("PM", nr), IND(A("Fw"), A("Wu")), A("M", 0, 256) if k > 2 else A("PM", 0, 256), OP.max)
             if len(blocks) % 2: pm()
-            if nr >= 3: tt(A("VX", nr, 80, 5), al, A("st", 80, 96), MUL)
+            if nr == 4: tt(A("VX", 3 * nr + 2, 240, 15), al, A("st", 80, 96), MUL)
             open_scores(k, 0)
-            scan(A("cum"), A("r15"), P(5, 256, 496), 0.0, MUL, OP.max)
-            tt(A("val"), A("VX", 0, 80), A("cum", 2, 240, 3), SUB)
-            scan(A("sv"), A("r5", 0, 80), A("val"), 0.0, MUL, OP.max)
-            if k == 5: ts(A("sm", 0, 80), A("val"), 4096.0, OP.is_ge)
-            cp(A("vi"), A("sv", 4, 80, 5))
-            tt(A("sm", 80, 96), A("sv", 4, 80, 5), A("dP", 32, 48), ADD)
+            if k == 5: act(A("sm", 0, 80), VX, AF.Sign)
+            ts(A("cum"), P(5, 256, 496), 0.0, GT, 32768.0, MUL)
             if k == 5: scan(A("t0", 0, 80), A("r5", 0, 80), A("sm", 0, 80), 0.0, MUL, ADD)
-            ts(A("Li", 0, 16), A("vi"), 4095, AND)
+            scan(A("sv"), A("cum"), A("VX"), 0.0, ADD, OP.max)
             if k == 5: ts(A("t0", 80, 96), A("t0", 4, 80, 5), 4.0, EQL, 4096.0, MUL)
+            ts(A("Li", 0, 16), A("sv", 14, 240, 15), 4095, AND)
+            ts(A("vi", 0, 16), A("sv", 14, 240, 15), 0x7000, AND)
+            if k == 5: ts(A("vi", 16, 32), A("sv", 14, 240, 15), 0x78000, AND)
+            else: tt(A("val"), A("sv", 2, 240, 3), VX, EQL)
             for u in range(2):
                 tt(A("XL", 128 * u, 128 * u + 128), IND(A("Li"), A("EL", 8 * u, 8 * u + 8)), A("mL", 128 * u, 128 * u + 128), MUL)
                 mm(P(4, 16 + u, 32, 2), A("XL", 128 * u, 128 * u + 128), D8)
-            act(A("VX", 0, 80), A("val"), AF.Relu)
+                if k == 5 and u == 0:
+                    ts(A("sm", 80, 96), A("vi", 16, 32), 0.0, EQL)
             if k == 5:
-                tt(A("sm", 80, 96), A("sm", 80, 96), A("t0", 80, 96), ADD)
-            if k == 5: tt(A("zq", 0, 80), P(5, 256, 496, 3), A("VX", 0, 80), EQL)
-            tt(A("Rf", 0, 16), A("sm", 80, 96), A("Li", 0, 16), SUB)
+                tt(A("sm", 80, 96), A("sm", 80, 96), A("t0", 80, 96), MUL)
+                tt(A("t0", 96, 112), A("vi", 0, 16), A("dP", 32, 48), ADD)
+                tt(A("val"), A("sv", 2, 240, 3), VX, EQL)
+                tt(A("Rf", 0, 16), A("sm", 80, 96), A("t0", 96, 112), ADD)
+            else:
+                tt(A("Rf", 0, 16), A("vi", 0, 16), A("dP", 32, 48), ADD)
+            tt(VX, VX, A("val"), MUL)
             act(A("XR"), IND(A("Rf"), A("E2")))
-            if k < 5: tt(A("zq", 0, 80), P(5, 256, 496, 3), A("VX", 0, 80), EQL)
+            if k == 5: act(A("sm", 0, 80), VX, AF.Sign)
             cp(A("Lu"), P(4, 16, 32))
+            tt(A("zq", 0, 80), P(5, 256, 496, 3), VX, EQL)
             mm(P(5, 200, 216), A("XR"), A("D256"))
             act(A("cG"), IND(A("Nw"), A("Lu")))
             if len(blocks) % 2 == 0: pm()
@@ -489,7 +486,7 @@ def rank_program(g, core, T, topo):
         cp(A("cu", 0, 64), IND(A("cT"), A("PC", 0, 4))); cp(A("cu", 64, 256), IND(A("cT"), A("PC", 4, 16)))
         if k > 1:
             if k == 5:
-                cp(A("s3"), IND(A("zq"), A("FS3")))
+                act(A("s3"), IND(A("zq"), A("FS3")))
                 send(lambda r: T.s3[:, 16 * r:16 * r + 16], T.l3[:, 16 * q:16 * q + 16], "a3", [A("s3")])
             for b in range(4):
                 ph, h = b // 2, b % 2; n = PH[ph][1]; mh = A("M", 128 * h, 128 * h + 128)
@@ -498,11 +495,10 @@ def rank_program(g, core, T, topo):
 
         def short(ph, h):
             n = PH[ph][1]; c = 960 * ph + 40 * n * h
-            act(A("pen", c, c + 40 * n), P(2 * ph + h, 0, 40 * n), AF.Relu, bias=1.0, scale=-1.0)
+            act(A("pen", c, c + 24 * n), P(2 * ph + h, 0, 24 * n), AF.Relu, bias=1.0, scale=-1.0)
 
         def bar(ph, h):
             n = PH[ph][1]; c = 960 * ph + 40 * n * h
-            mm(SCO(ph, h, 0, 16 * n), A("Ib"), A("pen", c + 24 * n, c + 40 * n), False, False)
             for o0, o1, t in ((0, 16, 0), (0, 16, 1), (0, 8, 2), (8, 16, 0)):
                 mm(SCO(ph, h, o0 * n, o1 * n), A("NI"), A("pen", c + 8 * n * t, c + n * (8 * t + o1 - o0)), False,
                    o0 == 8 and (ph == 0 or h == 1))
@@ -511,20 +507,25 @@ def rank_program(g, core, T, topo):
             if ph == 0: scan(A("sc", 192 * h, 192 * h + 192), A("r12"), SCO(0, h, 0, 192), 0.0, MUL, OP.max)
             else: scan(A("sc", 384, 512), A("r4"), P(7, 0, 128), 0.0, MUL, OP.max)
 
-        def zlist():
-            for rho in range(nr):
-                mm(P(0, 16 * rho, 16 + 16 * rho), A("XZ", 128 * rho, 128 * rho + 128), A("D16"))
+        def places(r0, r1, f=tt):
+            src = IND(A("zq"), A("EZ", 8 * r0, 8 * r1)) if k < 5 else IND(A("l3"), A("EY", 8 * r0, 8 * r1))
+            tt(A("XZ", 128 * r0, 128 * r1), src, A("DX", 128 * r0, 128 * r1), ADD, [("a3", gotall)] if k == 5 else ())
 
-        def clear(rho):
-            act(IND(A("Wo" if k < 5 else "Wf"), A("Zu", 16 * rho, 16 * rho + 16)), A("zr"), AF.Silu)
+        def zlist(r0, r1):
+            for rho in range(r0, r1):
+                mm(P((0, 1, 4, 4)[rho], 32 + 16 * rho, 48 + 16 * rho), A("XZ", 128 * rho, 128 * rho + 128), A("D16"))
+
+        def clear(h0, h1):
+            for c0, c1 in [(8 * h0, 8 * h1)] if h0 % 2 == 0 and h1 == h0 + 2 else [(8 * x, 8 * x + 8) for x in range(h0, h1)]:
+                act(IND(A("Wo" if k < 5 else "Wf"), A("Zu", c0, c1)), A("zr", 0, 16 * (c1 - c0)), AF.Silu)
         for p in range(16):
             ph = int(p >= PH[1][0]); f, n = PH[ph]
             if k == 1:
                 w = 1 if p < 4 or p >= 12 else (2, 0, 2, 0)[p % 4]
-                if w: (act if (p if w == 1 else p // 2) % 2 == 0 else cp)(A("CD", 256 * p, 256 * (p + w)),
+                if w: (act if (p if w == 1 else p // 2) % 2 == 0 else cp)(A("Vd", 256 * p, 256 * (p + w)),
                                                                           IND(A("Wl"), A("cu", 16 * p, 16 * (p + w))))
                 for h in range(2):
-                    mm(SCO(ph, h, p - f, 16 * n, n), A("CD", 256 * p + 128 * h, 256 * p + 128 * h + 128),
+                    mm(SCO(ph, h, p - f, 16 * n, n), A("Vd", 256 * p + 128 * h, 256 * p + 128 * h + 128),
                        A("SF", 24, 40), False, p == f + n - 1 and (ph == 0 or h == 1))
                 continue
             w = 1 if p < 2 else 2 - 2 * (p % 2)
@@ -534,41 +535,38 @@ def rank_program(g, core, T, topo):
             if w:
                 tt(A("Fd", 256 * p, 256 * (p + w)), IND(A("Fw", 0, 4096), A("cu", 16 * p, 16 * (p + w))), A("M", 0, 256 * w), OP.max)
             if p == 15:
-                cp(A("Vd", 3840, 3968), IND(A("Wl"), A("cu", 240, 248))); act(A("Vd", 3968, 4096), IND(A("Wl"), A("cu", 248, 256)))
+                cp(A("Vd", 3840, 3904), IND(A("Wl"), A("cu", 240, 244))); act(A("Vd", 3904, 4096), IND(A("Wl"), A("cu", 244, 256)))
                 short(0, 1)
             for h in range(2):
                 c0 = 256 * p + 128 * h
                 mm(SCO(ph, h, p - f, 16 * n, n), A("Fd", c0, c0 + 128), A("SF", 0, 16), False, False)
                 mm(P(2 * ph + h, p - f, 24 * n, n), A("Fd", c0, c0 + 128), A("SF", 0, 24), False, False)
-                mm(P(2 * ph + h, p - f, 40 * n, n), A("Vd", c0, c0 + 128), A("SV", 0, 40), False, p == f + n - 1)
+                mm(P(2 * ph + h, p - f, 24 * n, n), A("Vd", c0, c0 + 128), A("SV", 0, 24), False, p == f + n - 1)
+                mm(SCO(ph, h, p - f, 16 * n, n), A("Vd", c0, c0 + 128), A("SV", 24, 40), False, False)
             if p == 14 and k == 5: act(A("l3", 16 * q, 16 * q + 16), A("s3", 16 * q, 16 * q + 16))
         if k > 1:
-            short(1, 0); short(1, 1); bar(0, 1); bar(1, 0); bar(1, 1)
+            places(0, 1)
+            short(1, 0); short(1, 1); zlist(0, 1); bar(0, 1); bar(1, 0); bar(1, 1)
         best(0, 0)
-        if 1 < k < 5:
-            tt(A("XZ", 0, 128 * nr), IND(A("zq"), A("EZ", 0, 8 * nr)), A("DX", 0, 128 * nr), ADD)
-        if k == 5:
-            tt(A("XZ"), IND(A("l3"), A("EY")), A("DX"), ADD, [("a3", gotall)])
+        if k > 2: places(1, 2); zlist(1, 2)
+        if k > 1: cp(A("Zu", 0, 16), P(0, 32, 48)); clear(0, 2)
         best(0, 1)
         if k == 1: late(1)
         best(1, 0)
         tt(A("bi"), A("sc", 11, 384, 12), A("sc", 387, 512, 4), OP.max)
-        zlist()
         mm(P(5, 0, 256), A("DW"), A("onb", 0, 256), True, False)
-        if 1 < k < 4: cp(A("Zu", 0, 16 * nr), P(0, 0, 16 * nr))
+        if 1 < k < 5: act(A("DD"), VX, AF.Relu, bias=2.0 ** 17, scale=-(2.0 ** 17))
+        if k > 2: cp(A("Zu", 16, 32), P(1, 48, 64))
         ts(A("I1", 0, 32), A("bi"), 63, AND)
         ts(A("gi", 0, 32), A("bi"), 0xFFFC00, AND)
-        if k >= 4: cp(A("Zu", 0, 16 * nr), P(0, 0, 16 * nr))
-        if k > 1:
-            if k < 5: act(A("DD"), A("val"), AF.Relu, bias=2.0 ** 17, scale=-(2.0 ** 17))
-            clear(0)
+        if k > 2: clear(2, 3)
         cp(A("X1"), IND(A("I1"), A("E1")))
         for S in range(2):
             mm(P(4, 0, 16), A("X1", 128 * S, 128 * S + 128), A("D16b", 16 * S, 16 * S + 16), S == 0, S == 1)
         cp(A("Kt", 12, 512, 16), A("gi", 0, 32))
         ts(A("Kt", 15, 512, 16), A("bi"), 1023.5, GT)
-        if k < 5: tt(A("Kk", 0, 512, 16), A("gi", 0, 32), A("idc"), ADD)
-        else: cp(A("gi", 32, 112), A("VX", 0, 80))
+        if k < 5: ts(A("gi", 32, 64), A("bi"), 11, SHR); ts(A("gi", 64, 96), A("bi"), 1024, AND)
+        else: cp(A("gi", 32, 112), VX)
         tt(A("Kt", 13, 512, 16), A("gi", 0, 32), A("Kt", 12, 512, 16), SUB)
         cl = A("CL", 48 * nr, 48 * nr + 16)
         cp(cl, P(4, 0, 16))
@@ -582,49 +580,59 @@ def rank_program(g, core, T, topo):
                 mm(P(4, 16 + 16 * t, 32 + 16 * t), A("Sh", 128 * t, 128 * t + 128), A("ctf"))
         cp(A("La", 0, 128), IND(A("Bw"), A("CL", 48 * nr, 48 * nr + 8)))
         act(A("La", 128, 256), IND(A("Bw"), A("CL", 48 * nr + 8, 48 * nr + 16)))
+        if k < 5:
+            cp(A("Kk", 0, 512, 16), A("gi", 32, 64)); tt(A("Kk", 8, 512, 16), A("gi", 64, 96), A("idc"), ADD)
+            tt(A("Kk", 4, 512, 16), A("gi", 0, 32), A("idc"), ADD)
         tt(A("R"), P(5, 0, 256), A("La"), ADD)
         for h in range(2):
             mm(P(7, 128 + h, 192, 2), A("R", 128 * h, 128 * h + 128), A("SS", 32 * h, 32 * h + 32))
-        if nr == 3: clear(1)
+        if k > 2: clear(3, 4)
         ts(A("Lo"), A("La"), ODD, MUL)
         if k < 5: cp(A("CL", 48 * nr + 16, 48 * nr + 48), P(4, 16, 48)); late(k + 2)
+        if k >= 4: places(2, nr)
+        if k < 5: act(A("dP", 64, 80), A("dP", 64, 80), bias=4095.5 if k == 1 else 4096.0)
         act(A("st", 16, 64), P(7, 144, 192))
         al = A("al", 0, 16) if k < 5 else A("ow", 16, 32)
         if k == 5: tt(A("t2", 0, 80), A("gi", 32, 112), A("sm", 0, 80), ADD)
-        n = 0
-        for gg in (0, 2, 4, 6, 1, 3, 5, 7):
-            p0 = 16 * (gg - gg % 2); p1 = 16 * gg + 16
-            for h in ((0, 1) if n < 2 else (1, 0)):
-                b = (0, 1, 2)[n % 3] if h == 0 else (3, 6, 5)[n % 3]
-                mm(P(b, 0, 256), A("Lo" if gg % 2 else "La", 128 * h, 128 * h + 128, 1, p0, p1), A("R", 0, 256, 1, p0, p1))
-                col = A("acc", 2 * gg + h, 2 * gg + h + 1)
-                if h == 0: red(col, P(b, 0, 256), OP.max)
-                else: act(blk("CD", n), P(b, 0, 256), AF.Relu, bias=A("st", 33 + 2 * gg, 34 + 2 * gg), acc=col)
-            n += 1
-            if n == 1: tt(A("st", 64, 80) if k < 5 else A("o2", 16, 32), P(7, 128, 144), A("dP", 16, 32), SUB)
-            if n == 1 and k == 5: ts(A("o2", 0, 16), A("st", 16, 32), -(2.0 ** -15), MUL)
-            if n == 3 and k < 5: cp(A("XR"), IND(A("st", 64, 88), A("E2")))
-            if n == 3 and k == 5: cp(A("t4", 400, 432), IND(A("o2"), A("FS1")))
+        for n, ggs in enumerate(((0,), (1,), (2, 3), (4, 5), (6, 7))):
+            for h in ((0, 1) if n == 0 else (1, 0)):
+                b = ((0, 1, 2), (3, 6, 5))[h][n % 3]
+                for i, gg in enumerate(ggs):
+                    p0 = 16 * (gg - gg % 2); p1 = 16 * gg + 16
+                    mm(P(b, 256 * i, 256 * i + 256), A("Lo" if gg % 2 else "La", 128 * h, 128 * h + 128, 1, p0, p1),
+                       A("R", 0, 256, 1, p0, p1))
+                for i, gg in enumerate(ggs):
+                    col = A("acc", 2 * gg + h, 2 * gg + h + 1)
+                    if h == 0: red(col, P(b, 256 * i, 256 * i + 256), OP.max)
+                    else: act(blk("CD", gg), P(b, 256 * i, 256 * i + 256), AF.Relu, bias=A("st", 33 + 2 * gg, 34 + 2 * gg), acc=col)
+            if n == 0: tt(A("st", 64, 80) if k < 5 else A("o2", 16, 32), P(7, 128, 144), A("dP", 16, 32), SUB)
+            if n == 0 and k == 5: ts(A("o2", 0, 16), A("st", 16, 32), -(2.0 ** -15), MUL)
+            if n == 1 and k < 5: cp(A("XR"), IND(A("st", 64, 88), A("E2")))
+            if n == 2 and k >= 4: zlist(2, nr)
+            if n == 3 and k >= 4: cp(A("Zu", 32, 16 * nr), P(4, 64, 32 + 16 * nr))
+            if n == 1 and k == 5: cp(A("t4", 400, 432), IND(A("o2"), A("FS1")))
         if k < 5:
             for h in range(2):
                 mm(P(4, 256 + 128 * h, 384 + 128 * h), A("Kt", 256 * h, 256 * h + 128), A("Ib"), True, False)
                 mm(P(4, 256 + 128 * h, 384 + 128 * h), A("Kk", 256 * h, 256 * h + 128), A("I"), False, True)
             mm(P(2, 0, 16), A("DX", 0, 128), A("D16"), True, False)
-            if nr >= 2: clear(nr - 1)
+            if k == 4: clear(4, 6)
             else: act(A("Va"), P(4, 256, 512))
-        act(A("st", 80, 96), P(7, 128, 144), bias=2047.5 + (4096.0 * k if k < 5 else 1.0))
+        else:
+            act(A("st", 80, 96), P(7, 128, 144), bias=2048.5)
         tt(al, A("acc"), A("st", 48, 64), EQL)
         if k < 5:
             tt(A("XW"), IND(A("al"), A("E2")), A("XR"), MUL)
             mm(P(2, 0, 16), A("XW"), A("D16"), False, True)
-            if nr >= 2: cp(A("Va"), P(4, 256, 512))
+            tt(A("st", 80, 96), P(7, 128, 144), A("dP", 64, 80), ADD)
+            if k == 4: cp(A("Va"), P(4, 256, 512))
             act(A("NK", k, 80, 5), A("st", 16, 32))
             act(A("DD", k, 80, 5), al, bias=2.0 ** 17, scale=-(2.0 ** 17))
             act(A("ZD", k, 80, 5), A("st", 64, 80), bias=-256.0 * nr)
-            if nr < 2: tt(A("VX", k, 80, 5), al, A("st", 80, 96), MUL)
+            if k < 4: tt(A("VX", 3 * k + 2, 240, 15), al, A("st", 80, 96), MUL)
             cp(A("Wu"), P(2, 0, 16))
             if k == 1: late(7)
-            mm(P(5, 256, 496), A("Ib"), A("zb"), True, False)
+            mm(P(5, 256, 496), A("Ib"), A("PM", 0, 240), True, False)
             for t in (1, 2):
                 mm(P(5, 256 + t, 496, 3), A("I"), A("NK"), False, False)
             for rho in range(k):
@@ -633,30 +641,32 @@ def rank_program(g, core, T, topo):
                 mm(P(5, 256 + t, 496, 3), A("NI"), A("DD"), False, False)
             cp(IND(A("Wo"), A("Wu")), A("Va"))
             gr = "w%d" % k
-            dma("s", A("Wl", 0, 4096, 1, 0, 128, 16), A("Wo", 0, 4096, 1, 0, 128, 16), gr)
-            dma("s", A("Wl", 0, 4096, 1, 17, 128, 16), A("Wo", 0, 4096, 1, 0, 112, 16), gr)
-            dma("s", A("Wl", 0, 4096, 1, 3, 112, 16), A("Wo", 0, 4096, 1, 16, 128, 16), gr)
-            dma("s", A("Wl", 0, 4096, 1, 2, 128, 64), A("Wo", 0, 4096, 1, 48, 128, 64), gr)
-            dma("s", A("Wl", 0, 4096, 1, 52, 128, 64), A("Wo", 0, 4096, 1, 0, 128, 64), gr)
+            dma("s", A("Wl", 0, 4096, 1, 0, 128, 8), A("Wo", 0, 4096, 1, 0, 128, 8), gr)
+            dma("s", A("Wl", 0, 4096, 1, 17, 128, 8), A("Wo", 0, 4096, 1, 0, 112, 8), gr)
+            dma("s", A("Wl", 0, 4096, 1, 3, 112, 8), A("Wo", 0, 4096, 1, 16, 128, 8), gr)
+            for e in (0, 8):
+                dma("s", A("Wl", 0, 4096, 1, 2 + e, 128, 64), A("Wo", 0, 4096, 1, 48 + e, 128, 64), gr)
+                dma("s", A("Wl", 0, 4096, 1, 52 + e, 128, 64), A("Wo", 0, 4096, 1, e, 128, 64), gr)
             if k == 4:
                 for r in order:
-                    dma("s", ("!", T.ts[r]), A("Wo", 0, 4096, 1, 16 * r, 128, 64), "ts")
-                dma("s", A("Wf", 0, 4096, 1, 32 * q, 32 * q + 32, 16), A("Wo", 0, 4096, 1, 16 * q, 128, 64), "tf")
+                    dma("s", ("!", T.ts[r]), A("Wo", 0, 4096, 1, 16 * r + 4, 128, 64), "ts")
+                dma("s", A("Wf", 0, 4096, 1, 32 * q, 32 * q + 32, 16), A("Wo", 0, 4096, 1, 16 * q + 4, 128, 64), "tf")
                 send(lambda r: T.ts[r], T.tl[q], "at", [], [("@ts", 0)])
                 for s in order:
                     dma("s", A("Wf", 0, 4096, 1, 32 * s, 32 * s + 32, 16), ("!", T.tl[s]), "tf", [("at", gotall)])
 
     tt(A("s1"), IND(A("ow"), A("FS1")), A("t4", 400, 432), MUL)
     send(lambda r: T.s1[:, 8 * r:8 * r + 8], T.l1[:, 8 * q:8 * q + 8], "a1", [A("s1")])
-    clear(1)
+    clear(4, 6)
     ts(A("t1", 5, 81, 5), al, 8192.0, MUL)
     tt(A("t2", 5, 81, 5), al, A("st", 80, 96), MUL)
     scan(A("t0", 0, 80), A("r5", 0, 80), A("t1", 1, 81), 0.0, MUL, ADD)
     cp(A("l1", 8 * q, 8 * q + 8), A("s1", 8 * q, 8 * q + 8))
     tt(A("t0", 0, 80), A("t0", 0, 80), A("t2", 1, 81), ADD)
+    cp(A("PJ"), A("PJb")); cp(A("FR"), A("t2", 128, 144))
     for s in range(4):
         act(A("t4", 80 * s, 80 * s + 80), A("t0", 0, 80), AF.Abs, bias=A("fc", 52 + s, 53 + s))
-    clear(2); clear(3)
+    clear(6, 8)
     mm(P(4, 0, 16), A("onb", 0, 128, 1, 0, 1), A("tb", 0, 16, 1, 0, 1), True, False)
     scan(A("t5", 0, 320), A("t3", 0, 320), A("t4", 0, 320), 0.0, ADD, OP.min)
     ts(A("s2"), IND(A("t5", 0, 320), A("FS2")), 4096.0, OP.min, -2048.0, ADD)

from concourse.bass import DstId, RemoteDMATransfer
from concourse.mybir import AluOpType as OP, AxisListType as AX, ActivationFunctionType as AF

F32, BF, I32, U16, F16 = "float32", "bfloat16", "int32", "uint16", "float16"
SB = {
    "Fw": (4352, BF), "Nw": (4096, F32), "Wo": (5120, F32), "Wl": (4096, F32), "Bw": (4096, BF), "Wf": (5120, F32),
    "Fd": (4096, BF), "Vd": (4096, F16), "CD": (3072, BF), "PM": (1536, BF), "M": (512, BF),
    "sh": (16, I32), "lh": (64, I32), "sn": (1024, I32), "sf": (1024, BF), "sx": (1152, F16), "lx": (1152, F16), "lf": (1024, BF),
    "hf": (64, F32), "hx": (512, F16),
    "ic": (8, I32), "fc": (56, F32), "iof": (16, F32), "D16": (16, F32), "D16b": (32, BF), "BD": (16, F32),
    "I": (128, F32), "t0": (512, F32), "t1": (512, F32), "t2": (512, F32), "t3": (512, F32), "t4": (512, F32),
    "t5": (512, F32), "tb": (128, BF), "pw": (24, F32), "sg": (16, F32), "inc": (16, F32), "EU": (336, U16),
    "mL": (256, F32), "DX": (512, F32), "dP": (80, F32), "on": (256, F32), "onb": (320, BF),
    "r5": (80, F32), "r12": (192, F32), "r4": (128, F32), "PJ": (512, F16), "PJb": (512, BF), "Kt": (512, BF),
    "Kk": (512, F32), "idc": (32, F32), "CI": (256, BF), "CW": (1152, BF), "SF": (40, BF), "SM": (384, BF), "SV": (40, BF),
    "SU": (8, BF), "SC": (24, BF), "Sh": (256, F32), "SS": (64, BF), "SQ": (512, F16), "mH": (128, F32), "RH": (4, F16),
    "mD": (128, F32), "Ib": (128, BF), "D256": (16, F32), "zr": (256, F32), "NI": (128, BF), "DW": (128, BF),
    "VX": (240, F32), "NK": (80, F32), "DD": (80, BF), "cum": (240, F32), "val": (80, F32), "sv": (240, I32), "vi": (32, I32),
    "Li": (24, I32), "Rf": (24, F32), "XL": (256, F32), "XR": (128, F32), "cG": (256, F32),
    "cT": (256, F32), "cu": (256, U16), "zq": (88, F32), "ZD": (80, F32), "XZ": (512, F32),
    "pen": (1280, BF), "sc": (512, F32), "bi": (32, I32), "I1": (40, I32), "gi": (112, I32), "X1": (256, BF),
    "CL": (240, U16), "ctf": (16, F32), "La": (256, BF), "Lo": (256, BF), "R": (256, BF),
    "st": (96, F32), "acc": (16, F32), "al": (24, F32), "ow": (32, F32), "XW": (128, F32),
    "Va": (256, F32), "sm": (96, F32),
    "o2": (32, F32), "s1": (32, F32), "l1": (32, F32), "s2": (64, F16), "l2": (64, F16), "yo": (256, F32),
    "s3": (64, F32), "l3": (72, F32),
}
LISTS = {"E1": (0, 16), "E2": (16, 8), "EL": (32, 16), "EZ": (48, 32), "PC": (80, 16), "EH": (96, 32), "FS1": (128, 2),
         "FS2": (132, 4), "FR": (144, 16), "FS3": (176, 4), "EY": (192, 32), "Lu": (224, 16), "Mu": (240, 16), "Wu": (256, 16),
         "Zu": (272, 64)}
SCRATCH = {k: ("sbuf", [128, n], d) for k, (n, d) in SB.items()}
for _i in range(8):
    SCRATCH["p%d" % _i] = ("psum", [128, 512], F32)
SCRATCH["ts"] = ("dram", [4, 128, 64], F32)
SCRATCH["tl"] = ("dram", [4, 128, 64], F32)
NDMA = 30
SEMAPHORES = (["qv", "qa", "qt", "qg", "sent", "ah", "at", "a1", "a2", "a3"] + ["an%d" % i for i in range(4)]
              + ["af%d" % i for i in range(4)] + ["d%d" % i for i in range(NDMA)])
BIG = float(2 ** 40)
PH = ((0, 12), (12, 4))


def A(name, c0=0, c1=None, cs=1, p0=0, p1=128, ps=1):
    if name in LISTS:
        o, n = LISTS[name]
        return ("EU", o + c0, o + (n if c1 is None else c1), cs, p0, p1, ps)
    return (name, c0, SB[name][0] if c1 is None else c1, cs, p0, p1, ps)


def P(b, c0, c1, cs=1, p0=0, p1=128):
    return ("p%d" % b, c0, c1, cs, p0, p1, 1)


def IND(win, off):
    return ("*", win, off)


def _hit(a, b):
    if a[3] == b[3] and (a[1] - b[1]) % a[3]:
        return False
    return a[0] == b[0] and a[1] < b[2] and b[1] < a[2] and a[4] < b[5] and b[4] < a[5]


def rank_program(g, core, T, topo):
    q = T.rank_of(core)
    if q is None:
        return
    ops = []
    groups = {}

    def ap(a):
        if not isinstance(a, tuple):
            return a
        if a[0] == "*":
            return ap(a[1]).indirect(ap(a[2]))
        if a[0] == "!":
            return a[1]
        n, c0, c1, cs, p0, p1, ps = a
        return T[n][slice(p0, p1, ps) if ps > 1 else slice(p0, p1), slice(c0, c1, cs) if cs > 1 else slice(c0, c1)]

    def add(qu, emit, outs, ins, grp=None, waits=()):
        rd, wr = [], []
        for a in ins:
            if isinstance(a, tuple) and a[0] != "!":
                rd += [a[1], a[2]] if a[0] == "*" else [a]
        for a in outs:
            if isinstance(a, tuple) and a[0] != "!":
                if a[0] == "*":
                    wr.append(a[1]); rd.append(a[2])
                else:
                    wr.append(a)
        ops.append([qu, emit, rd, wr, grp, list(waits)])

    def cp(o, i, w=()): add("v", lambda: g.vector.tensor_copy(ap(o), ap(i)), [o], [i], None, w)
    def tt(o, a, b, op, w=()): add("v", lambda: g.vector.tensor_tensor(ap(o), ap(a), ap(b), op), [o], [a, b], None, w)
    def ms(o, c): add("v", lambda: g.vector.memset(ap(o), c), [o], [])
    def red(o, i, op): add("v", lambda: g.vector.tensor_reduce(ap(o), ap(i), AX.X, op), [o], [i])
    def scan(o, a, b, i0, o0, o1): add("v", lambda: g.vector.tensor_tensor_scan(ap(o), ap(a), ap(b), i0, o0, o1), [o], [a, b])
    def tr(o, i): add("v", lambda: g.vector.transpose(ap(o), ap(i)), [o], [i])

    def ts(o, a, s1, o0, s2=None, o1=None, w=()):
        if s2 is None:
            add("v", lambda: g.vector.tensor_scalar(ap(o), ap(a), ap(s1), None, o0), [o], [a, s1], None, w)
        else:
            add("v", lambda: g.vector.tensor_scalar(ap(o), ap(a), ap(s1), ap(s2), o0, o1), [o], [a, s1, s2])

    def act(o, i, f=AF.Identity, bias=None, scale=None, acc=None, w=()):
        kw = {}
        if bias is not None: kw["bias"] = bias
        if scale is not None: kw["scale"] = scale
        if acc is not None: kw["accum_out"] = acc
        add("a", lambda: g.scalar.activation(ap(o), ap(i), f, **{k: ap(v) for k, v in kw.items()}), [o, acc], [i, bias, scale], None, w)

    def mm(o, l, r, start=True, stop=True, w=()):
        add("t", lambda: g.tensor.matmul(ap(o), ap(l), ap(r), start, stop), [o], [l, r], None, w)

    def iota(o, pat, base=0, cm=0):
        if SB[o[0]][1] == I32:
            add("g", lambda: g.iota(ap(o), pat, base, cm), [o], [])
        else:
            add("g", lambda: g.iota(ap(o), pat, base, cm, allow_small_or_imprecise_dtypes=True), [o], [])

    def sel(o, pat, op, base, cm, src=None, fill=0.0):
        if src is None:
            n = 1
            for _s, c in pat: n *= c
            src = A("onb" if SB[o[0]][1] == BF else "on", 0, n)
        add("g", lambda: g.affine_select(ap(o), ap(src), pat, op, fill, base, cm), [o], [src])

    def zero(o):
        iota(o, [[0, len(range(o[1], o[2], o[3]))]])

    def own(o, pat):
        sel(o, [[-16 * s, c] for s, c in pat], OP.is_ge, 0, 1, o); sel(o, [[16 * s, c] for s, c in pat], OP.is_ge, 15, -1, o)

    def dma(qu, o, i, grp, w=()):
        groups[grp] = groups.get(grp, 0) + 1
        eng = g.sync if qu == "s" else g.scalar
        add(qu, lambda: eng.dma_start(ap(o), ap(i)), [o], [i], grp, w)

    def shares(src):
        others = [c for c in T.cores if c != src]
        far = [c for c in others if topo.chip(c) != topo.chip(src)]
        taken, out = set(), {}
        for i, c in enumerate(far):
            e = topo.engines(src, c); n = len(e) // len(far)
            out[c] = e[i * n:(i + 1) * n]; taken |= set(e)
        near = [c for c in others if c not in far]
        for i, c in enumerate(near):
            e = [x for x in topo.engines(src, c) if x not in taken]; n = len(e) // len(near)
            out[c] = e[i * n:(i + 1) * n]
        return out
    mine = shares(core)
    got = {s: len(shares(T.cores[s])[core]) for s in range(4) if s != q}
    gotall = sum(got.values())
    nsent = [0]

    def send(src_of, dst, sem, reads, w=()):
        trs = []
        for r in range(4):
            if r != q:
                c = T.cores[r]; rid, pid, _ = topo.addr(c)
                trs.append(RemoteDMATransfer(dst_ids=[DstId(rid=rid, pnc=pid)], dma_engine_mask=sum(1 << e for e in mine[c]),
                                             remote_sem=T.sem[sem], src=src_of(r), dst=dst))
                nsent[0] += len(mine[c])
        add("g", lambda: g.remote_dma_fused(trs, local_sem=T.sem.sent), [], reads, "remote", w)

    def fc(k): return A("fc", k, k + 1)
    AND, SHR, MUL, ADD, SUB = OP.bitwise_and, OP.logical_shift_right, OP.mult, OP.add, OP.subtract
    EQL, GT, NE = OP.is_equal, OP.is_gt, OP.not_equal
    blk = lambda n, s: A(n, 256 * s, 256 * s + 256)
    near = [s for s in range(4) if s != q and topo.chip(T.cores[s]) == topo.chip(core)]
    far = [s for s in range(4) if s != q and s not in near]
    order = far + near

    dma("s", A("sh"), ("!", T.home[:, :]), "ldh")
    for r in order:
        dma("a", blk("sf", r), ("!", T.feat[32 * r:32 * r + 32, :]), "ldf")
    for r in order + [q]:
        dma("s", blk("sn", r), ("!", T.nb[32 * r:32 * r + 32, :]), "ln%d" % r)
    dma("a", blk("lf", q), ("!", T.feat[32 * q:32 * q + 32, :]), "owf")
    PF = fc(8)
    iota(PF, [[0, 1]], 0, 1)
    iota(A("iof"), [[1, 16]])
    iota(A("tb"), [[64, 2], [0, 4], [4, 16]])
    iota(A("t3", 0, 16), [[2, 2], [4, 4], [0, 2]], -16)
    iota(A("t3", 16, 48), [[16, 4], [0, 8]])
    iota(A("mH"), [[1, 8], [0, 16]])
    zero(A("Li")); zero(A("I1"))
    send(lambda r: T.sh[:, :], T.lh[:, 16 * q:16 * q + 16], "ah", [A("sh")])
    iota(A("mL"), [[0, 8], [1, 2], [0, 16]])
    zero(A("VX")); iota(A("dP", 0, 16), [[0, 8], [8, 2]], 4096)

    P64, P32, G, P8, P4, P2 = [fc(k) for k in range(1, 7)]
    X, X8, HX, RK, ODD, X1, X6, X13, EQ, XG = [fc(k) for k in range(9, 19)]
    io = lambda a, b: A("iof", a, b)
    d16 = lambda k: A("D16", k, k + 1)
    BD, D8 = A("BD", 0, 8), A("BD", 8, 16)
    ms(A("zr"), 0.0); ms(A("t1", 0, 24), 2.0)
    scan(A("pw"), A("t1", 0, 24), A("zr", 0, 24), 2.0 ** -8, MUL, ADD)
    ts(A("ic"), A("pw", 0, 8), PF, MUL, -0.496, ADD)
    ms(A("onb"), 1.0)
    cp(A("fc", 0, 8), A("ic"))
    ms(A("on"), 1.0)
    ts(X, G, -16.0, MUL, PF, ADD); ts(X8, P8, -8.0, MUL, PF, ADD); ts(HX, G, -2.0, MUL, P8, ADD)
    ts(A("D16"), io(0, 16), X, EQL)
    ts(BD, io(0, 8), G, EQL)
    act(A("Wo", 0, 256), A("zr"), AF.Silu)
    act(A("inc", 0, 6), A("pw", 7, 13), scale=d16(7)); act(A("inc", 6, 12), A("pw", 7, 13), scale=d16(6))
    act(A("Wl", 0, 1), A("zr", 0, 1))
    act(A("sg"), A("D16"), scale=-2.0, bias=1.0)
    ts(fc(41), P4, -4.0, MUL, PF, ADD)
    ts(fc(30), X, 14.5, OP.is_lt)
    ts(fc(32), X, 11.5, OP.is_lt)
    ts(D8, io(0, 8), X8, EQL); tt(EQ, X8, G, EQL)
    ts(fc(43), P64, 4.0, MUL, fc(41), ADD)
    ts(A("Bw", 0, 1), fc(32), 2047.0, MUL, fc(30), ADD)
    tt(fc(37), fc(32), fc(30), SUB)
    ts(A("EH"), A("t3", 16, 48), X, ADD)
    ts(A("SU"), io(0, 8), fc(43), EQL)
    for qt in range(4):
        ts(A("SQ", 128 * qt, 128 * qt + 128), A("tb"), float(qt), ADD, PF, EQL)
    ts(A("mH"), A("mH"), X8, EQL)
    small = [(RK, P64, -4.0, G), (ODD, P32, -2.0, G), (X1, P2, -2.0, PF), (X13, P8, -4.0, P2), (X6, P2, 16.0, X1), (XG, X, 16.0, G),
             (A("dP", 64, 80), io(0, 16), 2.0 ** 19, 2048.0)]
    for k in range(12):
        n = min(1 << k, 1024)
        act(A("Wl", 1 << k, (1 << k) + n), A("Wl", 0, n), bias=A("inc", k, k + 1))
        if k < 8: act(A("Bw", 1 << k, 2 << k), A("Bw", 0, 1 << k), scale=A("sg", k, k + 1))
        if k < len(small):
            o, i, s, b = small[k]; act(o, i, scale=s, bias=b)

    def lst(name, src, col, zcol, c):
        n = LISTS[name][1]
        return [lambda: ts(A("t5", c, c + n), src, col, ADD, EQ, MUL), lambda: ts(A(name), A("t5", c, c + n), float(zcol), ADD)]
    el, e1, e2 = lst("EL", A("t3", 0, 16), HX, 16, 0), lst("E1", io(0, 16), fc(21), 32, 16), lst("E2", A("t1", 48, 56), HX, 16, 32)
    fill = [lambda: ts(fc(19), X8, 32.0, MUL), lambda: ts(fc(20), HX, 16.0, MUL), el[0],
            lambda: ts(A("t1", 48, 56), io(0, 8), 2.0, MUL, -16.0, ADD), lambda: ts(fc(34), d16(14), -0.75, MUL, fc(37), SUB),
            lambda: ts(A("PC"), io(0, 16), fc(19), ADD, fc(20), ADD), lambda: ts(fc(21), fc(20), -32.0, ADD), el[1], e2[0],
            lambda: ts(A("RH"), io(0, 4), float(4 * q), ADD, P8, EQL), lambda: tt(A("t1", 32, 48), A("pw", 7, 23), A("D16"), MUL),
            e1[0], e2[1], lambda: cp(A("lh", 16 * q, 16 * q + 16), A("sh")), lambda: red(fc(38), A("t1", 32, 48), ADD), e1[1]]
    sel(A("Ib"), [[1, 128]], EQL, 0, -1)

    def pieces(ss, b):
        for i, r in enumerate(ss):
            for c in range(2):
                for m in range(2):
                    mm(P(b, 16 * i + 2 * c + m, 16 * i + 16, 4), A("sf" if r != q else "lf", 256 * r + 128 * c, 256 * r + 128 * c + 128),
                       A("SU", 4 * m, 4 * m + 4))
        yield
        cp(A("X1", 0, 16 * len(ss)), P(b, 0, 16 * len(ss)))
        yield
        for i, r in enumerate(ss):
            cp(A("sx", 288 * r + 256, 288 * r + 288, 2), A("X1", 16 * i, 16 * i + 16))
            tt(A("sx", 288 * r + 257, 288 * r + 288, 2), P(b, 16 * i, 16 * i + 16), A("X1", 16 * i, 16 * i + 16), SUB)
        yield
    step = pieces(order, 4); next(step)
    for i, r in enumerate(order):
        for f in fill[(0, 8, 16)[i]:(8, 16, 16)[i]]: f()
        if i == 1: next(step)
        ts(A("sx", 288 * r, 288 * r + 256), blk("sn", r), -2048.0, ADD)
        if i == 1: next(step)
    send(lambda r: T.sx[:, 288 * r:288 * r + 288], T.lx[:, 288 * q:288 * q + 288], "an%d" % q,
         [A("sx", 288 * r, 288 * r + 288) for r in order])
    send(lambda r: T.sf[:, 256 * r:256 * r + 256], T.lf[:, 256 * q:256 * q + 256], "af%d" % q, [blk("sf", r) for r in order])
    step = pieces([q], 5); next(step); next(step)
    ts(A("sx", 288 * q, 288 * q + 256), blk("sn", q), -2048.0, ADD)
    next(step)
    ts(A("Bw", 256, 512), A("Bw", 0, 256), A("sg", 8, 9), MUL)
    ts(A("mL"), A("mL"), HX, EQL)
    ts(A("Bw", 512, 1024), A("Bw", 0, 512), A("sg", 9, 10), MUL)

    def spare(rho):
        dx = A("DX", 128 * rho, 128 * rho + 128)
        iota(dx, [[0, 8], [8, 2], [-255, 8]], 4096 + 256 * rho, 16)
        own(dx, [[0, 16], [1, 8]])
    sel(A("SF", 24, 40), [[1, 2], [16, 8]], EQL, 6, -1)
    for row in (5, 13):
        sel(A("SF", 24, 40), [[0, 2], [16, 8]], NE, row, -1, A("SF", 24, 40), 1024.0)
    iota(A("CW", 640, 832, 1, 0, 1), [[0, 16], [-64, 12]], 960); iota(A("CW", 832, 960, 1, 0, 1), [[0, 32], [-64, 4]], 192)
    zero(A("Wo", 256, 1024))
    iota(A("t2", 64, 96), [[1, 4], [10, 8]], 1 - 80)
    iota(A("t2", 128, 144), [[1, 2], [8, 4], [4, 2]], 2)
    iota(A("t2", 160, 192), [[2, 4], [8, 8]], -64)
    iota(A("t1", 256, 264), [[1, 8]])
    iota(A("t1", 264, 272, 4), [[4, 2]], 3); iota(A("t1", 275, 280, 4), [[4, 2]], 0)
    for m in range(2):
        iota(A("t1", 265 + 4 * m, 268 + 4 * m), [[1, 3]], 4 * m); iota(A("t1", 272 + 4 * m, 275 + 4 * m), [[1, 3]], 4 * m + 1)
    sel(A("r12"), [[0, 16], [1, 12]], GT, 0, 0)
    sel(A("r4"), [[0, 32], [1, 4]], GT, 0, 0)
    for h in range(2):
        zero(A("Kt", 256 * h, 256 * h + 128))
    iota(A("Kt", 14, 512, 16), [[-512, 2], [0, 16]], 1020, -4)
    for h in range(2):
        sel(A("PJb", 256 * h, 256 * h + 256), [[1, 16], [128, 2], [16, 8]], EQL, -128 * h, -1)
    iota(A("idc"), [[-128, 2], [0, 4], [-256, 4]], 1023, -1)
    for h in range(2):
        zero(A("Kk", 256 * h, 256 * h + 128))
    sel(A("I"), [[1, 128]], EQL, 0, -1)
    zero(A("al", 16, 24)); zero(A("st", 80, 88))
    spare(0)
    for ph, (f, n) in enumerate(PH):
        iota(A("SM", 288 * ph, 288 * ph + 24 * n), [[0, 3], [1, 8], [0, n]])
    zero(A("ZD")); zero(A("PM", 0, 256))
    iota(A("CI", 0, 256, 1, 0, 1), [[-1, 256]], 255)
    for ph, (f, n) in enumerate(PH):
        iota(A("CW", 480 * ph, 480 * ph + 24 * n, 1, 0, 1), [[0, 6], [-256, 4], [0, n]], 768)
    zero(A("zq")); zero(A("Rf"))
    iota(A("SF", 0, 24), [[0, 24]], 1024); own(A("SF", 0, 24), [[0, 3], [1, 8]])
    zero(A("SV", 0, 24))
    for row, wt in ((0, -2048.0), (8, -1.0)):
        sel(A("SV", 0, 24), [[2, 3], [16, 8]], NE, row, -1, A("SV", 0, 24), wt)
        for m in range(2):
            sel(A("SV", 9 + 4 * m, 12 + 4 * m), [[16, 3]], NE, 64 * m + 17 + row, -1, A("SV", 9 + 4 * m, 12 + 4 * m), wt)
            sel(A("SV", 16 + 4 * m, 19 + 4 * m), [[16, 3]], NE, 64 * m + 3 + row, -1, A("SV", 16 + 4 * m, 19 + 4 * m), wt)
    sel(A("SV", 24, 40), [[1, 2], [16, 8]], EQL, 6, -1)

    def rest():
        iota(A("mD"), [[0, 8], [1, 16]]); sel(A("r5"), [[0, 16], [1, 5]], GT, 0, 0)
        for rho in range(1, 4):
            spare(rho)
        iota(A("PM", 1280, 1536), [[0, 256]], 255)
        iota(A("ow", 0, 16), [[0, 16]], 1); iota(A("tb", 0, 16, 1, 0, 1), [[1, 16]])
        zero(A("l3", 64, 72)); iota(A("fc", 52, 56), [[-8192, 4]], -12288)
        zero(A("t3", 0, 320)); sel(A("t3", 0, 320), [[0, 64], [1, 5]], NE, 0, 0, A("t3", 0, 320), 8192.0)

    bank = [0]; nsum = [0]
    wf = lambda s: [("af%d" % s, got[s])] if s != q else []
    wn = lambda s: [("an%d" % s, got[s])] if s != q else []

    def spread(s, engs="aa"):
        for half in range(2):
            b = (0, 1, 2, 3, 6, 7, 2, 3)[bank[0]]; bank[0] += 1
            for j in range(2):
                mm(P(b, 256 * j, 256 * j + 256), A("SQ", 128 * (2 * half + j), 128 * (2 * half + j) + 128),
                   A("sx" if s == q else "lx", 288 * s, 288 * s + 256), w=wn(s))
            o = A("Nw", 1024 * s + 512 * half, 1024 * s + 512 * half + 512)
            if engs[half] == "a": act(o, P(b, 0, 512), bias=2048.0)
            else: ts(o, P(b, 0, 512), 2048.0, ADD)

    def sums(ss, eng, b=5):
        s = ss[0]
        for r in range(4):
            mm(P(b, 0, 128, 1, 32 * r, 32 * r + 32), A("sx" if s == q else "lx", 288 * s + 256, 288 * s + 288), A("Ib"), w=wn(s))
        (act if eng == "a" else cp)(A("t0", 128 * s, 128 * s + 128), P(b, 0, 128))
        for m in range(2):
            for e, row in enumerate((5, 13)):
                dma("s", A("Wl", 1024 * s, 1024 * s + 1024, 1, 64 * m + row, 64 * m + 64, 16),
                    A("t0", 128 * s, 128 * s + 128, 1, 2 * m + e, 128, 4), "su")
    ts(A("Bw", 2048, 3072), A("Bw", 0, 1024), A("sg", 11, 12), MUL)
    ts(A("Wl", 3072, 4096), A("Wl", 1024, 2048), A("inc", 11, 12), ADD)
    spread(q); sums([q], "a")
    ts(A("hf"), A("lh"), -2048.0, ADD, w=[("ah", gotall)])
    sums(near, "a"); spread(near[0])
    for r in range(4):
        tt(A("hx", 128 * r, 128 * r + 128), IND(A("hf"), A("EH", 8 * r, 8 * r + 8)), A("mH"), MUL)
        for m in range(2):
            mm(P(4, 8 * m + 2 * r, 8 * m + 2 * r + 2), A("hx", 128 * r, 128 * r + 128), A("RH", 2 * m, 2 * m + 2))
    ts(A("Bw", 3072, 4096), A("Bw", 2048, 3072), A("sg", 10, 11), MUL)
    ts(A("Li", 0, 16), P(4, 0, 16), 2048.0, ADD); tt(A("VX", 0, 240, 15), P(4, 0, 16), A("dP", 64, 80), ADD)
    tt(A("XL"), IND(A("Li"), A("EL")), A("mL"), MUL)
    sums(far[:1], "a", 0); sums(far[1:], "a", 1)
    spread(far[0], "av"); spread(far[1], "av")
    for u in range(2):
        mm(P(4, 16 + u, 32, 2), A("XL", 128 * u, 128 * u + 128), D8)
    cp(A("Lu"), P(4, 16, 32))
    act(A("Bw", 1024, 2048), A("Bw", 0, 1024), scale=A("sg", 10, 11))
    for s in [q] + near + far:
        dma("s", A("Fd", 1024 * s, 1024 * s + 1024, 1, 0, 32), blk("lf", s), "f1", wf(s))
    for c in range(1, 4):
        dma("s", A("Wo", 1024 * c, 1024 * c + 1024), A("Wo", 0, 1024), "wz")
    for gg in range(8):
        dma("s", A("Fw", 0, 4096, 1, 16 * gg, 16 * gg + 16), A("Fd", 0, 4096, 1, 16 * (gg // 4), 16 * (gg // 4) + 16), "f2")

    def late(k):
        if k == 0:
            for o, i, s, b in [(fc(22), RK, -(2.0 ** 23), 3 * 2.0 ** 23), (fc(24), HX, 5.0, None), (fc(51), fc(32), -(2.0 ** -12), None),
                               (fc(35), d16(15), fc(22), None), (fc(40), d16(15), -12.0 * 2 ** 22, fc(37)),
                               (fc(39), fc(38), fc(51), None), (fc(36), fc(34), 2.0 ** 15, fc(35)),
                               (A("D16b", 0, 16), A("D16"), 64.0, None), (A("D16b", 16, 32), A("D16"), None, None),
                               (fc(50), fc(36), -1.0, None)]:
                act(o, i, scale=s, bias=b)
        if k == 7:
            act(A("Fw", 4096, 4352), A("zr"))
            for o, i, s, b in [(fc(31), P4, -24.0, X6), (fc(27), X1, 5.0, 4.0), (fc(23), X, 16.0, 4096.0), (fc(25), P8, -16.0, fc(31)),
                               (fc(28), HX, 40.0, fc(27)), (fc(26), HX, 2.0, fc(25)), (fc(47), X13, 1.0, fc(28)),
                               (fc(29), X13, 80.0, fc(28)), (fc(48), fc(47), 1.0, -3.0)]:
                act(o, i, scale=s, bias=b)
        if k == 1:
            act(A("DW"), A("Ib"), scale=fc(37))
            for m in range(2):
                for o, i, n in ((0, 16, 48), (48, 0, 16), (128, 48, 16), (144, 0, 48)):
                    act(A("Sh", 64 * m + o, 64 * m + o + n), A("I", 64 * m + i, 64 * m + i + n))
            act(A("dP", 0, 16), A("dP", 0, 16), bias=XG)
            act(A("SS", 0, 8), BD, scale=fc(39)); act(A("SS", 8, 16), BD, scale=fc(50)); act(A("SS", 16, 24), BD, scale=fc(40))
            act(A("dP", 16, 32), A("dP", 0, 16), bias=-2047.5); act(A("dP", 32, 48), A("dP", 0, 16), bias=-65536.0, scale=16.0)
            act(A("SS", 24, 32), A("SS", 16, 24), scale=-1.0)
            act(A("SS", 32, 56), A("SS", 0, 24)); act(A("SS", 56, 64), A("zr", 0, 8))
            act(A("NI"), A("Ib"), scale=-(2.0 ** 23)); act(A("D256"), A("D16"), scale=1.0 / 16)
            act(A("NK"), A("zr", 0, 80)); act(A("DD"), A("zr", 0, 80), bias=2.0 ** 17)
            act(A("NK", 0, 80, 5), A("zr", 0, 16), bias=-BIG)
        ez, ey = lst("EZ", A("t2", 64, 96), fc(24), 80, 48), lst("EY", A("t2", 160, 192), HX, 64, 80)
        if k == 3:
            ez[0](); ts(A("SC"), A("t1", 256, 280), G, EQL, fc(36), MUL); ts(A("SM"), A("SM"), G, EQL, -1024.0, MUL); ez[1]()
        if k == 4:
            ey[0](); ts(A("FS1"), io(0, 2), 4.0, MUL, fc(26), ADD); ts(A("FS3"), io(0, 4), 10.0, MUL, fc(48), ADD); ey[1]()
        if k == 5:
            ts(A("mD"), A("mD"), X, EQL); ts(A("FS2"), io(0, 4), 10.0, MUL, fc(29), ADD)

    def SCO(ph, h, c0, c1, cs=1):
        return P(5 + h, c0, c1, cs) if ph == 0 else P(7, 64 * h + c0, 64 * h + c1, cs)

    def open_scores(k, part):
        one = A("onb", 0, 128, 1, 0, 1)
        if part == 1:
            mm(SCO(0, 0, 0, 192), one, A("CW", 640, 832, 1, 0, 1), True, False)
            return
        mm(SCO(0, 1, 0, 192), one, A("CW", 640, 832, 1, 0, 1), True, False)
        mm(P(7, 0, 128), one, A("CW", 832, 960, 1, 0, 1), True, False)
        for ph, (f, n) in enumerate(PH):
            for h in range(2 if k > 1 else 0):
                mm(P(2 * ph + h, 0, 24 * n), one, A("CW", 480 * ph, 480 * ph + 24 * n, 1, 0, 1), True, False)
                mm(P(2 * ph + h, 0, 24 * n), A("CI", 128 * h, 128 * h + 128, 1, 0, 1), A("onb", 0, 24 * n, 1, 0, 1), False, False)
    WO = A("Wo", 0, 4096)
    VX = A("VX", 2, 240, 3)

    for k in range(1, 6):
        nr = k - 1
        if k > 1:
            blocks = [i for i in range(3 * nr) if i != 3 * nr - 3]
            calls = {1: ((cp, 1, 1), (act, 2, 1)), 2: ((cp, 0, 2), (act, 4, 2), (act, 2, 1)),
                     3: ((cp, 0, 3), (act, 4, 2), (act, 7, 1), (cp, 3, 1), (act, 8, 1)),
                     4: ((cp, 0, 4), (act, 5, 4), (act, 10, 1), (cp, 4, 1), (act, 11, 1))}[nr]
            for n, (f, i0, w) in enumerate(calls):
                f(A("CD", 256 * i0, 256 * (i0 + w)), IND(WO, A("CL", 16 * i0, 16 * (i0 + w))))
                for i in range(i0, i0 + w):
                    rho, t = i // 3 + 1, i % 3
                    for h in range(2):
                        c0 = 256 + 15 * h + 3 * rho + t
                        mm(P(5, c0, 496, 30), A("CD", 256 * i + 128 * h, 256 * i + 128 * h + 128), A("SC", 8 * t, 8 * t + 8), False,
                           n == len(calls) - 1 and h == 1)
            pm = lambda: tt(blk("PM", nr), IND(A("Fw"), A("Wu")), A("M", 0, 256) if k > 2 else A("PM", 0, 256), OP.max)
            if len(blocks) % 2: pm()
            if nr == 4: tt(A("VX", 3 * nr + 2, 240, 15), al, A("st", 80, 96), MUL)
            open_scores(k, 0)
            if k == 5: act(A("sm", 0, 80), VX, AF.Sign)
            ts(A("cum"), P(5, 256, 496), 0.0, GT, 32768.0, MUL)
            if k == 5: scan(A("t0", 0, 80), A("r5", 0, 80), A("sm", 0, 80), 0.0, MUL, ADD)
            scan(A("sv"), A("cum"), A("VX"), 0.0, ADD, OP.max)
            if k == 5: ts(A("t0", 80, 96), A("t0", 4, 80, 5), 4.0, EQL, 4096.0, MUL)
            ts(A("Li", 0, 16), A("sv", 14, 240, 15), 4095, AND)
            ts(A("vi", 0, 16), A("sv", 14, 240, 15), 0x7000, AND)
            if k == 5: ts(A("vi", 16, 32), A("sv", 14, 240, 15), 0x78000, AND)
            else: tt(A("val"), A("sv", 2, 240, 3), VX, EQL)
            for u in range(2):
                tt(A("XL", 128 * u, 128 * u + 128), IND(A("Li"), A("EL", 8 * u, 8 * u + 8)), A("mL", 128 * u, 128 * u + 128), MUL)
                mm(P(4, 16 + u, 32, 2), A("XL", 128 * u, 128 * u + 128), D8)
                if k == 5 and u == 0:
                    ts(A("sm", 80, 96), A("vi", 16, 32), 0.0, EQL)
            if k == 5:
                tt(A("sm", 80, 96), A("sm", 80, 96), A("t0", 80, 96), MUL)
                tt(A("t0", 96, 112), A("vi", 0, 16), A("dP", 32, 48), ADD)
                tt(A("val"), A("sv", 2, 240, 3), VX, EQL)
                tt(A("Rf", 0, 16), A("sm", 80, 96), A("t0", 96, 112), ADD)
            else:
                tt(A("Rf", 0, 16), A("vi", 0, 16), A("dP", 32, 48), ADD)
            tt(VX, VX, A("val"), MUL)
            act(A("XR"), IND(A("Rf"), A("E2")))
            if k == 5: act(A("sm", 0, 80), VX, AF.Sign)
            cp(A("Lu"), P(4, 16, 32))
            tt(A("zq", 0, 80), P(5, 256, 496, 3), VX, EQL)
            mm(P(5, 200, 216), A("XR"), A("D256"))
            act(A("cG"), IND(A("Nw"), A("Lu")))
            if len(blocks) % 2 == 0: pm()
            cp(A("Mu"), P(5, 200, 216))
            tt(A("zq", 0, 80), A("zq", 0, 80), A("ZD"), MUL)
            open_scores(k, 1)
            act(A("M", 0, 256), IND(A("PM", 0, 256 * k if k < 5 else 1536), A("Mu")))
            sel(A("M", 256, 512), [[0, 256]], OP.is_ge, 0, 0, A("M", 0, 256))
            if k == 2: rest()
        else:
            cp(A("cG"), IND(A("Nw"), A("Lu")))
            open_scores(k, 0); open_scores(k, 1)
            late(0)
        tr(A("cT"), A("cG"))
        cp(A("cu", 0, 64), IND(A("cT"), A("PC", 0, 4))); cp(A("cu", 64, 256), IND(A("cT"), A("PC", 4, 16)))
        if k > 1:
            if k == 5:
                act(A("s3"), IND(A("zq"), A("FS3")))
                send(lambda r: T.s3[:, 16 * r:16 * r + 16], T.l3[:, 16 * q:16 * q + 16], "a3", [A("s3")])
            for b in range(4):
                ph, h = b // 2, b % 2; n = PH[ph][1]; mh = A("M", 128 * h, 128 * h + 128)
                mm(P(b, 0, 24 * n), mh, A("SM", 288 * ph, 288 * ph + 24 * n), False, False)
                mm(SCO(ph, h, 0, 16 * n), mh, A("SM", 288 * ph, 288 * ph + 16 * n), False, False)

        def short(ph, h):
            n = PH[ph][1]; c = 960 * ph + 40 * n * h
            act(A("pen", c, c + 24 * n), P(2 * ph + h, 0, 24 * n), AF.Relu, bias=1.0, scale=-1.0)

        def bar(ph, h):
            n = PH[ph][1]; c = 960 * ph + 40 * n * h
            for o0, o1, t in ((0, 16, 0), (0, 16, 1), (0, 8, 2), (8, 16, 0)):
                mm(SCO(ph, h, o0 * n, o1 * n), A("NI"), A("pen", c + 8 * n * t, c + n * (8 * t + o1 - o0)), False,
                   o0 == 8 and (ph == 0 or h == 1))

        def best(ph, h):
            if ph == 0: scan(A("sc", 192 * h, 192 * h + 192), A("r12"), SCO(0, h, 0, 192), 0.0, MUL, OP.max)
            else: scan(A("sc", 384, 512), A("r4"), P(7, 0, 128), 0.0, MUL, OP.max)

        def places(r0, r1, f=tt):
            src = IND(A("zq"), A("EZ", 8 * r0, 8 * r1)) if k < 5 else IND(A("l3"), A("EY", 8 * r0, 8 * r1))
            tt(A("XZ", 128 * r0, 128 * r1), src, A("DX", 128 * r0, 128 * r1), ADD, [("a3", gotall)] if k == 5 else ())

        def zlist(r0, r1):
            for rho in range(r0, r1):
                mm(P((0, 1, 4, 4)[rho], 32 + 16 * rho, 48 + 16 * rho), A("XZ", 128 * rho, 128 * rho + 128), A("D16"))

        def clear(h0, h1):
            for c0, c1 in [(8 * h0, 8 * h1)] if h0 % 2 == 0 and h1 == h0 + 2 else [(8 * x, 8 * x + 8) for x in range(h0, h1)]:
                act(IND(A("Wo" if k < 5 else "Wf"), A("Zu", c0, c1)), A("zr", 0, 16 * (c1 - c0)), AF.Silu)
        for p in range(16):
            ph = int(p >= PH[1][0]); f, n = PH[ph]
            if k == 1:
                w = 1 if p < 4 or p >= 12 else (2, 0, 2, 0)[p % 4]
                if w: (act if (p if w == 1 else p // 2) % 2 == 0 else cp)(A("Vd", 256 * p, 256 * (p + w)),
                                                                          IND(A("Wl"), A("cu", 16 * p, 16 * (p + w))))
                for h in range(2):
                    mm(SCO(ph, h, p - f, 16 * n, n), A("Vd", 256 * p + 128 * h, 256 * p + 128 * h + 128),
                       A("SF", 24, 40), False, p == f + n - 1 and (ph == 0 or h == 1))
                continue
            w = 1 if p < 2 else 2 - 2 * (p % 2)
            if p % 2 == 0 and p < 14:
                act(A("Vd", 256 * p, 256 * p + 512), IND(A("Wl"), A("cu", 16 * p, 16 * p + 32)))
            if p == 14: short(0, 0); act(blk("Vd", p), IND(A("Wl"), A("cu", 16 * p, 16 * p + 16))); bar(0, 0)
            if w:
                tt(A("Fd", 256 * p, 256 * (p + w)), IND(A("Fw", 0, 4096), A("cu", 16 * p, 16 * (p + w))), A("M", 0, 256 * w), OP.max)
            if p == 15:
                cp(A("Vd", 3840, 3904), IND(A("Wl"), A("cu", 240, 244))); act(A("Vd", 3904, 4096), IND(A("Wl"), A("cu", 244, 256)))
                short(0, 1)
            for h in range(2):
                c0 = 256 * p + 128 * h
                mm(SCO(ph, h, p - f, 16 * n, n), A("Fd", c0, c0 + 128), A("SF", 0, 16), False, False)
                mm(P(2 * ph + h, p - f, 24 * n, n), A("Fd", c0, c0 + 128), A("SF", 0, 24), False, False)
                mm(P(2 * ph + h, p - f, 24 * n, n), A("Vd", c0, c0 + 128), A("SV", 0, 24), False, p == f + n - 1)
                mm(SCO(ph, h, p - f, 16 * n, n), A("Vd", c0, c0 + 128), A("SV", 24, 40), False, False)
            if p == 14 and k == 5: act(A("l3", 16 * q, 16 * q + 16), A("s3", 16 * q, 16 * q + 16))
        if k > 1:
            places(0, 1)
            short(1, 0); short(1, 1); zlist(0, 1); bar(0, 1); bar(1, 0); bar(1, 1)
        best(0, 0)
        if k > 2: places(1, 2); zlist(1, 2)
        if k > 1: cp(A("Zu", 0, 16), P(0, 32, 48)); clear(0, 2)
        best(0, 1)
        if k == 1: late(1)
        best(1, 0)
        tt(A("bi"), A("sc", 11, 384, 12), A("sc", 387, 512, 4), OP.max)
        mm(P(5, 0, 256), A("DW"), A("onb", 0, 256), True, False)
        if 1 < k < 5: act(A("DD"), VX, AF.Relu, bias=2.0 ** 17, scale=-(2.0 ** 17))
        if k > 2: cp(A("Zu", 16, 32), P(1, 48, 64))
        ts(A("I1", 0, 32), A("bi"), 63, AND)
        ts(A("gi", 0, 32), A("bi"), 0xFFFC00, AND)
        if k > 2: clear(2, 3)
        cp(A("X1"), IND(A("I1"), A("E1")))
        for S in range(2):
            mm(P(4, 0, 16), A("X1", 128 * S, 128 * S + 128), A("D16b", 16 * S, 16 * S + 16), S == 0, S == 1)
        cp(A("Kt", 12, 512, 16), A("gi", 0, 32))
        ts(A("Kt", 15, 512, 16), A("bi"), 1023.5, GT)
        if k < 5: ts(A("gi", 32, 64), A("bi"), 11, SHR); ts(A("gi", 64, 96), A("bi"), 1024, AND)
        else: cp(A("gi", 32, 112), VX)
        tt(A("Kt", 13, 512, 16), A("gi", 0, 32), A("Kt", 12, 512, 16), SUB)
        cl = A("CL", 48 * nr, 48 * nr + 16)
        cp(cl, P(4, 0, 16))
        for h in range(2):
            mm(P(5, 0, 256), A("Kt", 256 * h, 256 * h + 128), A("PJb", 256 * h, 256 * h + 256), False, h == 1)
        if k == 5:
            ts(A("gi", 32, 112), A("gi", 32, 112), 4095, AND); act(A("t1", 0, 80), A("sm", 0, 80), scale=8192.0)
        if k < 5:
            cp(A("ctf"), P(4, 0, 16))
            for t in range(2):
                mm(P(4, 16 + 16 * t, 32 + 16 * t), A("Sh", 128 * t, 128 * t + 128), A("ctf"))
        cp(A("La", 0, 128), IND(A("Bw"), A("CL", 48 * nr, 48 * nr + 8)))
        act(A("La", 128, 256), IND(A("Bw"), A("CL", 48 * nr + 8, 48 * nr + 16)))
        if k < 5:
            cp(A("Kk", 0, 512, 16), A("gi", 32, 64)); tt(A("Kk", 8, 512, 16), A("gi", 64, 96), A("idc"), ADD)
            tt(A("Kk", 4, 512, 16), A("gi", 0, 32), A("idc"), ADD)
        tt(A("R"), P(5, 0, 256), A("La"), ADD)
        for h in range(2):
            mm(P(7, 128 + h, 192, 2), A("R", 128 * h, 128 * h + 128), A("SS", 32 * h, 32 * h + 32))
        if k > 2: clear(3, 4)
        ts(A("Lo"), A("La"), ODD, MUL)
        if k < 5: cp(A("CL", 48 * nr + 16, 48 * nr + 48), P(4, 16, 48)); late(k + 2)
        if k >= 4: places(2, nr)
        if k < 5: act(A("dP", 64, 80), A("dP", 64, 80), bias=4095.5 if k == 1 else 4096.0)
        act(A("st", 16, 64), P(7, 144, 192))
        al = A("al", 0, 16) if k < 5 else A("ow", 16, 32)
        if k == 5: tt(A("t2", 0, 80), A("gi", 32, 112), A("sm", 0, 80), ADD)
        for n, ggs in enumerate(((0,), (1,), (2, 3), (4, 5), (6, 7))):
            for h in ((0, 1) if n == 0 else (1, 0)):
                b = ((0, 1, 2), (3, 6, 5))[h][n % 3]
                for i, gg in enumerate(ggs):
                    p0 = 16 * (gg - gg % 2); p1 = 16 * gg + 16
                    mm(P(b, 256 * i, 256 * i + 256), A("Lo" if gg % 2 else "La", 128 * h, 128 * h + 128, 1, p0, p1),
                       A("R", 0, 256, 1, p0, p1))
                for i, gg in enumerate(ggs):
                    col = A("acc", 2 * gg + h, 2 * gg + h + 1)
                    if h == 0: red(col, P(b, 256 * i, 256 * i + 256), OP.max)
                    else: act(blk("CD", gg), P(b, 256 * i, 256 * i + 256), AF.Relu, bias=A("st", 33 + 2 * gg, 34 + 2 * gg), acc=col)
            if n == 0: tt(A("st", 64, 80) if k < 5 else A("o2", 16, 32), P(7, 128, 144), A("dP", 16, 32), SUB)
            if n == 0 and k == 5: ts(A("o2", 0, 16), A("st", 16, 32), -(2.0 ** -15), MUL)
            if n == 1 and k < 5: cp(A("XR"), IND(A("st", 64, 88), A("E2")))
            if n == 2 and k >= 4: zlist(2, nr)
            if n == 3 and k >= 4: cp(A("Zu", 32, 16 * nr), P(4, 64, 32 + 16 * nr))
            if n == 1 and k == 5: cp(A("t4", 400, 432), IND(A("o2"), A("FS1")))
        if k < 5:
            for h in range(2):
                mm(P(4, 256 + 128 * h, 384 + 128 * h), A("Kt", 256 * h, 256 * h + 128), A("Ib"), True, False)
                mm(P(4, 256 + 128 * h, 384 + 128 * h), A("Kk", 256 * h, 256 * h + 128), A("I"), False, True)
            mm(P(2, 0, 16), A("DX", 0, 128), A("D16"), True, False)
            if k == 4: clear(4, 6)
            else: act(A("Va"), P(4, 256, 512))
        else:
            act(A("st", 80, 96), P(7, 128, 144), bias=2048.5)
        tt(al, A("acc"), A("st", 48, 64), EQL)
        if k < 5:
            tt(A("XW"), IND(A("al"), A("E2")), A("XR"), MUL)
            mm(P(2, 0, 16), A("XW"), A("D16"), False, True)
            tt(A("st", 80, 96), P(7, 128, 144), A("dP", 64, 80), ADD)
            if k == 4: cp(A("Va"), P(4, 256, 512))
            act(A("NK", k, 80, 5), A("st", 16, 32))
            act(A("DD", k, 80, 5), al, bias=2.0 ** 17, scale=-(2.0 ** 17))
            act(A("ZD", k, 80, 5), A("st", 64, 80), bias=-256.0 * nr)
            if k < 4: tt(A("VX", 3 * k + 2, 240, 15), al, A("st", 80, 96), MUL)
            cp(A("Wu"), P(2, 0, 16))
            if k == 1: late(7)
            mm(P(5, 256, 496), A("Ib"), A("PM", 0, 240), True, False)
            for t in (1, 2):
                mm(P(5, 256 + t, 496, 3), A("I"), A("NK"), False, False)
            for rho in range(k):
                mm(P(5, 256 + 3 * rho, 496, 15), A("I"), A("NK", rho, 80, 5), False, False)
            for t in range(3):
                mm(P(5, 256 + t, 496, 3), A("NI"), A("DD"), False, False)
            cp(IND(A("Wo"), A("Wu")), A("Va"))
            gr = "w%d" % k
            dma("s", A("Wl", 0, 4096, 1, 0, 128, 8), A("Wo", 0, 4096, 1, 0, 128, 8), gr)
            dma("s", A("Wl", 0, 4096, 1, 17, 128, 8), A("Wo", 0, 4096, 1, 0, 112, 8), gr)
            dma("s", A("Wl", 0, 4096, 1, 3, 112, 8), A("Wo", 0, 4096, 1, 16, 128, 8), gr)
            for e in (0, 8):
                dma("s", A("Wl", 0, 4096, 1, 2 + e, 128, 64), A("Wo", 0, 4096, 1, 48 + e, 128, 64), gr)
                dma("s", A("Wl", 0, 4096, 1, 52 + e, 128, 64), A("Wo", 0, 4096, 1, e, 128, 64), gr)
            if k == 4:
                for r in order:
                    dma("s", ("!", T.ts[r]), A("Wo", 0, 4096, 1, 16 * r + 4, 128, 64), "ts")
                dma("s", A("Wf", 0, 4096, 1, 32 * q, 32 * q + 32, 16), A("Wo", 0, 4096, 1, 16 * q + 4, 128, 64), "tf")
                send(lambda r: T.ts[r], T.tl[q], "at", [], [("@ts", 0)])
                for s in order:
                    dma("s", A("Wf", 0, 4096, 1, 32 * s, 32 * s + 32, 16), ("!", T.tl[s]), "tf", [("at", gotall)])

    tt(A("s1"), IND(A("ow"), A("FS1")), A("t4", 400, 432), MUL)
    send(lambda r: T.s1[:, 8 * r:8 * r + 8], T.l1[:, 8 * q:8 * q + 8], "a1", [A("s1")])
    clear(4, 6)
    ts(A("t1", 5, 81, 5), al, 8192.0, MUL)
    tt(A("t2", 5, 81, 5), al, A("st", 80, 96), MUL)
    scan(A("t0", 0, 80), A("r5", 0, 80), A("t1", 1, 81), 0.0, MUL, ADD)
    cp(A("l1", 8 * q, 8 * q + 8), A("s1", 8 * q, 8 * q + 8))
    tt(A("t0", 0, 80), A("t0", 0, 80), A("t2", 1, 81), ADD)
    cp(A("PJ"), A("PJb")); cp(A("FR"), A("t2", 128, 144))
    for s in range(4):
        act(A("t4", 80 * s, 80 * s + 80), A("t0", 0, 80), AF.Abs, bias=A("fc", 52 + s, 53 + s))
    clear(6, 8)
    mm(P(4, 0, 16), A("onb", 0, 128, 1, 0, 1), A("tb", 0, 16, 1, 0, 1), True, False)
    scan(A("t5", 0, 320), A("t3", 0, 320), A("t4", 0, 320), 0.0, ADD, OP.min)
    ts(A("s2"), IND(A("t5", 0, 320), A("FS2")), 4096.0, OP.min, -2048.0, ADD)
    send(lambda r: T.s2[:, 16 * r:16 * r + 16], T.l2[:, 16 * q:16 * q + 16], "a2", [A("s2")])
    cp(A("l2", 16 * q, 16 * q + 16), A("s2", 16 * q, 16 * q + 16))
    for h in range(2):
        cp(A("Kk", 256 * h, 256 * h + 128, 8), A("l1", h, 32, 2), [("a1", gotall)])
        mm(P(5, 128 * h, 128 * h + 128), A("Kk", 256 * h, 256 * h + 128), A("I"))
    for h in range(2):
        tt(A("XL", 128 * h, 128 * h + 128), IND(A("l1"), A("FR", 8 * h, 8 * h + 8)), A("mD", 0, 128), MUL)
        mm(P(4, 8 * h, 8 * h + 8), A("XL", 128 * h, 128 * h + 128), BD, False, h == 1)
    act(A("Va"), P(5, 0, 256))
    ts(A("Wu"), P(4, 0, 16), fc(23), ADD)
    cp(IND(A("Wf"), A("Wu")), A("Va"))
    dma("s", ("!", T.yt[:, :]), A("Wf", 0, 4096, 1, 0, 128, 16), "yt")
    for h in range(2):
        mm(P(0, 0, 256, 1, 0, 32), A("l2", h, 64, 2), A("PJ", 256 * h, 256 * h + 256), h == 0, h == 1, [("a2", gotall)])
    act(A("yo", 0, 256, 1, 0, 32), P(0, 0, 256, 1, 0, 32), bias=2047.0, scale=-1.0)
    dma("a", ("!", T.yb[:, :]), A("yo", 0, 256, 1, 0, 32), "yb")

    gsem = {n: "d%d" % i for i, n in enumerate(groups)}
    needs = []; hist = {}; clock = {qu: {} for qu in "vatgs"}; snap = []; member = {}
    for i, (qu, _, rd, wr, grp, _w) in enumerate(ops):
        last = {}; known = clock[qu]
        cand = sorted(set(j for a in rd + wr for j in hist.get(a[0], ())), reverse=True)
        for a in rd + wr: hist.setdefault(a[0], set()).add(i)
        for j in cand:
            q2, _, rd2, wr2, grp2, _w2 = ops[j]
            key = q2 if grp2 is None else "@" + grp2
            if (key in last or known.get(key, -1) >= j or grp2 == "remote" or (grp2 is not None and grp2 == grp)
                    or (qu == "t" and q2 == "t")):
                continue
            if (any(_hit(a, b) for a in rd + wr for b in wr2) or any(_hit(a, b) for a in wr for b in rd2)
                    or (q2 != qu and any(a[0] == b[0] and a[0] not in SB for a in rd + wr for b in rd2 + wr2))):
                last[key] = j
        for key, j in sorted(last.items(), key=lambda e: -e[1]):
            if known.get(key, -1) >= j:
                del last[key]; continue
            for jj in (member[key[1:]] if key[0] == "@" else [j]):
                for k2, v2 in snap[jj].items():
                    if known.get(k2, -1) < v2: known[k2] = v2
            known[key] = len(ops) if key[0] == "@" else j
        needs.append(last); snap.append(dict(known))
        if grp is not None: member.setdefault(grp, []).append(i)
    marked = set(j for last in needs for key, j in last.items() if key[0] != "@")
    for qu in "vatg":
        marked.add(max(i for i, o in enumerate(ops) if o[0] == qu and o[4] is None))
    count, number = {}, {}
    for i, o in enumerate(ops):
        if i in marked:
            count[o[0]] = count.get(o[0], 0) + 1; number[i] = count[o[0]]
    eng = {"v": g.vector, "a": g.scalar, "t": g.tensor, "g": g, "s": g.sync}
    seen = {}

    def wait(qu, sem, n):
        if seen.get((qu, sem), 0) < n:
            seen[(qu, sem)] = n; eng[qu].wait_ge(T.sem[sem], n)
    for i, (qu, emit, rd, wr, grp, ws) in enumerate(ops):
        for key, j in needs[i].items():
            if key[0] == "@": wait(qu, gsem[key[1:]], 16 * groups[key[1:]])
            else: wait(qu, "q" + key, number[j])
        for sem, n in ws:
            if sem[0] == "@": wait(qu, gsem[sem[1:]], 16 * groups[sem[1:]])
            else: wait(qu, sem, n)
        ins = emit()
        if grp is not None and grp != "remote": ins.then_inc(T.sem[gsem[grp]], 16)
        elif i in marked: ins.then_inc(T.sem["q" + qu], 1)
    for qu in "vatg":
        wait("g", "q" + qu, count[qu])
    for n in groups:
        wait("g", gsem[n], 16 * groups[n])
    wait("g", "sent", nsent[0])
